import numpy as np
import ml_dtypes


def mxq(x, axis, fmt="e4m3"):
    dtype, down = {"e4m3": (ml_dtypes.float8_e4m3fn, 7), "e5m2": (ml_dtypes.float8_e5m2, 14)}[fmt]
    v = np.moveaxis(np.asarray(x, np.float32).astype(ml_dtypes.bfloat16).astype(np.float64), axis, -1)
    blocks = v.reshape(v.shape[:-1] + (-1, 32))
    amax = np.abs(blocks).max(-1, keepdims=True)
    byte = np.maximum(np.where(amax > 0, np.frexp(amax)[1] - 1 + 127, 0) - down, 1)
    scale = np.exp2(byte - 127.0)
    codes = (blocks / scale).astype(np.float32).astype(dtype).astype(np.float64)
    return np.moveaxis((codes * scale).reshape(v.shape), -1, axis)


WIDE = False


def mx_kscale(k):
    if not WIDE:
        return np.ones(k)
    levels = np.array([10, -10, 5, -5, 0])
    if k % 512:
        return np.exp2(np.random.permutation(np.resize(levels, k // 32))).repeat(32)
    a = np.empty((k // 512, 16))
    for p in range(k // 512):
        a[p, :8] = np.random.permutation(np.resize(levels, 8))
        for g in range(8):
            far = levels[np.abs(levels - a[p, g]) >= 10]
            a[p, g + 8] = far[np.random.randint(len(far))]
    return np.exp2(a.ravel()).repeat(32)


def f64(x):
    return np.asarray(x).astype(np.float64)


def striped(idx):
    return np.tile(idx.reshape(-1, 16).T, (8, 1)).astype(np.uint16)


def unstriped(offs):
    return offs[:16].T.reshape(-1).astype(np.int64)


E2M1 = np.array([0.0, 0.5, 1.0, 1.5, 2.0, 3.0, 4.0, 6.0, -0.0, -0.5, -1.0, -1.5, -2.0, -3.0, -4.0, -6.0])


def pack_weight(w, fmt):
    k, n = w.shape
    w = f64(np.asarray(w, np.float32).astype(ml_dtypes.bfloat16)).reshape(k // 32, 32, n)
    amax = np.abs(w).max(1)
    if fmt == "e4m3":
        byte = np.frexp(amax)[1] - 1 + 127 - 7
    else:
        mant, ex = np.frexp(amax / 6.0)
        byte = np.where(mant > 0.5, ex, ex - 1) + 127
    byte = np.clip(np.where(amax > 0, byte, 1), 1, 254)
    scaled = (w * np.exp2(127.0 - byte)[:, None, :]).reshape(k, n).astype(np.float32)
    by_word = np.ascontiguousarray(scaled.reshape(k // 512, 128, 4, n).transpose(0, 1, 3, 2))
    if fmt == "e4m3":
        words = by_word.astype(ml_dtypes.float8_e4m3fn).view(np.uint8)
    else:
        c = by_word.astype(ml_dtypes.float4_e2m1fn).view(np.uint8) & 0xF
        words = (c[..., 0::2] | (c[..., 1::2] << 4)).reshape(k // 512, 128, 2 * n)
    return np.ascontiguousarray(words), np.ascontiguousarray(byte.astype(np.uint8).reshape(k // 512, 16, n))


def unpack_weight(words, scales, fmt):
    g, _, n = scales.shape
    words = np.ascontiguousarray(words).reshape(g, 128, n, -1)
    if fmt == "e4m3":
        vals = words.view(ml_dtypes.float8_e4m3fn).astype(np.float64)
    else:
        nib = np.empty((g, 128, n, 4), np.uint8)
        nib[..., 0::2] = words & 0xF
        nib[..., 1::2] = words >> 4
        vals = E2M1[nib]
    vals = vals * np.repeat(np.exp2(scales.astype(np.float64) - 127.0), 8, axis=1)[..., None]
    return vals.transpose(0, 1, 3, 2).reshape(g * 512, n)


def gelu(v):
    return 0.5 * v * (1.0 + np.tanh(np.sqrt(2.0 / np.pi) * (v + 0.044715 * v**3)))


def bf(x):
    return np.asarray(x, np.float32).astype(ml_dtypes.bfloat16)


def planes(Y):
    n, m = Y.shape
    b = f64(bf(Y)).reshape(n // 32, 32, m)
    amax = np.abs(b).max(1)
    byte = np.clip(np.where(amax > 0, np.frexp(amax)[1] - 1 + 127 - 7, 1), 1, 254)
    codes = (b * np.exp2(127.0 - byte)[:, None, :]).reshape(n, m).astype(np.float32).astype(ml_dtypes.float8_e4m3fn).view(np.uint8)
    words = codes.reshape(n // 512, 128, 4, m).transpose(0, 1, 3, 2)
    return np.ascontiguousarray(words), np.ascontiguousarray(byte.astype(np.uint8).reshape(n // 512, 16, m))


K, H, N, T, S = 1024, 512, 768, 4096, 1024


def setup_inputs():
    n = np.random.standard_normal
    s = mx_kscale(K)[:, None]
    u = mx_kscale(H)[:, None]
    tab_words, tab_scales = pack_weight(n((K, T)) * s, "e4m3")
    wi_words, wi_scales = pack_weight(n((K, H)) / np.sqrt(K) / s * u.T, "e2m1")
    wc_words, wc_scales = pack_weight(n((K, N)) / np.sqrt(K) / s, "e4m3")
    return {
        "tab_words": tab_words, "tab_scales": tab_scales,
        "offs": striped(np.random.permutation(T)[:S]),
        "wi_words": wi_words, "wi_scales": wi_scales,
        "we": (n((K, H)) / np.sqrt(K) / s).astype(np.float32),
        "burn": (n((H, S)) * u).astype(np.float32),
        "wl": (n((H, N)) / np.sqrt(H) / u).astype(np.float32),
        "wc_words": wc_words, "wc_scales": wc_scales,
    }


def reference(tab_words, tab_scales, offs, wi_words, wi_scales, we, burn, wl, wc_words, wc_scales):
    v = unpack_weight(tab_words, tab_scales, "e4m3")[:, unstriped(offs)]
    inc = unpack_weight(wi_words, wi_scales, "e2m1").T @ v
    expo = mxq(f64(we), 0, "e4m3").T @ v
    h = f64(burn) + inc * expo
    words, scales = planes(h)
    load = mxq(f64(wl), 0, "e4m3").T @ mxq(h, 0, "e4m3")
    cap = unpack_weight(wc_words, wc_scales, "e4m3").T @ v
    y = np.minimum(load, cap)
    return y, h, words, scales

@@ -1,0 +1,248 @@
+from contextlib import ExitStack
+
+import concourse.mybir as mybir
+
+K, H, N, T, S = 1024, 512, 768, 4096, 1024
+FLOPS = 2 * S * (2 * K * H + H * N + K * N)
+
+F32 = mybir.dt.float32
+BF16 = mybir.dt.bfloat16
+I32 = mybir.dt.int32
+U32 = mybir.dt.uint32
+U16 = mybir.dt.uint16
+U8 = mybir.dt.uint8
+FP8X4 = mybir.dt.float8_e4m3fn_x4
+FP4X4 = mybir.dt.float4_e2m1fn_x4
+ALU = mybir.AluOpType
+
+P = 128
+PACK = 4
+PASSES = K // (P * PACK)
+HALF = 512
+HALVES = S // HALF
+N_TILES = N // P
+QUADS = 4
+WC_ROW = 8
+
+
+def tile_list_prepayment_burnout_cap_kernel(
+    tc, tab_words, tab_scales, offs, wi_words, wi_scales, we, burn, wl, wc_words, wc_scales,
+    out_0, out_1, out_2, out_3,
+):
+    nc = tc.nc
+    with ExitStack() as ctx:
+        lists = ctx.enter_context(tc.tile_pool(name="lists", bufs=1))
+        keep = ctx.enter_context(tc.tile_pool(name="keep", bufs=1))
+        psum_s = ctx.enter_context(tc.psum_pool(name="psum_s", bufs=4))
+        psum_v = ctx.enter_context(tc.psum_pool(name="psum_v", bufs=4))
+
+        def tile(shape, dtype, name):
+            return keep.tile(shape, dtype, name=name, align_bytes=64)
+
+        offsets = lists.tile([P, S // 16], U16, name="offsets")
+        tab = [tile([P, T], I32, f"tab{a}") for a in range(PASSES)]
+        tab_s = tile([P, PASSES * T], U8, "tab_s")
+        v = [[tile([P, HALF], U32, f"v{a}{u}") for u in range(HALVES)] for a in range(PASSES)]
+        v_s = [tile([P, S], U8, f"v_s{a}") for a in range(PASSES)]
+        wi_raw = tile([P, PASSES * 2 * H], U8, "wi_raw")
+        wi_s_raw = tile([P, PASSES * H], U8, "wi_s_raw")
+        wi_q = tile([P, PASSES * 2 * H], U8, "wi_q")
+        wi_s = tile([P, PASSES * H], U8, "wi_s")
+        we_raw = [tile([P, PACK, H], F32, f"we_raw{a}") for a in range(PASSES)]
+        we_bf = [tile([P, H * PACK], BF16, f"we_bf{a}") for a in range(PASSES)]
+        we_q = [tile([P, H], U32, f"we_q{a}") for a in range(PASSES)]
+        we_s = [tile([P, H], U8, f"we_s{a}") for a in range(PASSES)]
+        wl_raw = tile([P, PACK, N], F32, "wl_raw")
+        wl_bf = tile([P, N * PACK], BF16, "wl_bf")
+        wl_q = tile([P, N], U32, "wl_q")
+        wl_s = tile([P, N], U8, "wl_s")
+        wc_q = tile([P, PASSES * N], I32, "wc_q")
+        wc_s = tile([P, PASSES * N], U8, "wc_s")
+        h = [tile([P, PACK, HALF], F32, f"h{u}") for u in range(HALVES)]
+        inc = [tile([P, PACK, HALF], F32, f"inc{u}") for u in range(HALVES)]
+        prod = [tile([P, PACK, HALF], F32, f"prod{u}") for u in range(HALVES)]
+        h_bf = [tile([P, HALF * PACK], BF16, f"h_bf{u}") for u in range(HALVES)]
+        h_q = [tile([P, HALF], I32, f"h_q{u}") for u in range(HALVES)]
+        h_s = tile([P, S], U8, "h_s")
+        y = [tile([P, N_TILES, HALF], F32, f"y{u}") for u in range(HALVES)]
+
+        nc.gpsimd.memset(tab_s[:, :T].bitcast(I32), 0)
+        nc.vector.memset(tab_s[:, T:].bitcast(I32), 0)
+        nc.gpsimd.memset(wi_s_raw[:].bitcast(I32), 0)
+        nc.gpsimd.memset(wc_s[:].bitcast(I32), 0)
+
+        def load_tab(a):
+            nc.sync.dma_start(out=tab[a][:], in_=tab_words[a].rearrange("p t i -> p (t i)").bitcast(I32))
+
+        def load_scale_rows(dst, src, row):
+            for q in range(QUADS):
+                nc.sync.dma_start(
+                    out=dst[32 * q + row : 32 * q + row + 4, :].rearrange("r (a c) -> r a c", a=PASSES).bitcast(I32),
+                    in_=src[:, 4 * q : 4 * q + 4, :].rearrange("a r c -> r a c").bitcast(I32),
+                )
+
+        def load_we(a):
+            nc.sync.dma_start(
+                out=we_raw[a][:], in_=we[512 * a : 512 * (a + 1), :].rearrange("(p j) c -> p j c", j=PACK)
+            )
+
+        def load_burn(u):
+            nc.sync.dma_start(
+                out=h[u][:], in_=burn.rearrange("(p t) j -> p t j", t=PACK)[:, :, u * HALF : (u + 1) * HALF]
+            )
+
+        nc.sync.dma_start(offsets[:], offs)
+        load_scale_rows(tab_s, tab_scales, 0)
+        for a in range(PASSES):
+            nc.sync.dma_start(out=wi_raw[:, 2 * H * a : 2 * H * (a + 1)].bitcast(I32), in_=wi_words[a].bitcast(I32))
+        load_tab(0)
+        load_scale_rows(wi_s_raw, wi_scales, 0)
+        load_we(0)
+        load_tab(1)
+        load_we(1)
+        load_burn(0)
+        nc.sync.dma_start(
+            out=wc_q[:].rearrange("p (a c) -> p a c", a=PASSES),
+            in_=wc_words.rearrange("a p c i -> p a (c i)").bitcast(I32),
+        )
+        load_scale_rows(wc_s, wc_scales, WC_ROW)
+        nc.sync.dma_start(out=wl_raw[:], in_=wl.rearrange("(p j) c -> p j c", j=PACK))
+        load_burn(1)
+
+        def gather(a, u):
+            cols = HALF // 16
+            nc.vector.tensor_copy(v[a][u][:], tab[a][:].bitcast(U32).indirect(offsets[:, u * cols : (u + 1) * cols]))
+
+        def gather_scales(a):
+            nc.vector.tensor_copy(v_s[a][:], tab_s[:, a * T : (a + 1) * T].indirect(offsets[:]))
+
+        def quant_we(a, t0, t1, copy):
+            copy(
+                out=we_bf[a][:, t0 * H : t1 * H].rearrange("p (t m j) -> p m j t", m=P, j=PACK),
+                in_=we_raw[a][:].rearrange("p j (m t) -> p m j t", t=PACK)[:, :, :, t0:t1],
+            )
+            nc.vector.quantize_mx(
+                out=we_q[a][:, t0 * P : t1 * P].bitcast(FP8X4), scales=we_s[a][:, t0 * P : t1 * P],
+                in_=we_bf[a][:, t0 * H : t1 * H],
+            )
+
+        nc.vector.tensor_copy(
+            out=wi_q[:].bitcast(U16).rearrange("p (a t m) -> p a m t", a=PASSES, t=PACK),
+            in_=wi_raw[:].bitcast(U16).rearrange("p (a m t) -> p a m t", a=PASSES, t=PACK),
+        )
+        gather_scales(0)
+        gather(0, 0)
+        nc.vector.tensor_copy(
+            out=wi_s[:].rearrange("p (a t m) -> p a m t", a=PASSES, t=PACK),
+            in_=wi_s_raw[:].rearrange("p (a m t) -> p a m t", a=PASSES, t=PACK),
+        )
+        gather_scales(1)
+        gather(0, 1)
+        quant_we(0, 0, PACK, nc.scalar.copy)
+        for u in range(HALVES):
+            gather(1, u)
+        quant_we(1, 0, 2, nc.vector.tensor_copy)
+        quant_we(1, 2, PACK, nc.scalar.copy)
+
+        def v_plane(a, u):
+            cols = slice(u * HALF, (u + 1) * HALF)
+            return v_s[a][:, cols]
+
+        def inc_tile(u, t):
+            acc = psum_s.tile([P, HALF], F32, name="acc_s")
+            for a in range(PASSES):
+                c0 = a * H + t * P
+                nc.tensor.matmul_mx(
+                    out=acc[:], lhsT=wi_q[:, 2 * c0 : 2 * (c0 + P)].bitcast(FP4X4), lhsT_scale=wi_s[:, c0 : c0 + P],
+                    rhs=v[a][u][:].bitcast(FP8X4), rhs_scale=v_plane(a, u), start=(a == 0), stop=(a == PASSES - 1),
+                )
+            nc.scalar.copy(out=inc[u][:, t, :], in_=acc[:])
+
+        def inc_half(u):
+            for t in range(PACK):
+                inc_tile(u, t)
+
+        def interleave(engine_copy, dst, src):
+            engine_copy(
+                out=dst.rearrange("p (c i t) -> p c t i", i=4, t=PACK),
+                in_=src.rearrange("p t (c i) -> p c t i", i=4),
+            )
+
+        def expo_half(u):
+            accs = [psum_v.tile([P, HALF], F32, name="acc_v") for t in range(PACK)]
+            for a in range(PASSES):
+                for t in range(PACK):
+                    nc.tensor.matmul_mx(
+                        out=accs[t][:], lhsT=we_q[a][:, t * P : (t + 1) * P].bitcast(FP8X4),
+                        lhsT_scale=we_s[a][:, t * P : (t + 1) * P],
+                        rhs=v[a][u][:].bitcast(FP8X4), rhs_scale=v_plane(a, u),
+                        start=(a == 0), stop=(a == PASSES - 1),
+                    )
+            for t in range(PACK):
+                nc.vector.tensor_tensor(prod[u][:, t, :], accs[t][:], inc[u][:, t, :], ALU.mult)
+
+        def add_half(u):
+            for t in range(0, PACK, 2):
+                nc.vector.tensor_tensor(h[u][:, t : t + 2, :], h[u][:, t : t + 2, :], prod[u][:, t : t + 2, :], ALU.add)
+            nc.sync.dma_start(
+                out=out_1.rearrange("(p t) j -> p t j", t=PACK)[:, :, u * HALF : (u + 1) * HALF], in_=h[u][:]
+            )
+            interleave(nc.scalar.copy, h_bf[u][:], h[u][:])
+
+        def quant_half(u):
+            nc.vector.quantize_mx(
+                out=h_q[u][:].bitcast(FP8X4), scales=h_s[:, u * HALF : (u + 1) * HALF], in_=h_bf[u][:]
+            )
+            nc.sync.dma_start(
+                out=out_2[0].rearrange("p m t -> p (m t)").bitcast(I32)[:, u * HALF : (u + 1) * HALF], in_=h_q[u][:]
+            )
+
+        def cap_half(u):
+            for n in range(N_TILES):
+                acc = psum_s.tile([P, HALF], F32, name="acc_s")
+                for a in range(PASSES):
+                    c0 = a * N + n * P
+                    nc.tensor.matmul_mx(
+                        out=acc[:], lhsT=wc_q[:, c0 : c0 + P].bitcast(FP8X4), lhsT_scale=wc_s[WC_ROW:P, c0 : c0 + P],
+                        rhs=v[a][u][:].bitcast(FP8X4), rhs_scale=v_plane(a, u),
+                        start=(a == 0), stop=(a == PASSES - 1),
+                    )
+                nc.scalar.copy(out=y[u][:, n, :], in_=acc[:])
+
+        def load_half(u):
+            for n in range(N_TILES):
+                acc = psum_v.tile([P, HALF], F32, name="acc_v")
+                nc.tensor.matmul_mx(
+                    out=acc[:], lhsT=wl_q[:, n * P : (n + 1) * P].bitcast(FP8X4), lhsT_scale=wl_s[:, n * P : (n + 1) * P],
+                    rhs=h_q[u][:].bitcast(FP8X4), rhs_scale=h_s[:, u * HALF : (u + 1) * HALF], start=True, stop=True,
+                )
+                nc.vector.tensor_tensor(y[u][:, n, :], acc[:], y[u][:, n, :], ALU.min)
+                first = {1: 0, 3: 2, 5: 4} if u == 0 else {1: 0, 3: 2, 4: 4, 5: 5}
+                if n in first:
+                    nc.sync.dma_start(
+                        out=out_0.rearrange("(n p) j -> p n j", p=P)[:, first[n] : n + 1, u * HALF : (u + 1) * HALF],
+                        in_=y[u][:, first[n] : n + 1, :],
+                    )
+
+        inc_half(0)
+        expo_half(0)
+        inc_half(1)
+        add_half(0)
+        expo_half(1)
+        add_half(1)
+        for i, copy in enumerate((nc.scalar.copy, nc.scalar.copy, nc.scalar.copy)):
+            c0, c1 = 256 * i, 256 * (i + 1)
+            interleave(copy, wl_bf[:, PACK * c0 : PACK * c1], wl_raw[:, :, c0:c1])
+            nc.vector.quantize_mx(
+                out=wl_q[:, c0:c1].bitcast(FP8X4), scales=wl_s[:, c0:c1], in_=wl_bf[:, PACK * c0 : PACK * c1]
+            )
+        quant_half(0)
+        quant_half(1)
+        for q in range(QUADS):
+            nc.sync.dma_start(
+                out=out_3[0, 4 * q : 4 * q + 4, :].bitcast(I32), in_=h_s[32 * q : 32 * q + 4, :].bitcast(I32)
+            )
+        cap_half(0)
+        load_half(0)
+        cap_half(1)
+        load_half(1)

@@ -22,7 +22,9 @@ HALF = 512
 HALVES = S // HALF
 N_TILES = N // P
 QUADS = 4
-WC_ROW = 8
+ROWS = PASSES * 16
+V_COL, WI_COL, WC_COL, PLANE = 0, S, S + H, S + H + N
+CFG = {"loads":["offs wis ts wcs tab0 wi","tab1","","we0","we1 wc","burn0 wl burn1",""],"tags":{"tab1":"v_s","we_raw0":"tab0","we_raw1":"wi_raw","h0":"v_s","wc_q":"rows","wl_raw":"tab0","h1":"we_bf0"},"weearly":0,"mover":"P","we0":"V","we1":"VV","add":["VV","VV"],"hil":["S","S"],"wl":"SSS","wltag":"wl_bf","steps":"i00 i01 i10 i11 e00 e01 a0 q0 e10 e11 w0 a1 q1 s0 c006 c106 l0 l1"}
 
 
 def tile_list_prepayment_burnout_cap_kernel(
@@ -37,27 +39,26 @@ def tile_list_prepayment_burnout_cap_kernel(
         psum_v = ctx.enter_context(tc.psum_pool(name="psum_v", bufs=4))
 
         def tile(shape, dtype, name):
-            return keep.tile(shape, dtype, name=name, align_bytes=64)
+            return keep.tile(shape, dtype, name=name, tag=CFG["tags"].get(name, name), align_bytes=64)
 
         offsets = lists.tile([P, S // 16], U16, name="offsets")
-        tab = [tile([P, T], I32, f"tab{a}") for a in range(PASSES)]
-        tab_s = tile([P, PASSES * T], U8, "tab_s")
-        v = [[tile([P, HALF], U32, f"v{a}{u}") for u in range(HALVES)] for a in range(PASSES)]
-        v_s = [tile([P, S], U8, f"v_s{a}") for a in range(PASSES)]
+        tab_s = tile([P, T], U8, "tab_s")
+        v_s = tile([P, S], U8, "v_s")
+        rows = tile([P, PLANE], U8, "rows")
+        planes = [tile([P, PLANE], U8, f"planes{a}") for a in range(PASSES)]
         wi_raw = tile([P, PASSES * 2 * H], U8, "wi_raw")
-        wi_s_raw = tile([P, PASSES * H], U8, "wi_s_raw")
+        wi_s_raw = tile([P, H], U8, "wi_s_raw")
         wi_q = tile([P, PASSES * 2 * H], U8, "wi_q")
-        wi_s = tile([P, PASSES * H], U8, "wi_s")
+        tab = [tile([P, T], I32, f"tab{a}") for a in range(PASSES)]
+        v = [[tile([P, HALF], U32, f"v{a}{u}") for u in range(HALVES)] for a in range(PASSES)]
         we_raw = [tile([P, PACK, H], F32, f"we_raw{a}") for a in range(PASSES)]
         we_bf = [tile([P, H * PACK], BF16, f"we_bf{a}") for a in range(PASSES)]
         we_q = [tile([P, H], U32, f"we_q{a}") for a in range(PASSES)]
         we_s = [tile([P, H], U8, f"we_s{a}") for a in range(PASSES)]
         wl_raw = tile([P, PACK, N], F32, "wl_raw")
-        wl_bf = tile([P, N * PACK], BF16, "wl_bf")
         wl_q = tile([P, N], U32, "wl_q")
         wl_s = tile([P, N], U8, "wl_s")
         wc_q = tile([P, PASSES * N], I32, "wc_q")
-        wc_s = tile([P, PASSES * N], U8, "wc_s")
         h = [tile([P, PACK, HALF], F32, f"h{u}") for u in range(HALVES)]
         inc = [tile([P, PACK, HALF], F32, f"inc{u}") for u in range(HALVES)]
         prod = [tile([P, PACK, HALF], F32, f"prod{u}") for u in range(HALVES)]
@@ -66,20 +67,18 @@ def tile_list_prepayment_burnout_cap_kernel(
         h_s = tile([P, S], U8, "h_s")
         y = [tile([P, N_TILES, HALF], F32, f"y{u}") for u in range(HALVES)]
 
-        nc.gpsimd.memset(tab_s[:, :T].bitcast(I32), 0)
-        nc.vector.memset(tab_s[:, T:].bitcast(I32), 0)
-        nc.gpsimd.memset(wi_s_raw[:].bitcast(I32), 0)
-        nc.gpsimd.memset(wc_s[:].bitcast(I32), 0)
+        nc.vector.memset(tab_s[32:64, :].bitcast(I32), 0)
+        nc.vector.memset(tab_s[64:P, :].bitcast(I32), 0)
+        nc.vector.memset(wi_s_raw[32:64, :].bitcast(I32), 0)
+        nc.vector.memset(wi_s_raw[64:P, :].bitcast(I32), 0)
+        for a in range(PASSES):
+            nc.vector.memset(planes[a][:].bitcast(I32), 0)
 
         def load_tab(a):
             nc.sync.dma_start(out=tab[a][:], in_=tab_words[a].rearrange("p t i -> p (t i)").bitcast(I32))
 
-        def load_scale_rows(dst, src, row):
-            for q in range(QUADS):
-                nc.sync.dma_start(
-                    out=dst[32 * q + row : 32 * q + row + 4, :].rearrange("r (a c) -> r a c", a=PASSES).bitcast(I32),
-                    in_=src[:, 4 * q : 4 * q + 4, :].rearrange("a r c -> r a c").bitcast(I32),
-                )
+        def load_scale_rows(dst, src):
+            nc.sync.dma_start(out=dst.bitcast(I32), in_=src.rearrange("a q c -> (a q) c").bitcast(I32))
 
         def load_we(a):
             nc.sync.dma_start(
@@ -91,30 +90,36 @@ def tile_list_prepayment_burnout_cap_kernel(
                 out=h[u][:], in_=burn.rearrange("(p t) j -> p t j", t=PACK)[:, :, u * HALF : (u + 1) * HALF]
             )
 
-        nc.sync.dma_start(offsets[:], offs)
-        load_scale_rows(tab_s, tab_scales, 0)
-        for a in range(PASSES):
-            nc.sync.dma_start(out=wi_raw[:, 2 * H * a : 2 * H * (a + 1)].bitcast(I32), in_=wi_words[a].bitcast(I32))
-        load_tab(0)
-        load_scale_rows(wi_s_raw, wi_scales, 0)
-        load_we(0)
-        load_tab(1)
-        load_we(1)
-        load_burn(0)
-        nc.sync.dma_start(
-            out=wc_q[:].rearrange("p (a c) -> p a c", a=PASSES),
-            in_=wc_words.rearrange("a p c i -> p a (c i)").bitcast(I32),
-        )
-        load_scale_rows(wc_s, wc_scales, WC_ROW)
-        nc.sync.dma_start(out=wl_raw[:], in_=wl.rearrange("(p j) c -> p j c", j=PACK))
-        load_burn(1)
+        loads = {
+            "offs": lambda: nc.sync.dma_start(offsets[:], offs),
+            "ts": lambda: load_scale_rows(tab_s[0:ROWS, :], tab_scales),
+            "wis": lambda: load_scale_rows(wi_s_raw[0:ROWS, :], wi_scales),
+            "wcs": lambda: load_scale_rows(rows[0:ROWS, WC_COL:PLANE], wc_scales),
+            "wi": lambda: nc.sync.dma_start(
+                out=wi_raw[:].rearrange("p (a c) -> p a c", a=PASSES).bitcast(I32),
+                in_=wi_words.rearrange("a p c -> p a c").bitcast(I32)),
+            "wc": lambda: nc.sync.dma_start(
+                out=wc_q[:].rearrange("p (a c) -> p a c", a=PASSES),
+                in_=wc_words.rearrange("a p c i -> p a (c i)").bitcast(I32)),
+            "wl": lambda: nc.sync.dma_start(out=wl_raw[:], in_=wl.rearrange("(p j) c -> p j c", j=PACK)),
+            "tab0": lambda: load_tab(0), "tab1": lambda: load_tab(1), "we0": lambda: load_we(0),
+            "we1": lambda: load_we(1), "burn0": lambda: load_burn(0), "burn1": lambda: load_burn(1),
+        }
+        def load(k):
+            for name in CFG["loads"][k].split():
+                loads[name]()
+
+        load(0)
+
+        def gp_copy(out, in_):
+            nc.gpsimd.tensor_scalar(out, in_, 1.0, 0.0, ALU.mult, ALU.add)
+
+        copies = {"S": nc.scalar.copy, "V": nc.vector.tensor_copy, "G": gp_copy}
+        adders = {"V": nc.vector, "G": nc.gpsimd}
 
         def gather(a, u):
             cols = HALF // 16
             nc.vector.tensor_copy(v[a][u][:], tab[a][:].bitcast(U32).indirect(offsets[:, u * cols : (u + 1) * cols]))
-
-        def gather_scales(a):
-            nc.vector.tensor_copy(v_s[a][:], tab_s[:, a * T : (a + 1) * T].indirect(offsets[:]))
 
         def quant_we(a, t0, t1, copy):
             copy(
@@ -127,40 +132,68 @@ def tile_list_prepayment_burnout_cap_kernel(
             )
 
         nc.vector.tensor_copy(
+            out=rows[:, WI_COL:WC_COL].rearrange("p (t m) -> p m t", t=PACK),
+            in_=wi_s_raw[:].rearrange("p (m t) -> p m t", t=PACK),
+        )
+        nc.vector.tensor_copy(v_s[:], tab_s[:].indirect(offsets[:]))
+        nc.vector.tensor_copy(out=rows[:, V_COL:WI_COL].bitcast(I32), in_=v_s[:].bitcast(I32))
+        mover = {"G": nc.gpsimd, "S": nc.scalar, "P": nc.sync}[CFG["mover"]]
+        for a in range(PASSES):
+            for r in range(4):
+                mover.dma_start(
+                    out=planes[a][r:P:32, :].bitcast(I32), in_=rows[16 * a + r : 16 * (a + 1) : 4, :].bitcast(I32)
+                )
+            load(1 + a)
+        for u in range(HALVES):
+            gather(0, u)
+        load(3)
+        nc.vector.tensor_copy(
             out=wi_q[:].bitcast(U16).rearrange("p (a t m) -> p a m t", a=PASSES, t=PACK),
             in_=wi_raw[:].bitcast(U16).rearrange("p (a m t) -> p a m t", a=PASSES, t=PACK),
         )
-        gather_scales(0)
-        gather(0, 0)
-        nc.vector.tensor_copy(
-            out=wi_s[:].rearrange("p (a t m) -> p a m t", a=PASSES, t=PACK),
-            in_=wi_s_raw[:].rearrange("p (a m t) -> p a m t", a=PASSES, t=PACK),
-        )
-        gather_scales(1)
-        gather(0, 1)
-        quant_we(0, 0, PACK, nc.scalar.copy)
+        load(4)
+        if CFG["weearly"]:
+            quant_we(0, 0, PACK, copies[CFG["we0"]])
         for u in range(HALVES):
             gather(1, u)
-        quant_we(1, 0, 2, nc.vector.tensor_copy)
-        quant_we(1, 2, PACK, nc.scalar.copy)
+        if not CFG["weearly"]:
+            quant_we(0, 0, PACK, copies[CFG["we0"]])
+        load(5)
+        if len(CFG["we1"]) == 1:
+            quant_we(1, 0, PACK, copies[CFG["we1"]])
+        else:
+            quant_we(1, 0, 2, copies[CFG["we1"][0]])
+            quant_we(1, 2, PACK, copies[CFG["we1"][1]])
+
+        load(6)
 
         def v_plane(a, u):
-            cols = slice(u * HALF, (u + 1) * HALF)
-            return v_s[a][:, cols]
+            return planes[a][:, V_COL + u * HALF : V_COL + (u + 1) * HALF]
 
-        def inc_tile(u, t):
-            acc = psum_s.tile([P, HALF], F32, name="acc_s")
-            for a in range(PASSES):
+        def inc_pass(u, accs, a):
+            for t in range(PACK):
                 c0 = a * H + t * P
                 nc.tensor.matmul_mx(
-                    out=acc[:], lhsT=wi_q[:, 2 * c0 : 2 * (c0 + P)].bitcast(FP4X4), lhsT_scale=wi_s[:, c0 : c0 + P],
+                    out=accs[t][:], lhsT=wi_q[:, 2 * c0 : 2 * (c0 + P)].bitcast(FP4X4),
+                    lhsT_scale=planes[a][:, WI_COL + t * P : WI_COL + (t + 1) * P],
                     rhs=v[a][u][:].bitcast(FP8X4), rhs_scale=v_plane(a, u), start=(a == 0), stop=(a == PASSES - 1),
                 )
-            nc.scalar.copy(out=inc[u][:, t, :], in_=acc[:])
+                if a == PASSES - 1:
+                    nc.scalar.copy(out=inc[u][:, t, :], in_=accs[t][:])
 
-        def inc_half(u):
+        def expo_pass(u, accs, a):
             for t in range(PACK):
-                inc_tile(u, t)
+                nc.tensor.matmul_mx(
+                    out=accs[t][:], lhsT=we_q[a][:, t * P : (t + 1) * P].bitcast(FP8X4),
+                    lhsT_scale=we_s[a][:, t * P : (t + 1) * P],
+                    rhs=v[a][u][:].bitcast(FP8X4), rhs_scale=v_plane(a, u),
+                    start=(a == 0), stop=(a == PASSES - 1),
+                )
+                if a == PASSES - 1:
+                    nc.vector.tensor_tensor(prod[u][:, t, :], accs[t][:], inc[u][:, t, :], ALU.mult)
+
+        def banks(pool, name):
+            return [pool.tile([P, HALF], F32, name=name) for t in range(PACK)]
 
         def interleave(engine_copy, dst, src):
             engine_copy(
@@ -168,26 +201,17 @@ def tile_list_prepayment_burnout_cap_kernel(
                 in_=src.rearrange("p t (c i) -> p c t i", i=4),
             )
 
-        def expo_half(u):
-            accs = [psum_v.tile([P, HALF], F32, name="acc_v") for t in range(PACK)]
-            for a in range(PASSES):
-                for t in range(PACK):
-                    nc.tensor.matmul_mx(
-                        out=accs[t][:], lhsT=we_q[a][:, t * P : (t + 1) * P].bitcast(FP8X4),
-                        lhsT_scale=we_s[a][:, t * P : (t + 1) * P],
-                        rhs=v[a][u][:].bitcast(FP8X4), rhs_scale=v_plane(a, u),
-                        start=(a == 0), stop=(a == PASSES - 1),
-                    )
-            for t in range(PACK):
-                nc.vector.tensor_tensor(prod[u][:, t, :], accs[t][:], inc[u][:, t, :], ALU.mult)
-
         def add_half(u):
-            for t in range(0, PACK, 2):
-                nc.vector.tensor_tensor(h[u][:, t : t + 2, :], h[u][:, t : t + 2, :], prod[u][:, t : t + 2, :], ALU.add)
+            n = PACK // len(CFG["add"][u])
+            for i, e in enumerate(CFG["add"][u]):
+                ts = slice(n * i, n * (i + 1))
+                adders[e].tensor_tensor(h[u][:, ts, :], h[u][:, ts, :], prod[u][:, ts, :], ALU.add)
             nc.sync.dma_start(
                 out=out_1.rearrange("(p t) j -> p t j", t=PACK)[:, :, u * HALF : (u + 1) * HALF], in_=h[u][:]
             )
-            interleave(nc.scalar.copy, h_bf[u][:], h[u][:])
+            w = HALF // len(CFG["hil"][u])
+            for i, e in enumerate(CFG["hil"][u]):
+                interleave(copies[e], h_bf[u][:, PACK * w * i : PACK * w * (i + 1)], h[u][:, :, w * i : w * (i + 1)])
 
         def quant_half(u):
             nc.vector.quantize_mx(
@@ -197,13 +221,14 @@ def tile_list_prepayment_burnout_cap_kernel(
                 out=out_2[0].rearrange("p m t -> p (m t)").bitcast(I32)[:, u * HALF : (u + 1) * HALF], in_=h_q[u][:]
             )
 
-        def cap_half(u):
-            for n in range(N_TILES):
+        def cap_half(u, n0, n1):
+            for n in range(n0, n1):
                 acc = psum_s.tile([P, HALF], F32, name="acc_s")
                 for a in range(PASSES):
                     c0 = a * N + n * P
                     nc.tensor.matmul_mx(
-                        out=acc[:], lhsT=wc_q[:, c0 : c0 + P].bitcast(FP8X4), lhsT_scale=wc_s[WC_ROW:P, c0 : c0 + P],
+                        out=acc[:], lhsT=wc_q[:, c0 : c0 + P].bitcast(FP8X4),
+                        lhsT_scale=planes[a][:, WC_COL + n * P : WC_COL + (n + 1) * P],
                         rhs=v[a][u][:].bitcast(FP8X4), rhs_scale=v_plane(a, u),
                         start=(a == 0), stop=(a == PASSES - 1),
                     )
@@ -224,25 +249,41 @@ def tile_list_prepayment_burnout_cap_kernel(
                         in_=y[u][:, first[n] : n + 1, :],
                     )
 
-        inc_half(0)
-        expo_half(0)
-        inc_half(1)
-        add_half(0)
-        expo_half(1)
-        add_half(1)
-        for i, copy in enumerate((nc.scalar.copy, nc.scalar.copy, nc.scalar.copy)):
-            c0, c1 = 256 * i, 256 * (i + 1)
-            interleave(copy, wl_bf[:, PACK * c0 : PACK * c1], wl_raw[:, :, c0:c1])
-            nc.vector.quantize_mx(
-                out=wl_q[:, c0:c1].bitcast(FP8X4), scales=wl_s[:, c0:c1], in_=wl_bf[:, PACK * c0 : PACK * c1]
-            )
-        quant_half(0)
-        quant_half(1)
-        for q in range(QUADS):
-            nc.sync.dma_start(
-                out=out_3[0, 4 * q : 4 * q + 4, :].bitcast(I32), in_=h_s[32 * q : 32 * q + 4, :].bitcast(I32)
-            )
-        cap_half(0)
-        load_half(0)
-        cap_half(1)
-        load_half(1)
+        state = {}
+
+        def step(name):
+            kind, u = name[0], int(name[1])
+            if kind == "i":
+                a = int(name[2])
+                if a == 0:
+                    state["i"] = banks(psum_s, "acc_s")
+                inc_pass(u, state["i"], a)
+            elif kind == "e":
+                a = int(name[2])
+                if a == 0:
+                    state["e"] = banks(psum_v, "acc_v")
+                expo_pass(u, state["e"], a)
+            elif kind == "a":
+                add_half(u)
+            elif kind == "q":
+                quant_half(u)
+            elif kind == "c":
+                cap_half(u, int(name[2]), int(name[3]))
+            elif kind == "l":
+                load_half(u)
+            elif kind == "w":
+                wl_bf = keep.tile([P, N * PACK], BF16, name="wl_bf", tag=CFG["wltag"], align_bytes=64)
+                for i, e in enumerate(CFG["wl"]):
+                    c0, c1 = 256 * i, 256 * (i + 1)
+                    interleave(copies[e], wl_bf[:, PACK * c0 : PACK * c1], wl_raw[:, :, c0:c1])
+                    nc.vector.quantize_mx(
+                        out=wl_q[:, c0:c1].bitcast(FP8X4), scales=wl_s[:, c0:c1], in_=wl_bf[:, PACK * c0 : PACK * c1]
+                    )
+            elif kind == "s":
+                for q in range(QUADS):
+                    nc.sync.dma_start(
+                        out=out_3[0].rearrange("(q r) m -> r q m", r=4)[q].bitcast(I32), in_=h_s[q:P:32, :].bitcast(I32)
+                    )
+
+        for name in CFG["steps"].split():
+            step(name)

@@ -24,7 +24,7 @@ N_TILES = N // P
 QUADS = 4
 ROWS = PASSES * 16
 V_COL, WI_COL, WC_COL, PLANE = 0, S, S + H, S + H + N
-CFG = {"loads":["offs wis ts wcs tab0 wi","tab1","","we0","we1 wc","burn0 wl burn1",""],"tags":{"tab1":"v_s","we_raw0":"tab0","we_raw1":"wi_raw","h0":"v_s","wc_q":"rows","wl_raw":"tab0","h1":"we_bf0"},"weearly":0,"mover":"P","we0":"V","we1":"VV","add":["VV","VV"],"hil":["S","S"],"wl":"SSS","wltag":"wl_bf","steps":"i00 i01 i10 i11 e00 e01 a0 q0 e10 e11 w0 a1 q1 s0 c006 c106 l0 l1"}
+WL_PIECE = 256
 
 
 def tile_list_prepayment_burnout_cap_kernel(
@@ -35,44 +35,47 @@ def tile_list_prepayment_burnout_cap_kernel(
     with ExitStack() as ctx:
         lists = ctx.enter_context(tc.tile_pool(name="lists", bufs=1))
         keep = ctx.enter_context(tc.tile_pool(name="keep", bufs=1))
-        psum_s = ctx.enter_context(tc.psum_pool(name="psum_s", bufs=4))
-        psum_v = ctx.enter_context(tc.psum_pool(name="psum_v", bufs=4))
+        late = ctx.enter_context(tc.tile_pool(name="late", bufs=1))
+        psum_a = ctx.enter_context(tc.psum_pool(name="psum_a", bufs=4))
+        psum_b = ctx.enter_context(tc.psum_pool(name="psum_b", bufs=4))
 
         def tile(shape, dtype, name):
-            return keep.tile(shape, dtype, name=name, tag=CFG["tags"].get(name, name), align_bytes=64)
+            return keep.tile(shape, dtype, name=name, align_bytes=64)
+
+        late_bytes = [0]
+
+        def late_tile(shape, dtype, name):
+            start = late_bytes[-1]
+            late_bytes.append(start + 4 * shape[1] * (shape[2] if len(shape) > 2 else 1))
+            return late.tile(shape, dtype, name=name, align_bytes=64, offset=start)
 
         offsets = lists.tile([P, S // 16], U16, name="offsets")
         tab_s = tile([P, T], U8, "tab_s")
-        v_s = tile([P, S], U8, "v_s")
         rows = tile([P, PLANE], U8, "rows")
         planes = [tile([P, PLANE], U8, f"planes{a}") for a in range(PASSES)]
         wi_raw = tile([P, PASSES * 2 * H], U8, "wi_raw")
         wi_s_raw = tile([P, H], U8, "wi_s_raw")
         wi_q = tile([P, PASSES * 2 * H], U8, "wi_q")
-        tab = [tile([P, T], I32, f"tab{a}") for a in range(PASSES)]
+        tab = [tile([P, T], I32, "tab0"), late_tile([P, T], I32, "tab1")]
         v = [[tile([P, HALF], U32, f"v{a}{u}") for u in range(HALVES)] for a in range(PASSES)]
-        we_raw = [tile([P, PACK, H], F32, f"we_raw{a}") for a in range(PASSES)]
-        we_bf = [tile([P, H * PACK], BF16, f"we_bf{a}") for a in range(PASSES)]
+        we_raw = [tile([P, PACK, H], F32, "we_raw0"), late_tile([P, PACK, H], F32, "we_raw1")]
+        we_bf = [[tile([P, H * 2], BF16, f"we_bf{a}{i}") for i in range(2)] for a in range(PASSES)]
         we_q = [tile([P, H], U32, f"we_q{a}") for a in range(PASSES)]
         we_s = [tile([P, H], U8, f"we_s{a}") for a in range(PASSES)]
-        wl_raw = tile([P, PACK, N], F32, "wl_raw")
+        wl_raw = late_tile([P, PACK, N], F32, "wl_raw")
+        wl_bf = [tile([P, WL_PIECE * PACK], BF16, f"wl_bf{i}") for i in range(N // WL_PIECE)]
         wl_q = tile([P, N], U32, "wl_q")
         wl_s = tile([P, N], U8, "wl_s")
-        wc_q = tile([P, PASSES * N], I32, "wc_q")
-        h = [tile([P, PACK, HALF], F32, f"h{u}") for u in range(HALVES)]
+        wc_q = late_tile([P, PASSES * N], I32, "wc_q")
+        h = [late_tile([P, PACK, HALF], F32, f"h{u}") for u in range(HALVES)]
         inc = [tile([P, PACK, HALF], F32, f"inc{u}") for u in range(HALVES)]
         prod = [tile([P, PACK, HALF], F32, f"prod{u}") for u in range(HALVES)]
         h_bf = [tile([P, HALF * PACK], BF16, f"h_bf{u}") for u in range(HALVES)]
         h_q = [tile([P, HALF], I32, f"h_q{u}") for u in range(HALVES)]
         h_s = tile([P, S], U8, "h_s")
         y = [tile([P, N_TILES, HALF], F32, f"y{u}") for u in range(HALVES)]
-
-        nc.vector.memset(tab_s[32:64, :].bitcast(I32), 0)
-        nc.vector.memset(tab_s[64:P, :].bitcast(I32), 0)
-        nc.vector.memset(wi_s_raw[32:64, :].bitcast(I32), 0)
-        nc.vector.memset(wi_s_raw[64:P, :].bitcast(I32), 0)
-        for a in range(PASSES):
-            nc.vector.memset(planes[a][:].bitcast(I32), 0)
+        staging = late.tile([P, late_bytes[-1]], U8, name="staging", align_bytes=64, offset=0)
+        v_s = staging[:, 0:S]
 
         def load_tab(a):
             nc.sync.dma_start(out=tab[a][:], in_=tab_words[a].rearrange("p t i -> p (t i)").bitcast(I32))
@@ -90,88 +93,43 @@ def tile_list_prepayment_burnout_cap_kernel(
                 out=h[u][:], in_=burn.rearrange("(p t) j -> p t j", t=PACK)[:, :, u * HALF : (u + 1) * HALF]
             )
 
-        loads = {
-            "offs": lambda: nc.sync.dma_start(offsets[:], offs),
-            "ts": lambda: load_scale_rows(tab_s[0:ROWS, :], tab_scales),
-            "wis": lambda: load_scale_rows(wi_s_raw[0:ROWS, :], wi_scales),
-            "wcs": lambda: load_scale_rows(rows[0:ROWS, WC_COL:PLANE], wc_scales),
-            "wi": lambda: nc.sync.dma_start(
-                out=wi_raw[:].rearrange("p (a c) -> p a c", a=PASSES).bitcast(I32),
-                in_=wi_words.rearrange("a p c -> p a c").bitcast(I32)),
-            "wc": lambda: nc.sync.dma_start(
+        def load_wc():
+            nc.sync.dma_start(
                 out=wc_q[:].rearrange("p (a c) -> p a c", a=PASSES),
-                in_=wc_words.rearrange("a p c i -> p a (c i)").bitcast(I32)),
-            "wl": lambda: nc.sync.dma_start(out=wl_raw[:], in_=wl.rearrange("(p j) c -> p j c", j=PACK)),
-            "tab0": lambda: load_tab(0), "tab1": lambda: load_tab(1), "we0": lambda: load_we(0),
-            "we1": lambda: load_we(1), "burn0": lambda: load_burn(0), "burn1": lambda: load_burn(1),
-        }
-        def load(k):
-            for name in CFG["loads"][k].split():
-                loads[name]()
+                in_=wc_words.rearrange("a p c i -> p a (c i)").bitcast(I32),
+            )
 
-        load(0)
+        def load_wl():
+            nc.sync.dma_start(out=wl_raw[:], in_=wl.rearrange("(p j) c -> p j c", j=PACK))
 
-        def gp_copy(out, in_):
-            nc.gpsimd.tensor_scalar(out, in_, 1.0, 0.0, ALU.mult, ALU.add)
-
-        copies = {"S": nc.scalar.copy, "V": nc.vector.tensor_copy, "G": gp_copy}
-        adders = {"V": nc.vector, "G": nc.gpsimd}
+        def move_planes(a):
+            for r in range(4):
+                nc.sync.dma_start(
+                    out=planes[a][r:P:32, :].bitcast(I32), in_=rows[16 * a + r : 16 * (a + 1) : 4, :].bitcast(I32)
+                )
 
         def gather(a, u):
             cols = HALF // 16
             nc.vector.tensor_copy(v[a][u][:], tab[a][:].bitcast(U32).indirect(offsets[:, u * cols : (u + 1) * cols]))
 
-        def quant_we(a, t0, t1, copy):
+        def weave_we(a, i, copy):
             copy(
-                out=we_bf[a][:, t0 * H : t1 * H].rearrange("p (t m j) -> p m j t", m=P, j=PACK),
-                in_=we_raw[a][:].rearrange("p j (m t) -> p m j t", t=PACK)[:, :, :, t0:t1],
-            )
-            nc.vector.quantize_mx(
-                out=we_q[a][:, t0 * P : t1 * P].bitcast(FP8X4), scales=we_s[a][:, t0 * P : t1 * P],
-                in_=we_bf[a][:, t0 * H : t1 * H],
+                out=we_bf[a][i][:].rearrange("p (t m j) -> p m j t", m=P, j=PACK),
+                in_=we_raw[a][:].rearrange("p j (m t) -> p m j t", t=PACK)[:, :, :, 2 * i : 2 * i + 2],
             )
 
-        nc.vector.tensor_copy(
-            out=rows[:, WI_COL:WC_COL].rearrange("p (t m) -> p m t", t=PACK),
-            in_=wi_s_raw[:].rearrange("p (m t) -> p m t", t=PACK),
-        )
-        nc.vector.tensor_copy(v_s[:], tab_s[:].indirect(offsets[:]))
-        nc.vector.tensor_copy(out=rows[:, V_COL:WI_COL].bitcast(I32), in_=v_s[:].bitcast(I32))
-        mover = {"G": nc.gpsimd, "S": nc.scalar, "P": nc.sync}[CFG["mover"]]
-        for a in range(PASSES):
-            for r in range(4):
-                mover.dma_start(
-                    out=planes[a][r:P:32, :].bitcast(I32), in_=rows[16 * a + r : 16 * (a + 1) : 4, :].bitcast(I32)
-                )
-            load(1 + a)
-        for u in range(HALVES):
-            gather(0, u)
-        load(3)
-        nc.vector.tensor_copy(
-            out=wi_q[:].bitcast(U16).rearrange("p (a t m) -> p a m t", a=PASSES, t=PACK),
-            in_=wi_raw[:].bitcast(U16).rearrange("p (a m t) -> p a m t", a=PASSES, t=PACK),
-        )
-        load(4)
-        if CFG["weearly"]:
-            quant_we(0, 0, PACK, copies[CFG["we0"]])
-        for u in range(HALVES):
-            gather(1, u)
-        if not CFG["weearly"]:
-            quant_we(0, 0, PACK, copies[CFG["we0"]])
-        load(5)
-        if len(CFG["we1"]) == 1:
-            quant_we(1, 0, PACK, copies[CFG["we1"]])
-        else:
-            quant_we(1, 0, 2, copies[CFG["we1"][0]])
-            quant_we(1, 2, PACK, copies[CFG["we1"][1]])
-
-        load(6)
+        def quant_we(a, i):
+            cols = slice(2 * i * P, 2 * (i + 1) * P)
+            nc.vector.quantize_mx(out=we_q[a][:, cols].bitcast(FP8X4), scales=we_s[a][:, cols], in_=we_bf[a][i][:])
 
         def v_plane(a, u):
             return planes[a][:, V_COL + u * HALF : V_COL + (u + 1) * HALF]
 
-        def inc_pass(u, accs, a):
-            for t in range(PACK):
+        def banks(pool):
+            return [pool.tile([P, HALF], F32, name="acc") for t in range(PACK)]
+
+        def inc_pass(u, accs, a, slices=range(PACK)):
+            for t in slices:
                 c0 = a * H + t * P
                 nc.tensor.matmul_mx(
                     out=accs[t][:], lhsT=wi_q[:, 2 * c0 : 2 * (c0 + P)].bitcast(FP4X4),
@@ -181,8 +139,8 @@ def tile_list_prepayment_burnout_cap_kernel(
                 if a == PASSES - 1:
                     nc.scalar.copy(out=inc[u][:, t, :], in_=accs[t][:])
 
-        def expo_pass(u, accs, a):
-            for t in range(PACK):
+        def expo_pass(u, accs, a, slices=range(PACK)):
+            for t in slices:
                 nc.tensor.matmul_mx(
                     out=accs[t][:], lhsT=we_q[a][:, t * P : (t + 1) * P].bitcast(FP8X4),
                     lhsT_scale=we_s[a][:, t * P : (t + 1) * P],
@@ -192,28 +150,27 @@ def tile_list_prepayment_burnout_cap_kernel(
                 if a == PASSES - 1:
                     nc.vector.tensor_tensor(prod[u][:, t, :], accs[t][:], inc[u][:, t, :], ALU.mult)
 
-        def banks(pool, name):
-            return [pool.tile([P, HALF], F32, name=name) for t in range(PACK)]
-
-        def interleave(engine_copy, dst, src):
-            engine_copy(
+        def weave(copy, dst, src):
+            copy(
                 out=dst.rearrange("p (c i t) -> p c t i", i=4, t=PACK),
                 in_=src.rearrange("p t (c i) -> p c t i", i=4),
             )
 
-        def add_half(u):
-            n = PACK // len(CFG["add"][u])
-            for i, e in enumerate(CFG["add"][u]):
+        def add_burn(u, engines):
+            n = PACK // len(engines)
+            for i, engine in enumerate(engines):
                 ts = slice(n * i, n * (i + 1))
-                adders[e].tensor_tensor(h[u][:, ts, :], h[u][:, ts, :], prod[u][:, ts, :], ALU.add)
+                engine.tensor_tensor(h[u][:, ts, :], h[u][:, ts, :], prod[u][:, ts, :], ALU.add)
             nc.sync.dma_start(
                 out=out_1.rearrange("(p t) j -> p t j", t=PACK)[:, :, u * HALF : (u + 1) * HALF], in_=h[u][:]
             )
-            w = HALF // len(CFG["hil"][u])
-            for i, e in enumerate(CFG["hil"][u]):
-                interleave(copies[e], h_bf[u][:, PACK * w * i : PACK * w * (i + 1)], h[u][:, :, w * i : w * (i + 1)])
 
-        def quant_half(u):
+        def weave_h(u, copies):
+            w = HALF // len(copies)
+            for i, copy in enumerate(copies):
+                weave(copy, h_bf[u][:, PACK * w * i : PACK * w * (i + 1)], h[u][:, :, w * i : w * (i + 1)])
+
+        def quant_h(u):
             nc.vector.quantize_mx(
                 out=h_q[u][:].bitcast(FP8X4), scales=h_s[:, u * HALF : (u + 1) * HALF], in_=h_bf[u][:]
             )
@@ -221,9 +178,16 @@ def tile_list_prepayment_burnout_cap_kernel(
                 out=out_2[0].rearrange("p m t -> p (m t)").bitcast(I32)[:, u * HALF : (u + 1) * HALF], in_=h_q[u][:]
             )
 
-        def cap_half(u, n0, n1):
-            for n in range(n0, n1):
-                acc = psum_s.tile([P, HALF], F32, name="acc_s")
+        def weave_wl(i, copy):
+            weave(copy, wl_bf[i][:], wl_raw[:, :, WL_PIECE * i : WL_PIECE * (i + 1)])
+
+        def quant_wl(i):
+            cols = slice(WL_PIECE * i, WL_PIECE * (i + 1))
+            nc.vector.quantize_mx(out=wl_q[:, cols].bitcast(FP8X4), scales=wl_s[:, cols], in_=wl_bf[i][:])
+
+        def cap_tiles(u, tiles):
+            for n in tiles:
+                acc = psum_a.tile([P, HALF], F32, name="acc")
                 for a in range(PASSES):
                     c0 = a * N + n * P
                     nc.tensor.matmul_mx(
@@ -234,56 +198,103 @@ def tile_list_prepayment_burnout_cap_kernel(
                     )
                 nc.scalar.copy(out=y[u][:, n, :], in_=acc[:])
 
-        def load_half(u):
-            for n in range(N_TILES):
-                acc = psum_v.tile([P, HALF], F32, name="acc_v")
-                nc.tensor.matmul_mx(
-                    out=acc[:], lhsT=wl_q[:, n * P : (n + 1) * P].bitcast(FP8X4), lhsT_scale=wl_s[:, n * P : (n + 1) * P],
-                    rhs=h_q[u][:].bitcast(FP8X4), rhs_scale=h_s[:, u * HALF : (u + 1) * HALF], start=True, stop=True,
+        def min_tiles(u, groups):
+            for n0, n1 in groups:
+                for n in range(n0, n1):
+                    acc = psum_b.tile([P, HALF], F32, name="acc")
+                    nc.tensor.matmul_mx(
+                        out=acc[:], lhsT=wl_q[:, n * P : (n + 1) * P].bitcast(FP8X4),
+                        lhsT_scale=wl_s[:, n * P : (n + 1) * P], rhs=h_q[u][:].bitcast(FP8X4),
+                        rhs_scale=h_s[:, u * HALF : (u + 1) * HALF], start=True, stop=True,
+                    )
+                    nc.vector.tensor_tensor(y[u][:, n, :], acc[:], y[u][:, n, :], ALU.min)
+                nc.sync.dma_start(
+                    out=out_0.rearrange("(n p) j -> p n j", p=P)[:, n0:n1, u * HALF : (u + 1) * HALF],
+                    in_=y[u][:, n0:n1, :],
                 )
-                nc.vector.tensor_tensor(y[u][:, n, :], acc[:], y[u][:, n, :], ALU.min)
-                first = {1: 0, 3: 2, 5: 4} if u == 0 else {1: 0, 3: 2, 4: 4, 5: 5}
-                if n in first:
-                    nc.sync.dma_start(
-                        out=out_0.rearrange("(n p) j -> p n j", p=P)[:, first[n] : n + 1, u * HALF : (u + 1) * HALF],
-                        in_=y[u][:, first[n] : n + 1, :],
-                    )
 
-        state = {}
+        def store_h_scales():
+            for r in range(QUADS):
+                nc.sync.dma_start(
+                    out=out_3[0].rearrange("(q r) m -> r q m", r=4)[r].bitcast(I32), in_=h_s[r:P:32, :].bitcast(I32)
+                )
 
-        def step(name):
-            kind, u = name[0], int(name[1])
-            if kind == "i":
-                a = int(name[2])
-                if a == 0:
-                    state["i"] = banks(psum_s, "acc_s")
-                inc_pass(u, state["i"], a)
-            elif kind == "e":
-                a = int(name[2])
-                if a == 0:
-                    state["e"] = banks(psum_v, "acc_v")
-                expo_pass(u, state["e"], a)
-            elif kind == "a":
-                add_half(u)
-            elif kind == "q":
-                quant_half(u)
-            elif kind == "c":
-                cap_half(u, int(name[2]), int(name[3]))
-            elif kind == "l":
-                load_half(u)
-            elif kind == "w":
-                wl_bf = keep.tile([P, N * PACK], BF16, name="wl_bf", tag=CFG["wltag"], align_bytes=64)
-                for i, e in enumerate(CFG["wl"]):
-                    c0, c1 = 256 * i, 256 * (i + 1)
-                    interleave(copies[e], wl_bf[:, PACK * c0 : PACK * c1], wl_raw[:, :, c0:c1])
-                    nc.vector.quantize_mx(
-                        out=wl_q[:, c0:c1].bitcast(FP8X4), scales=wl_s[:, c0:c1], in_=wl_bf[:, PACK * c0 : PACK * c1]
-                    )
-            elif kind == "s":
-                for q in range(QUADS):
-                    nc.sync.dma_start(
-                        out=out_3[0].rearrange("(q r) m -> r q m", r=4)[q].bitcast(I32), in_=h_s[q:P:32, :].bitcast(I32)
-                    )
+        on_v, on_s = nc.vector.tensor_copy, nc.scalar.copy
 
-        for name in CFG["steps"].split():
-            step(name)
+        nc.sync.dma_start(offsets[:], offs)
+        load_scale_rows(wi_s_raw[0:ROWS, :], wi_scales)
+        load_scale_rows(tab_s[0:ROWS, :], tab_scales)
+        load_scale_rows(rows[0:ROWS, WC_COL:PLANE], wc_scales)
+        nc.sync.dma_start(
+            out=wi_raw[:].rearrange("p (a c) -> p a c", a=PASSES).bitcast(I32),
+            in_=wi_words.rearrange("a p c -> p a c").bitcast(I32),
+        )
+        load_tab(0)
+        load_we(0)
+
+        for part in (slice(32, 64), slice(64, P)):
+            nc.vector.memset(wi_s_raw[part, :].bitcast(I32), 0)
+        nc.vector.memset(tab_s[64:P, :].bitcast(I32), 0)
+        nc.gpsimd.memset(tab_s[32:64, :].bitcast(I32), 0)
+        for a in range(PASSES):
+            nc.gpsimd.memset(planes[a][:].bitcast(I32), 0)
+
+        nc.vector.tensor_copy(
+            out=rows[:, WI_COL:WC_COL].rearrange("p (t m) -> p m t", t=PACK),
+            in_=wi_s_raw[:].rearrange("p (m t) -> p m t", t=PACK),
+        )
+        nc.vector.tensor_copy(v_s, tab_s[:].indirect(offsets[:]))
+        nc.vector.tensor_copy(out=rows[:, V_COL:WI_COL].bitcast(I32), in_=v_s.bitcast(I32))
+        nc.vector.tensor_copy(
+            out=wi_q[:].bitcast(U16).rearrange("p (a t m) -> p a m t", a=PASSES, t=PACK),
+            in_=wi_raw[:].bitcast(U16).rearrange("p (a m t) -> p a m t", a=PASSES, t=PACK),
+        )
+        move_planes(0)
+        load_tab(1)
+        move_planes(1)
+        load_we(1)
+        load_burn(0)
+        load_wc()
+        load_wl()
+        load_burn(1)
+
+        inc_banks, expo_banks = banks(psum_a), banks(psum_b)
+        gather(0, 0)
+        inc_pass(0, inc_banks, 0)
+        gather(0, 1)
+        for i in range(2):
+            weave_we(0, i, on_v)
+        for i in range(2):
+            quant_we(0, i)
+        expo_pass(0, expo_banks, 0)
+        gather(1, 0)
+        inc_pass(0, inc_banks, 1)
+        gather(1, 1)
+        for i in range(2):
+            weave_we(1, i, on_v)
+            quant_we(1, i)
+        expo_pass(0, expo_banks, 1)
+        inc_banks, expo_banks = banks(psum_a), banks(psum_b)
+        for t in range(PACK):
+            for a in range(PASSES):
+                inc_pass(1, inc_banks, a, [t])
+        add_burn(0, [nc.vector, nc.vector])
+        weave_h(0, [on_s])
+        for t in range(PACK):
+            for a in range(PASSES):
+                expo_pass(1, expo_banks, a, [t])
+        weave_wl(0, on_v)
+        weave_wl(1, on_s)
+        weave_wl(2, on_s)
+        quant_h(0)
+        quant_wl(0)
+        add_burn(1, [nc.vector, nc.vector])
+        quant_wl(1)
+        quant_wl(2)
+        cap_tiles(0, range(N_TILES))
+        weave_h(1, [on_s])
+        cap_tiles(1, range(N_TILES))
+        min_tiles(0, [(0, 2), (2, 4), (4, 6)])
+        quant_h(1)
+        store_h_scales()
+        min_tiles(1, [(0, 2), (2, 4), (4, 5), (5, 6)])

@@ -25,6 +25,7 @@ QUADS = 4
 ROWS = PASSES * 16
 V_COL, WI_COL, WC_COL, PLANE = 0, S, S + H, S + H + N
 WL_PIECE = 256
+GROUPS = (((0, 2), (2, 4), (4, 6)), ((0, 2), (2, 4), (4, 5), (5, 6)))
 
 
 def tile_list_prepayment_burnout_cap_kernel(
@@ -64,16 +65,18 @@ def tile_list_prepayment_burnout_cap_kernel(
         we_s = [tile([P, H], U8, f"we_s{a}") for a in range(PASSES)]
         wl_raw = late_tile([P, PACK, N], F32, "wl_raw")
         wl_bf = [tile([P, WL_PIECE * PACK], BF16, f"wl_bf{i}") for i in range(N // WL_PIECE)]
-        wl_q = tile([P, N], U32, "wl_q")
-        wl_s = tile([P, N], U8, "wl_s")
+        wl_q = [tile([P, WL_PIECE], U32, f"wl_q{i}") for i in range(N // WL_PIECE)]
+        wl_s = [tile([P, WL_PIECE], U8, f"wl_s{i}") for i in range(N // WL_PIECE)]
         wc_q = late_tile([P, PASSES * N], I32, "wc_q")
-        h = [late_tile([P, PACK, HALF], F32, f"h{u}") for u in range(HALVES)]
+        burn_in = [late_tile([P, PACK, HALF], F32, f"burn_in{u}") for u in range(HALVES)]
         inc = [tile([P, PACK, HALF], F32, f"inc{u}") for u in range(HALVES)]
         prod = [tile([P, PACK, HALF], F32, f"prod{u}") for u in range(HALVES)]
+        h = [burn_in[0], tile([P, PACK, HALF], F32, "prod0")]
         h_bf = [tile([P, HALF * PACK], BF16, f"h_bf{u}") for u in range(HALVES)]
         h_q = [tile([P, HALF], I32, f"h_q{u}") for u in range(HALVES)]
         h_s = tile([P, S], U8, "h_s")
-        y = [tile([P, N_TILES, HALF], F32, f"y{u}") for u in range(HALVES)]
+        y_group = {(u, n0): tile([P, n1 - n0, HALF], F32, f"y{u}{n0}") for u in range(HALVES) for n0, n1 in GROUPS[u]}
+        y = [[y_group[u, n0][:, n - n0, :] for n0, n1 in GROUPS[u] for n in range(n0, n1)] for u in range(HALVES)]
         staging = late.tile([P, late_bytes[-1]], U8, name="staging", align_bytes=64, offset=0)
         v_s = staging[:, 0:S]
 
@@ -90,7 +93,7 @@ def tile_list_prepayment_burnout_cap_kernel(
 
         def load_burn(u):
             nc.sync.dma_start(
-                out=h[u][:], in_=burn.rearrange("(p t) j -> p t j", t=PACK)[:, :, u * HALF : (u + 1) * HALF]
+                out=burn_in[u][:], in_=burn.rearrange("(p t) j -> p t j", t=PACK)[:, :, u * HALF : (u + 1) * HALF]
             )
 
         def load_wc():
@@ -156,11 +159,10 @@ def tile_list_prepayment_burnout_cap_kernel(
                 in_=src.rearrange("p t (c i) -> p c t i", i=4),
             )
 
-        def add_burn(u, engines):
-            n = PACK // len(engines)
-            for i, engine in enumerate(engines):
-                ts = slice(n * i, n * (i + 1))
-                engine.tensor_tensor(h[u][:, ts, :], h[u][:, ts, :], prod[u][:, ts, :], ALU.add)
+        def add_burn(engine, u, t0, t1):
+            engine.tensor_tensor(h[u][:, t0:t1, :], burn_in[u][:, t0:t1, :], prod[u][:, t0:t1, :], ALU.add)
+
+        def store_h(u):
             nc.sync.dma_start(
                 out=out_1.rearrange("(p t) j -> p t j", t=PACK)[:, :, u * HALF : (u + 1) * HALF], in_=h[u][:]
             )
@@ -182,36 +184,34 @@ def tile_list_prepayment_burnout_cap_kernel(
             weave(copy, wl_bf[i][:], wl_raw[:, :, WL_PIECE * i : WL_PIECE * (i + 1)])
 
         def quant_wl(i):
-            cols = slice(WL_PIECE * i, WL_PIECE * (i + 1))
-            nc.vector.quantize_mx(out=wl_q[:, cols].bitcast(FP8X4), scales=wl_s[:, cols], in_=wl_bf[i][:])
+            nc.vector.quantize_mx(out=wl_q[i][:].bitcast(FP8X4), scales=wl_s[i][:], in_=wl_bf[i][:])
 
-        def cap_tiles(u, tiles):
-            for n in tiles:
-                acc = psum_a.tile([P, HALF], F32, name="acc")
-                for a in range(PASSES):
-                    c0 = a * N + n * P
-                    nc.tensor.matmul_mx(
-                        out=acc[:], lhsT=wc_q[:, c0 : c0 + P].bitcast(FP8X4),
-                        lhsT_scale=planes[a][:, WC_COL + n * P : WC_COL + (n + 1) * P],
-                        rhs=v[a][u][:].bitcast(FP8X4), rhs_scale=v_plane(a, u),
-                        start=(a == 0), stop=(a == PASSES - 1),
-                    )
-                nc.scalar.copy(out=y[u][:, n, :], in_=acc[:])
-
-        def min_tiles(u, groups):
-            for n0, n1 in groups:
-                for n in range(n0, n1):
-                    acc = psum_b.tile([P, HALF], F32, name="acc")
-                    nc.tensor.matmul_mx(
-                        out=acc[:], lhsT=wl_q[:, n * P : (n + 1) * P].bitcast(FP8X4),
-                        lhsT_scale=wl_s[:, n * P : (n + 1) * P], rhs=h_q[u][:].bitcast(FP8X4),
-                        rhs_scale=h_s[:, u * HALF : (u + 1) * HALF], start=True, stop=True,
-                    )
-                    nc.vector.tensor_tensor(y[u][:, n, :], acc[:], y[u][:, n, :], ALU.min)
-                nc.sync.dma_start(
-                    out=out_0.rearrange("(n p) j -> p n j", p=P)[:, n0:n1, u * HALF : (u + 1) * HALF],
-                    in_=y[u][:, n0:n1, :],
+        def cap_tile(n, u):
+            acc = psum_a.tile([P, HALF], F32, name="acc")
+            for a in range(PASSES):
+                c0 = a * N + n * P
+                nc.tensor.matmul_mx(
+                    out=acc[:], lhsT=wc_q[:, c0 : c0 + P].bitcast(FP8X4),
+                    lhsT_scale=planes[a][:, WC_COL + n * P : WC_COL + (n + 1) * P],
+                    rhs=v[a][u][:].bitcast(FP8X4), rhs_scale=v_plane(a, u),
+                    start=(a == 0), stop=(a == PASSES - 1),
                 )
+            nc.scalar.copy(out=y[u][n], in_=acc[:])
+
+        def min_tile(n, u):
+            acc = psum_b.tile([P, HALF], F32, name="acc")
+            nc.tensor.matmul_mx(
+                out=acc[:], lhsT=wl_q[n // 2][:, n % 2 * P : (n % 2 + 1) * P].bitcast(FP8X4),
+                lhsT_scale=wl_s[n // 2][:, n % 2 * P : (n % 2 + 1) * P], rhs=h_q[u][:].bitcast(FP8X4),
+                rhs_scale=h_s[:, u * HALF : (u + 1) * HALF], start=True, stop=True,
+            )
+            nc.vector.tensor_tensor(y[u][n], acc[:], y[u][n], ALU.min)
+
+        def store_y(u, n0, n1):
+            nc.sync.dma_start(
+                out=out_0.rearrange("(n p) j -> p n j", p=P)[:, n0:n1, u * HALF : (u + 1) * HALF],
+                in_=y_group[u, n0][:],
+            )
 
         def store_h_scales():
             for r in range(QUADS):
@@ -255,8 +255,8 @@ def tile_list_prepayment_burnout_cap_kernel(
         load_we(1)
         load_burn(0)
         load_wc()
-        load_wl()
         load_burn(1)
+        load_wl()
 
         inc_banks, expo_banks = banks(psum_a), banks(psum_b)
         gather(0, 0)
@@ -278,23 +278,39 @@ def tile_list_prepayment_burnout_cap_kernel(
         for t in range(PACK):
             for a in range(PASSES):
                 inc_pass(1, inc_banks, a, [t])
-        add_burn(0, [nc.vector, nc.vector])
+        for t in range(2):
+            add_burn(nc.gpsimd, 0, t, t + 1)
+        for a in range(PASSES):
+            expo_pass(1, expo_banks, a, [0])
+        add_burn(nc.vector, 0, 2, PACK)
+        store_h(0)
         weave_h(0, [on_s])
-        for t in range(PACK):
+        add_burn(nc.gpsimd, 1, 0, 1)
+        for t in range(1, PACK):
             for a in range(PASSES):
                 expo_pass(1, expo_banks, a, [t])
+        add_burn(nc.vector, 1, 1, PACK)
+        store_h(1)
         weave_wl(0, on_v)
-        weave_wl(1, on_s)
-        weave_wl(2, on_s)
-        quant_h(0)
+        weave_wl(1, on_v)
         quant_wl(0)
-        add_burn(1, [nc.vector, nc.vector])
+        quant_h(0)
         quant_wl(1)
-        quant_wl(2)
-        cap_tiles(0, range(N_TILES))
+        for n in range(4):
+            cap_tile(n, 0)
+        weave_wl(2, on_s)
+        for n in range(4, N_TILES):
+            cap_tile(n, 0)
         weave_h(1, [on_s])
-        cap_tiles(1, range(N_TILES))
-        min_tiles(0, [(0, 2), (2, 4), (4, 6)])
-        quant_h(1)
-        store_h_scales()
-        min_tiles(1, [(0, 2), (2, 4), (4, 5), (5, 6)])
+        for n in range(N_TILES):
+            cap_tile(n, 1)
+        for u in range(HALVES):
+            for n0, n1 in GROUPS[u]:
+                for n in range(n0, n1):
+                    min_tile(n, u)
+                store_y(u, n0, n1)
+                if (u, n0) == (0, 0):
+                    quant_wl(2)
+            if u == 0:
+                quant_h(1)
+                store_h_scales()

@@ -1,3 +1,4 @@
+import math
 from contextlib import ExitStack
 
 import concourse.mybir as mybir
@@ -16,16 +17,22 @@ FP4X4 = mybir.dt.float4_e2m1fn_x4
 ALU = mybir.AluOpType
 
 P = 128
+ALIGN = 256
 PACK = 4
-PASSES = K // (P * PACK)
+K_PASS = P * PACK
+PASSES = K // K_PASS
 HALF = 512
 HALVES = S // HALF
 N_TILES = N // P
-QUADS = 4
-ROWS = PASSES * 16
+QUADRANT = 32
+LIVE = 4
+BLOCKS = 16
+ROWS = PASSES * BLOCKS
 V_COL, WI_COL, WC_COL, PLANE = 0, S, S + H, S + H + N
-WL_PIECE = 256
+WL_PIECE = 2 * P
 GROUPS = (((0, 2), (2, 4), (4, 6)), ((0, 2), (2, 4), (4, 5), (5, 6)))
+GPSIMD_SLICES = (2, 1)
+CAPS_FIRST = 4
 
 
 def tile_list_prepayment_burnout_cap_kernel(
@@ -41,18 +48,17 @@ def tile_list_prepayment_burnout_cap_kernel(
         psum_b = ctx.enter_context(tc.psum_pool(name="psum_b", bufs=4))
 
         def tile(shape, dtype, name):
-            return keep.tile(shape, dtype, name=name, align_bytes=64)
+            return keep.tile(shape, dtype, name=name, align_bytes=ALIGN)
 
         late_bytes = [0]
 
         def late_tile(shape, dtype, name):
             start = late_bytes[-1]
-            late_bytes.append(start + 4 * shape[1] * (shape[2] if len(shape) > 2 else 1))
-            return late.tile(shape, dtype, name=name, align_bytes=64, offset=start)
+            late_bytes.append(start + 4 * math.prod(shape[1:]))
+            return late.tile(shape, dtype, name=name, align_bytes=ALIGN, offset=start)
 
         offsets = lists.tile([P, S // 16], U16, name="offsets")
         tab_s = tile([P, T], U8, "tab_s")
-        rows = tile([P, PLANE], U8, "rows")
         planes = [tile([P, PLANE], U8, f"planes{a}") for a in range(PASSES)]
         wi_raw = tile([P, PASSES * 2 * H], U8, "wi_raw")
         wi_s_raw = tile([P, H], U8, "wi_s_raw")
@@ -77,8 +83,11 @@ def tile_list_prepayment_burnout_cap_kernel(
         h_s = tile([P, S], U8, "h_s")
         y_group = {(u, n0): tile([P, n1 - n0, HALF], F32, f"y{u}{n0}") for u in range(HALVES) for n0, n1 in GROUPS[u]}
         y = [[y_group[u, n0][:, n - n0, :] for n0, n1 in GROUPS[u] for n in range(n0, n1)] for u in range(HALVES)]
-        staging = late.tile([P, late_bytes[-1]], U8, name="staging", align_bytes=64, offset=0)
-        v_s = staging[:, 0:S]
+        first = late_bytes[2]
+        v_s_area = late.tile([P, first], U8, name="v_s_area", align_bytes=ALIGN, offset=0)
+        v_s = v_s_area[:, 0:S]
+        rows_area = late.tile([P, late_bytes[-1] - first], U8, name="rows_area", align_bytes=ALIGN, offset=first)
+        rows = rows_area[:, 0:PLANE]
 
         def load_tab(a):
             nc.sync.dma_start(out=tab[a][:], in_=tab_words[a].rearrange("p t i -> p (t i)").bitcast(I32))
@@ -88,7 +97,7 @@ def tile_list_prepayment_burnout_cap_kernel(
 
         def load_we(a):
             nc.sync.dma_start(
-                out=we_raw[a][:], in_=we[512 * a : 512 * (a + 1), :].rearrange("(p j) c -> p j c", j=PACK)
+                out=we_raw[a][:], in_=we[K_PASS * a : K_PASS * (a + 1), :].rearrange("(p j) c -> p j c", j=PACK)
             )
 
         def load_burn(u):
@@ -105,18 +114,19 @@ def tile_list_prepayment_burnout_cap_kernel(
         def load_wl():
             nc.sync.dma_start(out=wl_raw[:], in_=wl.rearrange("(p j) c -> p j c", j=PACK))
 
-        def move_planes(a):
-            for r in range(4):
-                nc.sync.dma_start(
-                    out=planes[a][r:P:32, :].bitcast(I32), in_=rows[16 * a + r : 16 * (a + 1) : 4, :].bitcast(I32)
+        def move_planes(a, queue):
+            for r in range(LIVE):
+                queue.dma_start(
+                    out=planes[a][r:P:QUADRANT, :].bitcast(I32),
+                    in_=rows[BLOCKS * a + r : BLOCKS * (a + 1) : LIVE, :].bitcast(I32),
                 )
 
         def gather(a, u):
             cols = HALF // 16
             nc.vector.tensor_copy(v[a][u][:], tab[a][:].bitcast(U32).indirect(offsets[:, u * cols : (u + 1) * cols]))
 
-        def weave_we(a, i, copy):
-            copy(
+        def weave_we(a, i):
+            nc.vector.tensor_copy(
                 out=we_bf[a][i][:].rearrange("p (t m j) -> p m j t", m=P, j=PACK),
                 in_=we_raw[a][:].rearrange("p j (m t) -> p m j t", t=PACK)[:, :, :, 2 * i : 2 * i + 2],
             )
@@ -167,10 +177,8 @@ def tile_list_prepayment_burnout_cap_kernel(
                 out=out_1.rearrange("(p t) j -> p t j", t=PACK)[:, :, u * HALF : (u + 1) * HALF], in_=h[u][:]
             )
 
-        def weave_h(u, copies):
-            w = HALF // len(copies)
-            for i, copy in enumerate(copies):
-                weave(copy, h_bf[u][:, PACK * w * i : PACK * w * (i + 1)], h[u][:, :, w * i : w * (i + 1)])
+        def weave_h(u):
+            weave(nc.scalar.copy, h_bf[u][:], h[u][:])
 
         def quant_h(u):
             nc.vector.quantize_mx(
@@ -200,9 +208,10 @@ def tile_list_prepayment_burnout_cap_kernel(
 
         def min_tile(n, u):
             acc = psum_b.tile([P, HALF], F32, name="acc")
+            piece, c0 = divmod(n * P, WL_PIECE)
             nc.tensor.matmul_mx(
-                out=acc[:], lhsT=wl_q[n // 2][:, n % 2 * P : (n % 2 + 1) * P].bitcast(FP8X4),
-                lhsT_scale=wl_s[n // 2][:, n % 2 * P : (n % 2 + 1) * P], rhs=h_q[u][:].bitcast(FP8X4),
+                out=acc[:], lhsT=wl_q[piece][:, c0 : c0 + P].bitcast(FP8X4),
+                lhsT_scale=wl_s[piece][:, c0 : c0 + P], rhs=h_q[u][:].bitcast(FP8X4),
                 rhs_scale=h_s[:, u * HALF : (u + 1) * HALF], start=True, stop=True,
             )
             nc.vector.tensor_tensor(y[u][n], acc[:], y[u][n], ALU.min)
@@ -214,12 +223,11 @@ def tile_list_prepayment_burnout_cap_kernel(
             )
 
         def store_h_scales():
-            for r in range(QUADS):
+            for r in range(LIVE):
                 nc.sync.dma_start(
-                    out=out_3[0].rearrange("(q r) m -> r q m", r=4)[r].bitcast(I32), in_=h_s[r:P:32, :].bitcast(I32)
+                    out=out_3[0].rearrange("(q r) m -> r q m", r=LIVE)[r].bitcast(I32),
+                    in_=h_s[r:P:QUADRANT, :].bitcast(I32),
                 )
-
-        on_v, on_s = nc.vector.tensor_copy, nc.scalar.copy
 
         nc.sync.dma_start(offsets[:], offs)
         load_scale_rows(wi_s_raw[0:ROWS, :], wi_scales)
@@ -249,9 +257,10 @@ def tile_list_prepayment_burnout_cap_kernel(
             out=wi_q[:].bitcast(U16).rearrange("p (a t m) -> p a m t", a=PASSES, t=PACK),
             in_=wi_raw[:].bitcast(U16).rearrange("p (a m t) -> p a m t", a=PASSES, t=PACK),
         )
-        move_planes(0)
+
+        move_planes(0, nc.sync)
         load_tab(1)
-        move_planes(1)
+        move_planes(1, nc.gpsimd)
         load_we(1)
         load_burn(0)
         load_wc()
@@ -263,7 +272,7 @@ def tile_list_prepayment_burnout_cap_kernel(
         inc_pass(0, inc_banks, 0)
         gather(0, 1)
         for i in range(2):
-            weave_we(0, i, on_v)
+            weave_we(0, i)
         for i in range(2):
             quant_we(0, i)
         expo_pass(0, expo_banks, 0)
@@ -271,39 +280,42 @@ def tile_list_prepayment_burnout_cap_kernel(
         inc_pass(0, inc_banks, 1)
         gather(1, 1)
         for i in range(2):
-            weave_we(1, i, on_v)
+            weave_we(1, i)
             quant_we(1, i)
         expo_pass(0, expo_banks, 1)
+
         inc_banks, expo_banks = banks(psum_a), banks(psum_b)
         for t in range(PACK):
             for a in range(PASSES):
                 inc_pass(1, inc_banks, a, [t])
-        for t in range(2):
+        for t in range(GPSIMD_SLICES[0]):
             add_burn(nc.gpsimd, 0, t, t + 1)
         for a in range(PASSES):
             expo_pass(1, expo_banks, a, [0])
-        add_burn(nc.vector, 0, 2, PACK)
+        add_burn(nc.vector, 0, GPSIMD_SLICES[0], PACK)
         store_h(0)
-        weave_h(0, [on_s])
-        add_burn(nc.gpsimd, 1, 0, 1)
+        weave_h(0)
+        add_burn(nc.gpsimd, 1, 0, GPSIMD_SLICES[1])
         for t in range(1, PACK):
             for a in range(PASSES):
                 expo_pass(1, expo_banks, a, [t])
-        add_burn(nc.vector, 1, 1, PACK)
+        add_burn(nc.vector, 1, GPSIMD_SLICES[1], PACK)
         store_h(1)
-        weave_wl(0, on_v)
-        weave_wl(1, on_v)
+
+        weave_wl(0, nc.vector.tensor_copy)
+        weave_wl(1, nc.vector.tensor_copy)
         quant_wl(0)
         quant_h(0)
         quant_wl(1)
-        for n in range(4):
+        for n in range(CAPS_FIRST):
             cap_tile(n, 0)
-        weave_wl(2, on_s)
-        for n in range(4, N_TILES):
+        weave_wl(2, nc.scalar.copy)
+        for n in range(CAPS_FIRST, N_TILES):
             cap_tile(n, 0)
-        weave_h(1, [on_s])
+        weave_h(1)
         for n in range(N_TILES):
             cap_tile(n, 1)
+
         for u in range(HALVES):
             for n0, n1 in GROUPS[u]:
                 for n in range(n0, n1):

@@ -31,7 +31,7 @@ ROWS = PASSES * BLOCKS
 V_COL, WI_COL, WC_COL, PLANE = 0, S, S + H, S + H + N
 WL_PIECE = 2 * P
 GROUPS = (((0, 2), (2, 4), (4, 6)), ((0, 2), (2, 4), (4, 5), (5, 6)))
-GPSIMD_SLICES = (2, 1)
+GPSIMD_SLICES = (3, 0)
 CAPS_FIRST = 4
 
 
@@ -59,13 +59,14 @@ def tile_list_prepayment_burnout_cap_kernel(
 
         offsets = lists.tile([P, S // 16], U16, name="offsets")
         tab_s = tile([P, T], U8, "tab_s")
-        planes = [tile([P, PLANE], U8, f"planes{a}") for a in range(PASSES)]
+        plane_pair = tile([P, PASSES * PLANE], U8, "plane_pair")
+        planes = [plane_pair[:, a * PLANE : (a + 1) * PLANE] for a in range(PASSES)]
         wi_raw = tile([P, PASSES * 2 * H], U8, "wi_raw")
         wi_s_raw = tile([P, H], U8, "wi_s_raw")
         wi_q = tile([P, PASSES * 2 * H], U8, "wi_q")
         tab = [tile([P, T], I32, "tab0"), late_tile([P, T], I32, "tab1")]
         v = [[tile([P, HALF], U32, f"v{a}{u}") for u in range(HALVES)] for a in range(PASSES)]
-        we_raw = [tile([P, PACK, H], F32, "we_raw0"), late_tile([P, PACK, H], F32, "we_raw1")]
+        we_raw = [late_tile([P, PACK, H], F32, f"we_raw{a}") for a in range(PASSES)]
         we_bf = [[tile([P, H * 2], BF16, f"we_bf{a}{i}") for i in range(2)] for a in range(PASSES)]
         we_q = [tile([P, H], U32, f"we_q{a}") for a in range(PASSES)]
         we_s = [tile([P, H], U8, f"we_s{a}") for a in range(PASSES)]
@@ -83,17 +84,15 @@ def tile_list_prepayment_burnout_cap_kernel(
         h_s = tile([P, S], U8, "h_s")
         y_group = {(u, n0): tile([P, n1 - n0, HALF], F32, f"y{u}{n0}") for u in range(HALVES) for n0, n1 in GROUPS[u]}
         y = [[y_group[u, n0][:, n - n0, :] for n0, n1 in GROUPS[u] for n in range(n0, n1)] for u in range(HALVES)]
-        first = late_bytes[2]
-        v_s_area = late.tile([P, first], U8, name="v_s_area", align_bytes=ALIGN, offset=0)
+        v_s_area = late.tile([P, late_bytes[-1]], U8, name="v_s_area", align_bytes=ALIGN, offset=0)
         v_s = v_s_area[:, 0:S]
-        rows_area = late.tile([P, late_bytes[-1] - first], U8, name="rows_area", align_bytes=ALIGN, offset=first)
-        rows = rows_area[:, 0:PLANE]
+        rows = tile([P, PLANE], U8, "rows")
 
         def load_tab(a):
             nc.sync.dma_start(out=tab[a][:], in_=tab_words[a].rearrange("p t i -> p (t i)").bitcast(I32))
 
         def load_scale_rows(dst, src):
-            nc.sync.dma_start(out=dst.bitcast(I32), in_=src.rearrange("a q c -> (a q) c").bitcast(I32))
+            nc.sync.dma_start(out=dst.bitcast(I32), in_=src.rearrange("a q c -> q a c").bitcast(I32))
 
         def load_we(a):
             nc.sync.dma_start(
@@ -114,11 +113,11 @@ def tile_list_prepayment_burnout_cap_kernel(
         def load_wl():
             nc.sync.dma_start(out=wl_raw[:], in_=wl.rearrange("(p j) c -> p j c", j=PACK))
 
-        def move_planes(a, queue):
-            for r in range(LIVE):
-                queue.dma_start(
-                    out=planes[a][r:P:QUADRANT, :].bitcast(I32),
-                    in_=rows[BLOCKS * a + r : BLOCKS * (a + 1) : LIVE, :].bitcast(I32),
+        def move_planes():
+            for quad in range(P // QUADRANT):
+                nc.sync.dma_start(
+                    out=plane_pair[QUADRANT * quad : QUADRANT * quad + LIVE, :].rearrange("p (a c) -> p a c", a=PASSES).bitcast(I32),
+                    in_=rows[PASSES * LIVE * quad : PASSES * LIVE * (quad + 1), :].bitcast(I32),
                 )
 
         def gather(a, u):
@@ -233,19 +232,17 @@ def tile_list_prepayment_burnout_cap_kernel(
         load_scale_rows(wi_s_raw[0:ROWS, :], wi_scales)
         load_scale_rows(tab_s[0:ROWS, :], tab_scales)
         load_scale_rows(rows[0:ROWS, WC_COL:PLANE], wc_scales)
+        load_tab(0)
         nc.sync.dma_start(
             out=wi_raw[:].rearrange("p (a c) -> p a c", a=PASSES).bitcast(I32),
             in_=wi_words.rearrange("a p c -> p a c").bitcast(I32),
         )
-        load_tab(0)
-        load_we(0)
 
         for part in (slice(32, 64), slice(64, P)):
             nc.vector.memset(wi_s_raw[part, :].bitcast(I32), 0)
         nc.vector.memset(tab_s[64:P, :].bitcast(I32), 0)
         nc.gpsimd.memset(tab_s[32:64, :].bitcast(I32), 0)
-        for a in range(PASSES):
-            nc.gpsimd.memset(planes[a][:].bitcast(I32), 0)
+        nc.gpsimd.memset(plane_pair[:].bitcast(I32), 0)
 
         nc.vector.tensor_copy(
             out=rows[:, WI_COL:WC_COL].rearrange("p (t m) -> p m t", t=PACK),
@@ -258,48 +255,39 @@ def tile_list_prepayment_burnout_cap_kernel(
             in_=wi_raw[:].bitcast(U16).rearrange("p (a m t) -> p a m t", a=PASSES, t=PACK),
         )
 
-        move_planes(0, nc.sync)
+        move_planes()
         load_tab(1)
-        move_planes(1, nc.gpsimd)
+        load_we(0)
         load_we(1)
         load_burn(0)
         load_wc()
         load_burn(1)
         load_wl()
 
-        inc_banks, expo_banks = banks(psum_a), banks(psum_b)
-        gather(0, 0)
-        inc_pass(0, inc_banks, 0)
-        gather(0, 1)
+        inc_banks = [banks(psum_a), banks(psum_b)]
+        for a in range(PASSES):
+            for u in range(HALVES):
+                gather(a, u)
+                inc_pass(u, inc_banks[u], a)
+        expo_banks = [banks(psum_a), banks(psum_b)]
         for i in range(2):
             weave_we(0, i)
         for i in range(2):
             quant_we(0, i)
-        expo_pass(0, expo_banks, 0)
-        gather(1, 0)
-        inc_pass(0, inc_banks, 1)
-        gather(1, 1)
+        expo_pass(0, expo_banks[0], 0)
         for i in range(2):
             weave_we(1, i)
+        for i in range(2):
             quant_we(1, i)
-        expo_pass(0, expo_banks, 1)
-
-        inc_banks, expo_banks = banks(psum_a), banks(psum_b)
-        for t in range(PACK):
-            for a in range(PASSES):
-                inc_pass(1, inc_banks, a, [t])
+        expo_pass(0, expo_banks[0], 1)
+        expo_pass(1, expo_banks[1], 0)
         for t in range(GPSIMD_SLICES[0]):
             add_burn(nc.gpsimd, 0, t, t + 1)
-        for a in range(PASSES):
-            expo_pass(1, expo_banks, a, [0])
+        expo_pass(1, expo_banks[1], 1)
         add_burn(nc.vector, 0, GPSIMD_SLICES[0], PACK)
         store_h(0)
         weave_h(0)
-        add_burn(nc.gpsimd, 1, 0, GPSIMD_SLICES[1])
-        for t in range(1, PACK):
-            for a in range(PASSES):
-                expo_pass(1, expo_banks, a, [t])
-        add_burn(nc.vector, 1, GPSIMD_SLICES[1], PACK)
+        add_burn(nc.vector, 1, 0, PACK)
         store_h(1)
 
         weave_wl(0, nc.vector.tensor_copy)

@@ -30,9 +30,7 @@ BLOCKS = 16
 ROWS = PASSES * BLOCKS
 V_COL, WI_COL, WC_COL, PLANE = 0, S, S + H, S + H + N
 WL_PIECE = 2 * P
-GROUPS = (((0, 2), (2, 4), (4, 6)), ((0, 2), (2, 4), (4, 5), (5, 6)))
-GPSIMD_SLICES = (3, 0)
-CAPS_FIRST = 4
+GPSIMD_SLICES = 2
 
 
 def tile_list_prepayment_burnout_cap_kernel(
@@ -44,8 +42,11 @@ def tile_list_prepayment_burnout_cap_kernel(
         lists = ctx.enter_context(tc.tile_pool(name="lists", bufs=1))
         keep = ctx.enter_context(tc.tile_pool(name="keep", bufs=1))
         late = ctx.enter_context(tc.tile_pool(name="late", bufs=1))
-        psum_a = ctx.enter_context(tc.psum_pool(name="psum_a", bufs=4))
-        psum_b = ctx.enter_context(tc.psum_pool(name="psum_b", bufs=4))
+        reuse = ctx.enter_context(tc.tile_pool(name="reuse", bufs=1))
+        psum = ctx.enter_context(tc.psum_pool(name="psum", bufs=1))
+
+        def bank(b, name):
+            return psum.tile([P, HALF], F32, name=name, offset=b * HALF * 4)
 
         def tile(shape, dtype, name):
             return keep.tile(shape, dtype, name=name, align_bytes=ALIGN)
@@ -71,19 +72,31 @@ def tile_list_prepayment_burnout_cap_kernel(
         we_q = [tile([P, H], U32, f"we_q{a}") for a in range(PASSES)]
         we_s = [tile([P, H], U8, f"we_s{a}") for a in range(PASSES)]
         wl_raw = late_tile([P, PACK, N], F32, "wl_raw")
-        wl_bf = [tile([P, WL_PIECE * PACK], BF16, f"wl_bf{i}") for i in range(N // WL_PIECE)]
+        wl_bf = [tile([P, WL_PIECE * PACK], BF16, f"wl_bf{i}") for i in range(2)] + [None]
         wl_q = [tile([P, WL_PIECE], U32, f"wl_q{i}") for i in range(N // WL_PIECE)]
         wl_s = [tile([P, WL_PIECE], U8, f"wl_s{i}") for i in range(N // WL_PIECE)]
         wc_q = late_tile([P, PASSES * N], I32, "wc_q")
-        burn_in = [late_tile([P, PACK, HALF], F32, f"burn_in{u}") for u in range(HALVES)]
+        burn_in = [late_tile([P, 2, S], F32, f"burn_in{i}") for i in range(2)]
         inc = [tile([P, PACK, HALF], F32, f"inc{u}") for u in range(HALVES)]
-        prod = [tile([P, PACK, HALF], F32, f"prod{u}") for u in range(HALVES)]
-        h = [burn_in[0], tile([P, PACK, HALF], F32, "prod0")]
+        slab = PACK * HALF * 4
+        prod_area = [
+            reuse.tile([P, 2, PACK, HALF], F32, name=f"prod{u}", align_bytes=ALIGN, offset=2 * u * slab)
+            for u in range(HALVES)
+        ]
+        prod = [prod_area[u][:, 0, :, :] for u in range(HALVES)]
+        h = [
+            tile([P, PACK, HALF], F32, "h0"),
+            reuse.tile([P, PACK, HALF], F32, name="h1", align_bytes=ALIGN, offset=0),
+        ]
         h_bf = [tile([P, HALF * PACK], BF16, f"h_bf{u}") for u in range(HALVES)]
-        h_q = [tile([P, HALF], I32, f"h_q{u}") for u in range(HALVES)]
+        h_words = tile([P, S], I32, "h_words")
+        h_q = [h_words[:, u * HALF : (u + 1) * HALF] for u in range(HALVES)]
         h_s = tile([P, S], U8, "h_s")
-        y_group = {(u, n0): tile([P, n1 - n0, HALF], F32, f"y{u}{n0}") for u in range(HALVES) for n0, n1 in GROUPS[u]}
-        y = [[y_group[u, n0][:, n - n0, :] for n0, n1 in GROUPS[u] for n in range(n0, n1)] for u in range(HALVES)]
+        wl_bf[2] = reuse.tile([P, WL_PIECE * PACK], BF16, name="wl_bf_last", align_bytes=ALIGN, offset=slab)
+        y_rows = [tile([P, S], F32, f"y{n}") for n in range(2)] + [
+            reuse.tile([P, S], F32, name=f"y{n}", align_bytes=ALIGN, offset=slab + (n - 1) * S * 4) for n in range(2, N_TILES)
+        ]
+        y = [[y_rows[n][:, u * HALF : (u + 1) * HALF] for n in range(N_TILES)] for u in range(HALVES)]
         v_s_area = late.tile([P, late_bytes[-1]], U8, name="v_s_area", align_bytes=ALIGN, offset=0)
         v_s = v_s_area[:, 0:S]
         rows = tile([P, PLANE], U8, "rows")
@@ -99,10 +112,8 @@ def tile_list_prepayment_burnout_cap_kernel(
                 out=we_raw[a][:], in_=we[K_PASS * a : K_PASS * (a + 1), :].rearrange("(p j) c -> p j c", j=PACK)
             )
 
-        def load_burn(u):
-            nc.sync.dma_start(
-                out=burn_in[u][:], in_=burn.rearrange("(p t) j -> p t j", t=PACK)[:, :, u * HALF : (u + 1) * HALF]
-            )
+        def load_burn(i):
+            nc.sync.dma_start(out=burn_in[i][:], in_=burn.rearrange("(p t) j -> p t j", t=PACK)[:, 2 * i : 2 * i + 2, :])
 
         def load_wc():
             nc.sync.dma_start(
@@ -124,8 +135,8 @@ def tile_list_prepayment_burnout_cap_kernel(
             cols = HALF // 16
             nc.vector.tensor_copy(v[a][u][:], tab[a][:].bitcast(U32).indirect(offsets[:, u * cols : (u + 1) * cols]))
 
-        def weave_we(a, i):
-            nc.vector.tensor_copy(
+        def weave_we(a, i, copy):
+            copy(
                 out=we_bf[a][i][:].rearrange("p (t m j) -> p m j t", m=P, j=PACK),
                 in_=we_raw[a][:].rearrange("p j (m t) -> p m j t", t=PACK)[:, :, :, 2 * i : 2 * i + 2],
             )
@@ -137,9 +148,6 @@ def tile_list_prepayment_burnout_cap_kernel(
         def v_plane(a, u):
             return planes[a][:, V_COL + u * HALF : V_COL + (u + 1) * HALF]
 
-        def banks(pool):
-            return [pool.tile([P, HALF], F32, name="acc") for t in range(PACK)]
-
         def inc_pass(u, accs, a, slices=range(PACK)):
             for t in slices:
                 c0 = a * H + t * P
@@ -148,8 +156,10 @@ def tile_list_prepayment_burnout_cap_kernel(
                     lhsT_scale=planes[a][:, WI_COL + t * P : WI_COL + (t + 1) * P],
                     rhs=v[a][u][:].bitcast(FP8X4), rhs_scale=v_plane(a, u), start=(a == 0), stop=(a == PASSES - 1),
                 )
-                if a == PASSES - 1:
-                    nc.scalar.copy(out=inc[u][:, t, :], in_=accs[t][:])
+
+        def inc_out(u, accs):
+            for t in range(PACK):
+                nc.scalar.copy(out=inc[u][:, t, :], in_=accs[t][:])
 
         def expo_pass(u, accs, a, slices=range(PACK)):
             for t in slices:
@@ -169,7 +179,8 @@ def tile_list_prepayment_burnout_cap_kernel(
             )
 
         def add_burn(engine, u, t0, t1):
-            engine.tensor_tensor(h[u][:, t0:t1, :], burn_in[u][:, t0:t1, :], prod[u][:, t0:t1, :], ALU.add)
+            given = burn_in[t0 // 2][:, t0 % 2 : t0 % 2 + t1 - t0, u * HALF : (u + 1) * HALF]
+            engine.tensor_tensor(h[u][:, t0:t1, :], given, prod[u][:, t0:t1, :], ALU.add)
 
         def store_h(u):
             nc.sync.dma_start(
@@ -181,11 +192,11 @@ def tile_list_prepayment_burnout_cap_kernel(
 
         def quant_h(u):
             nc.vector.quantize_mx(
-                out=h_q[u][:].bitcast(FP8X4), scales=h_s[:, u * HALF : (u + 1) * HALF], in_=h_bf[u][:]
+                out=h_q[u].bitcast(FP8X4), scales=h_s[:, u * HALF : (u + 1) * HALF], in_=h_bf[u][:]
             )
-            nc.sync.dma_start(
-                out=out_2[0].rearrange("p m t -> p (m t)").bitcast(I32)[:, u * HALF : (u + 1) * HALF], in_=h_q[u][:]
-            )
+
+        def store_h_words():
+            nc.sync.dma_start(out=out_2[0].rearrange("p m t -> p (m t)").bitcast(I32), in_=h_words[:])
 
         def weave_wl(i, copy):
             weave(copy, wl_bf[i][:], wl_raw[:, :, WL_PIECE * i : WL_PIECE * (i + 1)])
@@ -193,8 +204,11 @@ def tile_list_prepayment_burnout_cap_kernel(
         def quant_wl(i):
             nc.vector.quantize_mx(out=wl_q[i][:].bitcast(FP8X4), scales=wl_s[i][:], in_=wl_bf[i][:])
 
+        def cap_bank(k):
+            return k if k < 2 * PACK else k - PACK
+
         def cap_tile(n, u):
-            acc = psum_a.tile([P, HALF], F32, name="acc")
+            acc = bank(cap_bank(HALVES * n + u), f"cap{u}{n}")
             for a in range(PASSES):
                 c0 = a * N + n * P
                 nc.tensor.matmul_mx(
@@ -206,20 +220,17 @@ def tile_list_prepayment_burnout_cap_kernel(
             nc.scalar.copy(out=y[u][n], in_=acc[:])
 
         def min_tile(n, u):
-            acc = psum_b.tile([P, HALF], F32, name="acc")
+            acc = bank((HALVES * n + u) % PACK, f"load{u}{n}")
             piece, c0 = divmod(n * P, WL_PIECE)
             nc.tensor.matmul_mx(
                 out=acc[:], lhsT=wl_q[piece][:, c0 : c0 + P].bitcast(FP8X4),
-                lhsT_scale=wl_s[piece][:, c0 : c0 + P], rhs=h_q[u][:].bitcast(FP8X4),
+                lhsT_scale=wl_s[piece][:, c0 : c0 + P], rhs=h_q[u].bitcast(FP8X4),
                 rhs_scale=h_s[:, u * HALF : (u + 1) * HALF], start=True, stop=True,
             )
             nc.vector.tensor_tensor(y[u][n], acc[:], y[u][n], ALU.min)
 
-        def store_y(u, n0, n1):
-            nc.sync.dma_start(
-                out=out_0.rearrange("(n p) j -> p n j", p=P)[:, n0:n1, u * HALF : (u + 1) * HALF],
-                in_=y_group[u, n0][:],
-            )
+        def store_y(n, c0, c1):
+            nc.sync.dma_start(out=out_0[n * P : (n + 1) * P, c0:c1], in_=y_rows[n][:, c0:c1])
 
         def store_h_scales():
             for r in range(LIVE):
@@ -259,58 +270,60 @@ def tile_list_prepayment_burnout_cap_kernel(
         load_tab(1)
         load_we(0)
         load_we(1)
-        load_burn(0)
         load_wc()
+        load_burn(0)
         load_burn(1)
         load_wl()
 
-        inc_banks = [banks(psum_a), banks(psum_b)]
+        inc_banks = [[bank(PACK * u + t, f"inc{u}{t}") for t in range(PACK)] for u in range(HALVES)]
         for a in range(PASSES):
             for u in range(HALVES):
                 gather(a, u)
                 inc_pass(u, inc_banks[u], a)
-        expo_banks = [banks(psum_a), banks(psum_b)]
+        inc_out(0, inc_banks[0])
+        weave_we(1, 1, nc.scalar.copy)
+        inc_out(1, inc_banks[1])
+        expo_banks = [[bank(PACK * u + t, f"expo{u}{t}") for t in range(PACK)] for u in range(HALVES)]
         for i in range(2):
-            weave_we(0, i)
+            weave_we(0, i, nc.vector.tensor_copy)
         for i in range(2):
             quant_we(0, i)
         expo_pass(0, expo_banks[0], 0)
-        for i in range(2):
-            weave_we(1, i)
+        weave_we(1, 0, nc.vector.tensor_copy)
         for i in range(2):
             quant_we(1, i)
         expo_pass(0, expo_banks[0], 1)
         expo_pass(1, expo_banks[1], 0)
-        for t in range(GPSIMD_SLICES[0]):
+        for t in range(GPSIMD_SLICES):
             add_burn(nc.gpsimd, 0, t, t + 1)
         expo_pass(1, expo_banks[1], 1)
-        add_burn(nc.vector, 0, GPSIMD_SLICES[0], PACK)
+        add_burn(nc.vector, 0, 2, PACK)
         store_h(0)
         weave_h(0)
-        add_burn(nc.vector, 1, 0, PACK)
+        for i in range(2):
+            add_burn(nc.vector, 1, 2 * i, 2 * i + 2)
         store_h(1)
+        weave_h(1)
 
         weave_wl(0, nc.vector.tensor_copy)
         weave_wl(1, nc.vector.tensor_copy)
+        weave_wl(2, nc.scalar.copy)
         quant_wl(0)
         quant_h(0)
         quant_wl(1)
-        for n in range(CAPS_FIRST):
-            cap_tile(n, 0)
-        weave_wl(2, nc.scalar.copy)
-        for n in range(CAPS_FIRST, N_TILES):
-            cap_tile(n, 0)
-        weave_h(1)
+        quant_h(1)
+        store_h_words()
+        store_h_scales()
         for n in range(N_TILES):
-            cap_tile(n, 1)
+            for u in range(HALVES):
+                cap_tile(n, u)
 
-        for u in range(HALVES):
-            for n0, n1 in GROUPS[u]:
-                for n in range(n0, n1):
-                    min_tile(n, u)
-                store_y(u, n0, n1)
-                if (u, n0) == (0, 0):
-                    quant_wl(2)
-            if u == 0:
-                quant_h(1)
-                store_h_scales()
+        for n in range(N_TILES):
+            for u in range(HALVES):
+                min_tile(n, u)
+                if n == N_TILES - 1:
+                    store_y(n, u * HALF, (u + 1) * HALF)
+            if n < N_TILES - 1:
+                store_y(n, 0, S)
+            if n == 1:
+                quant_wl(2)

@@ -67,8 +67,13 @@ def tile_list_prepayment_burnout_cap_kernel(
         wi_q = tile([P, PASSES * 2 * H], U8, "wi_q")
         tab = [tile([P, T], I32, "tab0"), late_tile([P, T], I32, "tab1")]
         v = [[tile([P, HALF], U32, f"v{a}{u}") for u in range(HALVES)] for a in range(PASSES)]
-        we_raw = [late_tile([P, PACK, H], F32, f"we_raw{a}") for a in range(PASSES)]
-        we_bf = [[tile([P, H * 2], BF16, f"we_bf{a}{i}") for i in range(2)] for a in range(PASSES)]
+        we_first = [tile([P, PACK, H // 2], F32, "we_first0"), late_tile([P, PACK, H // 2], F32, "we_first1")]
+        we_raw = [None, late_tile([P, PACK, H], F32, "we_raw1")]
+        we_first_bf = tile([P, H * PACK], BF16, "we_first_bf")
+        we_bf = [
+            [we_first_bf[:, H * 2 * i : H * 2 * (i + 1)] for i in range(2)],
+            [tile([P, H * 2], BF16, f"we_bf1{i}")[:] for i in range(2)],
+        ]
         we_q = [tile([P, H], U32, f"we_q{a}") for a in range(PASSES)]
         we_s = [tile([P, H], U8, f"we_s{a}") for a in range(PASSES)]
         wl_raw = late_tile([P, PACK, N], F32, "wl_raw")
@@ -92,7 +97,7 @@ def tile_list_prepayment_burnout_cap_kernel(
         h_words = tile([P, S], I32, "h_words")
         h_q = [h_words[:, u * HALF : (u + 1) * HALF] for u in range(HALVES)]
         h_s = tile([P, S], U8, "h_s")
-        wl_bf[2] = reuse.tile([P, WL_PIECE * PACK], BF16, name="wl_bf_last", align_bytes=ALIGN, offset=slab)
+        wl_bf[2] = reuse.tile([P, WL_PIECE * PACK], BF16, name="wl_bf_last", align_bytes=ALIGN, offset=2 * slab + 3 * S * 4)
         y_rows = [tile([P, S], F32, f"y{n}") for n in range(2)] + [
             reuse.tile([P, S], F32, name=f"y{n}", align_bytes=ALIGN, offset=slab + (n - 1) * S * 4) for n in range(2, N_TILES)
         ]
@@ -110,6 +115,17 @@ def tile_list_prepayment_burnout_cap_kernel(
         def load_we(a):
             nc.sync.dma_start(
                 out=we_raw[a][:], in_=we[K_PASS * a : K_PASS * (a + 1), :].rearrange("(p j) c -> p j c", j=PACK)
+            )
+
+        def load_we_first(i):
+            rows_in = we[0:K_PASS, :].rearrange("(p j) c -> p j c", j=PACK)
+            nc.sync.dma_start(out=we_first[i][:], in_=rows_in[:, :, i * H // 2 : (i + 1) * H // 2])
+
+        def weave_we_first(i):
+            dealt = we_first_bf[:].rearrange("p (t m j) -> p m j t", m=P, j=PACK)
+            nc.vector.tensor_copy(
+                out=dealt[:, i * P // 2 : (i + 1) * P // 2, :, :],
+                in_=we_first[i][:].rearrange("p j (m t) -> p m j t", t=PACK),
             )
 
         def load_burn(i):
@@ -137,13 +153,13 @@ def tile_list_prepayment_burnout_cap_kernel(
 
         def weave_we(a, i, copy):
             copy(
-                out=we_bf[a][i][:].rearrange("p (t m j) -> p m j t", m=P, j=PACK),
+                out=we_bf[a][i].rearrange("p (t m j) -> p m j t", m=P, j=PACK),
                 in_=we_raw[a][:].rearrange("p j (m t) -> p m j t", t=PACK)[:, :, :, 2 * i : 2 * i + 2],
             )
 
         def quant_we(a, i):
             cols = slice(2 * i * P, 2 * (i + 1) * P)
-            nc.vector.quantize_mx(out=we_q[a][:, cols].bitcast(FP8X4), scales=we_s[a][:, cols], in_=we_bf[a][i][:])
+            nc.vector.quantize_mx(out=we_q[a][:, cols].bitcast(FP8X4), scales=we_s[a][:, cols], in_=we_bf[a][i])
 
         def v_plane(a, u):
             return planes[a][:, V_COL + u * HALF : V_COL + (u + 1) * HALF]
@@ -195,8 +211,9 @@ def tile_list_prepayment_burnout_cap_kernel(
                 out=h_q[u].bitcast(FP8X4), scales=h_s[:, u * HALF : (u + 1) * HALF], in_=h_bf[u][:]
             )
 
-        def store_h_words():
-            nc.sync.dma_start(out=out_2[0].rearrange("p m t -> p (m t)").bitcast(I32), in_=h_words[:])
+        def store_h_words(u):
+            words = out_2[0].rearrange("p m t -> p (m t)").bitcast(I32)
+            nc.sync.dma_start(out=words[:, u * HALF : (u + 1) * HALF], in_=h_q[u])
 
         def weave_wl(i, copy):
             weave(copy, wl_bf[i][:], wl_raw[:, :, WL_PIECE * i : WL_PIECE * (i + 1)])
@@ -240,14 +257,16 @@ def tile_list_prepayment_burnout_cap_kernel(
                 )
 
         nc.sync.dma_start(offsets[:], offs)
-        load_scale_rows(wi_s_raw[0:ROWS, :], wi_scales)
         load_scale_rows(tab_s[0:ROWS, :], tab_scales)
+        load_scale_rows(wi_s_raw[0:ROWS, :], wi_scales)
         load_scale_rows(rows[0:ROWS, WC_COL:PLANE], wc_scales)
         load_tab(0)
         nc.sync.dma_start(
             out=wi_raw[:].rearrange("p (a c) -> p a c", a=PASSES).bitcast(I32),
             in_=wi_words.rearrange("a p c -> p a c").bitcast(I32),
         )
+
+        load_we_first(0)
 
         for part in (slice(32, 64), slice(64, P)):
             nc.vector.memset(wi_s_raw[part, :].bitcast(I32), 0)
@@ -268,7 +287,7 @@ def tile_list_prepayment_burnout_cap_kernel(
 
         move_planes()
         load_tab(1)
-        load_we(0)
+        load_we_first(1)
         load_we(1)
         load_wc()
         load_burn(0)
@@ -285,7 +304,7 @@ def tile_list_prepayment_burnout_cap_kernel(
         inc_out(1, inc_banks[1])
         expo_banks = [[bank(PACK * u + t, f"expo{u}{t}") for t in range(PACK)] for u in range(HALVES)]
         for i in range(2):
-            weave_we(0, i, nc.vector.tensor_copy)
+            weave_we_first(i)
         for i in range(2):
             quant_we(0, i)
         expo_pass(0, expo_banks[0], 0)
@@ -310,9 +329,10 @@ def tile_list_prepayment_burnout_cap_kernel(
         weave_wl(2, nc.scalar.copy)
         quant_wl(0)
         quant_h(0)
+        store_h_words(0)
         quant_wl(1)
         quant_h(1)
-        store_h_words()
+        store_h_words(1)
         store_h_scales()
         for n in range(N_TILES):
             for u in range(HALVES):

@@ -29,7 +29,7 @@ LIVE = 4
 BLOCKS = 16
 ROWS = PASSES * BLOCKS
 V_COL, WI_COL, WC_COL, PLANE = 0, S, S + H, S + H + N
-WL_PIECE = 2 * P
+WL_CUTS = (0, 4 * P, N)
 GPSIMD_SLICES = 2
 
 
@@ -67,8 +67,9 @@ def tile_list_prepayment_burnout_cap_kernel(
         wi_q = tile([P, PASSES * 2 * H], U8, "wi_q")
         tab = [tile([P, T], I32, "tab0"), late_tile([P, T], I32, "tab1")]
         v = [[tile([P, HALF], U32, f"v{a}{u}") for u in range(HALVES)] for a in range(PASSES)]
-        we_first = [tile([P, PACK, H // 2], F32, "we_first0"), late_tile([P, PACK, H // 2], F32, "we_first1")]
-        we_raw = [None, late_tile([P, PACK, H], F32, "we_raw1")]
+        we_last_at = late_bytes[-1]
+        we_raw = [None, late_tile([P, 6, H], F32, "we_raw1")[:, 0:PACK, :]]
+        we_raw[0] = late_tile([P, PACK, H], F32, "we_raw0")[:]
         we_first_bf = tile([P, H * PACK], BF16, "we_first_bf")
         we_bf = [
             [we_first_bf[:, H * 2 * i : H * 2 * (i + 1)] for i in range(2)],
@@ -76,13 +77,18 @@ def tile_list_prepayment_burnout_cap_kernel(
         ]
         we_q = [tile([P, H], U32, f"we_q{a}") for a in range(PASSES)]
         we_s = [tile([P, H], U8, f"we_s{a}") for a in range(PASSES)]
-        wl_raw = late_tile([P, PACK, N], F32, "wl_raw")
-        wl_bf = [tile([P, WL_PIECE * PACK], BF16, f"wl_bf{i}") for i in range(2)] + [None]
-        wl_q = [tile([P, WL_PIECE], U32, f"wl_q{i}") for i in range(N // WL_PIECE)]
-        wl_s = [tile([P, WL_PIECE], U8, f"wl_s{i}") for i in range(N // WL_PIECE)]
+        wl_raw = [late_tile([P, PACK, WL_CUTS[i + 1] - WL_CUTS[i]], F32, f"wl_raw{i}") for i in range(2)]
+        wl_bf = [tile([P, WL_CUTS[1] * PACK], BF16, "wl_bf0"), None]
+        wl_q = [tile([P, WL_CUTS[i + 1] - WL_CUTS[i]], U32, f"wl_q{i}") for i in range(2)]
+        wl_s = [tile([P, WL_CUTS[i + 1] - WL_CUTS[i]], U8, f"wl_s{i}") for i in range(2)]
         wc_q = late_tile([P, PASSES * N], I32, "wc_q")
         burn_in = [late_tile([P, 2, S], F32, f"burn_in{i}") for i in range(2)]
-        inc = [tile([P, PACK, HALF], F32, f"inc{u}") for u in range(HALVES)]
+        slice_bytes = HALF * 4
+        inc_tiles = [tile([P, HALF], F32, f"inc{i}") for i in range(4)] + [
+            late.tile([P, HALF], F32, name=f"inc{i}", align_bytes=ALIGN, offset=we_last_at + (i - 4) * slice_bytes)
+            for i in range(4, 8)
+        ]
+        inc = [inc_tiles[PACK * u : PACK * (u + 1)] for u in range(HALVES)]
         slab = PACK * HALF * 4
         prod_area = [
             reuse.tile([P, 2, PACK, HALF], F32, name=f"prod{u}", align_bytes=ALIGN, offset=2 * u * slab)
@@ -91,13 +97,13 @@ def tile_list_prepayment_burnout_cap_kernel(
         prod = [prod_area[u][:, 0, :, :] for u in range(HALVES)]
         h = [
             tile([P, PACK, HALF], F32, "h0"),
-            reuse.tile([P, PACK, HALF], F32, name="h1", align_bytes=ALIGN, offset=0),
+            tile([P, PACK, HALF], F32, "h1"),
         ]
         h_bf = [tile([P, HALF * PACK], BF16, f"h_bf{u}") for u in range(HALVES)]
         h_words = tile([P, S], I32, "h_words")
         h_q = [h_words[:, u * HALF : (u + 1) * HALF] for u in range(HALVES)]
         h_s = tile([P, S], U8, "h_s")
-        wl_bf[2] = reuse.tile([P, WL_PIECE * PACK], BF16, name="wl_bf_last", align_bytes=ALIGN, offset=2 * slab + 3 * S * 4)
+        wl_bf[1] = reuse.tile([P, (N - WL_CUTS[1]) * PACK], BF16, name="wl_bf_last", align_bytes=ALIGN, offset=2 * slab + 3 * S * 4)
         y_rows = [tile([P, S], F32, f"y{n}") for n in range(2)] + [
             reuse.tile([P, S], F32, name=f"y{n}", align_bytes=ALIGN, offset=slab + (n - 1) * S * 4) for n in range(2, N_TILES)
         ]
@@ -114,18 +120,7 @@ def tile_list_prepayment_burnout_cap_kernel(
 
         def load_we(a):
             nc.sync.dma_start(
-                out=we_raw[a][:], in_=we[K_PASS * a : K_PASS * (a + 1), :].rearrange("(p j) c -> p j c", j=PACK)
-            )
-
-        def load_we_first(i):
-            rows_in = we[0:K_PASS, :].rearrange("(p j) c -> p j c", j=PACK)
-            nc.sync.dma_start(out=we_first[i][:], in_=rows_in[:, :, i * H // 2 : (i + 1) * H // 2])
-
-        def weave_we_first(i):
-            dealt = we_first_bf[:].rearrange("p (t m j) -> p m j t", m=P, j=PACK)
-            nc.vector.tensor_copy(
-                out=dealt[:, i * P // 2 : (i + 1) * P // 2, :, :],
-                in_=we_first[i][:].rearrange("p j (m t) -> p m j t", t=PACK),
+                out=we_raw[a], in_=we[K_PASS * a : K_PASS * (a + 1), :].rearrange("(p j) c -> p j c", j=PACK)
             )
 
         def load_burn(i):
@@ -137,8 +132,9 @@ def tile_list_prepayment_burnout_cap_kernel(
                 in_=wc_words.rearrange("a p c i -> p a (c i)").bitcast(I32),
             )
 
-        def load_wl():
-            nc.sync.dma_start(out=wl_raw[:], in_=wl.rearrange("(p j) c -> p j c", j=PACK))
+        def load_wl(i):
+            rows_in = wl.rearrange("(p j) c -> p j c", j=PACK)
+            nc.sync.dma_start(out=wl_raw[i][:], in_=rows_in[:, :, WL_CUTS[i] : WL_CUTS[i + 1]])
 
         def move_planes():
             for quad in range(P // QUADRANT):
@@ -154,7 +150,7 @@ def tile_list_prepayment_burnout_cap_kernel(
         def weave_we(a, i, copy):
             copy(
                 out=we_bf[a][i].rearrange("p (t m j) -> p m j t", m=P, j=PACK),
-                in_=we_raw[a][:].rearrange("p j (m t) -> p m j t", t=PACK)[:, :, :, 2 * i : 2 * i + 2],
+                in_=we_raw[a].rearrange("p j (m t) -> p m j t", t=PACK)[:, :, :, 2 * i : 2 * i + 2],
             )
 
         def quant_we(a, i):
@@ -175,7 +171,7 @@ def tile_list_prepayment_burnout_cap_kernel(
 
         def inc_out(u, accs):
             for t in range(PACK):
-                nc.scalar.copy(out=inc[u][:, t, :], in_=accs[t][:])
+                nc.scalar.copy(out=inc[u][t][:], in_=accs[t][:])
 
         def expo_pass(u, accs, a, slices=range(PACK)):
             for t in slices:
@@ -186,7 +182,7 @@ def tile_list_prepayment_burnout_cap_kernel(
                     start=(a == 0), stop=(a == PASSES - 1),
                 )
                 if a == PASSES - 1:
-                    nc.vector.tensor_tensor(prod[u][:, t, :], accs[t][:], inc[u][:, t, :], ALU.mult)
+                    nc.vector.tensor_tensor(prod[u][:, t, :], inc[u][t][:], accs[t][:], ALU.mult)
 
         def weave(copy, dst, src):
             copy(
@@ -216,13 +212,13 @@ def tile_list_prepayment_burnout_cap_kernel(
             nc.sync.dma_start(out=words[:, u * HALF : (u + 1) * HALF], in_=h_q[u])
 
         def weave_wl(i, copy):
-            weave(copy, wl_bf[i][:], wl_raw[:, :, WL_PIECE * i : WL_PIECE * (i + 1)])
+            weave(copy, wl_bf[i][:], wl_raw[i][:])
 
         def quant_wl(i):
             nc.vector.quantize_mx(out=wl_q[i][:].bitcast(FP8X4), scales=wl_s[i][:], in_=wl_bf[i][:])
 
         def cap_bank(k):
-            return k if k < 2 * PACK else k - PACK
+            return k % (2 * PACK)
 
         def cap_tile(n, u):
             acc = bank(cap_bank(HALVES * n + u), f"cap{u}{n}")
@@ -237,14 +233,14 @@ def tile_list_prepayment_burnout_cap_kernel(
             nc.scalar.copy(out=y[u][n], in_=acc[:])
 
         def min_tile(n, u):
-            acc = bank((HALVES * n + u) % PACK, f"load{u}{n}")
-            piece, c0 = divmod(n * P, WL_PIECE)
+            acc = bank(PACK + (HALVES * n + u) % PACK, f"load{u}{n}")
+            piece, c0 = divmod(n * P, WL_CUTS[1])
             nc.tensor.matmul_mx(
                 out=acc[:], lhsT=wl_q[piece][:, c0 : c0 + P].bitcast(FP8X4),
                 lhsT_scale=wl_s[piece][:, c0 : c0 + P], rhs=h_q[u].bitcast(FP8X4),
                 rhs_scale=h_s[:, u * HALF : (u + 1) * HALF], start=True, stop=True,
             )
-            nc.vector.tensor_tensor(y[u][n], acc[:], y[u][n], ALU.min)
+            nc.vector.tensor_tensor(y[u][n], y[u][n], acc[:], ALU.min)
 
         def store_y(n, c0, c1):
             nc.sync.dma_start(out=out_0[n * P : (n + 1) * P, c0:c1], in_=y_rows[n][:, c0:c1])
@@ -266,7 +262,6 @@ def tile_list_prepayment_burnout_cap_kernel(
             in_=wi_words.rearrange("a p c -> p a c").bitcast(I32),
         )
 
-        load_we_first(0)
 
         for part in (slice(32, 64), slice(64, P)):
             nc.vector.memset(wi_s_raw[part, :].bitcast(I32), 0)
@@ -287,50 +282,53 @@ def tile_list_prepayment_burnout_cap_kernel(
 
         move_planes()
         load_tab(1)
-        load_we_first(1)
+        load_we(0)
         load_we(1)
-        load_wc()
         load_burn(0)
+        load_wc()
         load_burn(1)
-        load_wl()
+        load_wl(0)
+        load_wl(1)
 
         inc_banks = [[bank(PACK * u + t, f"inc{u}{t}") for t in range(PACK)] for u in range(HALVES)]
         for a in range(PASSES):
             for u in range(HALVES):
                 gather(a, u)
                 inc_pass(u, inc_banks[u], a)
-        inc_out(0, inc_banks[0])
+        weave_we(0, 0, nc.vector.tensor_copy)
+        weave_we(0, 1, nc.vector.tensor_copy)
         weave_we(1, 1, nc.scalar.copy)
+        inc_out(0, inc_banks[0])
         inc_out(1, inc_banks[1])
         expo_banks = [[bank(PACK * u + t, f"expo{u}{t}") for t in range(PACK)] for u in range(HALVES)]
-        for i in range(2):
-            weave_we_first(i)
-        for i in range(2):
-            quant_we(0, i)
-        expo_pass(0, expo_banks[0], 0)
+        nc.vector.quantize_mx(out=we_q[0][:].bitcast(FP8X4), scales=we_s[0][:], in_=we_first_bf[:])
         weave_we(1, 0, nc.vector.tensor_copy)
         for i in range(2):
             quant_we(1, i)
-        expo_pass(0, expo_banks[0], 1)
-        expo_pass(1, expo_banks[1], 0)
+        for t in range(PACK):
+            for a in range(PASSES):
+                expo_pass(0, expo_banks[0], a, [t])
         for t in range(GPSIMD_SLICES):
             add_burn(nc.gpsimd, 0, t, t + 1)
-        expo_pass(1, expo_banks[1], 1)
+        for t in range(PACK):
+            for a in range(PASSES):
+                expo_pass(1, expo_banks[1], a, [t])
+        for t in range(GPSIMD_SLICES):
+            add_burn(nc.gpsimd, 1, t, t + 1)
         add_burn(nc.vector, 0, 2, PACK)
         store_h(0)
         weave_h(0)
-        for i in range(2):
-            add_burn(nc.vector, 1, 2 * i, 2 * i + 2)
+        add_burn(nc.vector, 1, 2, PACK)
         store_h(1)
-        weave_h(1)
+        cut = HALF // 2
+        weave(nc.scalar.copy, h_bf[1][:, 0 : cut * PACK], h[1][:, :, 0:cut])
 
         weave_wl(0, nc.vector.tensor_copy)
-        weave_wl(1, nc.vector.tensor_copy)
-        weave_wl(2, nc.scalar.copy)
+        weave(nc.vector.tensor_copy, h_bf[1][:, cut * PACK :], h[1][:, :, cut:])
+        weave_wl(1, nc.scalar.copy)
         quant_wl(0)
         quant_h(0)
         store_h_words(0)
-        quant_wl(1)
         quant_h(1)
         store_h_words(1)
         store_h_scales()
@@ -346,4 +344,4 @@ def tile_list_prepayment_burnout_cap_kernel(
             if n < N_TILES - 1:
                 store_y(n, 0, S)
             if n == 1:
-                quant_wl(2)
+                quant_wl(1)

@@ -29,8 +29,9 @@ LIVE = 4
 BLOCKS = 16
 ROWS = PASSES * BLOCKS
 V_COL, WI_COL, WC_COL, PLANE = 0, S, S + H, S + H + N
-WL_CUTS = (0, 4 * P, N)
-GPSIMD_SLICES = 2
+WL_PIECE = 2 * P
+WL_CUTS = (0, 2 * P, N)
+GPSIMD_SLICES = 3
 
 
 def tile_list_prepayment_burnout_cap_kernel(
@@ -78,11 +79,11 @@ def tile_list_prepayment_burnout_cap_kernel(
         we_q = [tile([P, H], U32, f"we_q{a}") for a in range(PASSES)]
         we_s = [tile([P, H], U8, f"we_s{a}") for a in range(PASSES)]
         wl_raw = [late_tile([P, PACK, WL_CUTS[i + 1] - WL_CUTS[i]], F32, f"wl_raw{i}") for i in range(2)]
-        wl_bf = [tile([P, WL_CUTS[1] * PACK], BF16, "wl_bf0"), None]
-        wl_q = [tile([P, WL_CUTS[i + 1] - WL_CUTS[i]], U32, f"wl_q{i}") for i in range(2)]
-        wl_s = [tile([P, WL_CUTS[i + 1] - WL_CUTS[i]], U8, f"wl_s{i}") for i in range(2)]
+        wl_bf = [tile([P, WL_PIECE * PACK], BF16, "wl_bf0"), None, None]
+        wl_q = [tile([P, WL_PIECE], U32, f"wl_q{i}") for i in range(3)]
+        wl_s = [tile([P, WL_PIECE], U8, f"wl_s{i}") for i in range(3)]
         wc_q = late_tile([P, PASSES * N], I32, "wc_q")
-        burn_in = [late_tile([P, 2, S], F32, f"burn_in{i}") for i in range(2)]
+        burn_in = [late_tile([P, PACK, HALF], F32, f"burn_in{u}") for u in range(HALVES)]
         slice_bytes = HALF * 4
         inc_tiles = [tile([P, HALF], F32, f"inc{i}") for i in range(4)] + [
             late.tile([P, HALF], F32, name=f"inc{i}", align_bytes=ALIGN, offset=we_last_at + (i - 4) * slice_bytes)
@@ -97,13 +98,15 @@ def tile_list_prepayment_burnout_cap_kernel(
         prod = [prod_area[u][:, 0, :, :] for u in range(HALVES)]
         h = [
             tile([P, PACK, HALF], F32, "h0"),
-            tile([P, PACK, HALF], F32, "h1"),
+            reuse.tile([P, PACK, HALF], F32, name="h1", align_bytes=ALIGN, offset=0),
         ]
         h_bf = [tile([P, HALF * PACK], BF16, f"h_bf{u}") for u in range(HALVES)]
         h_words = tile([P, S], I32, "h_words")
         h_q = [h_words[:, u * HALF : (u + 1) * HALF] for u in range(HALVES)]
         h_s = tile([P, S], U8, "h_s")
-        wl_bf[1] = reuse.tile([P, (N - WL_CUTS[1]) * PACK], BF16, name="wl_bf_last", align_bytes=ALIGN, offset=2 * slab + 3 * S * 4)
+        for i in (1, 2):
+            at = 2 * slab + 3 * S * 4 + (i - 1) * WL_PIECE * PACK * 2
+            wl_bf[i] = reuse.tile([P, WL_PIECE * PACK], BF16, name=f"wl_bf{i}", align_bytes=ALIGN, offset=at)
         y_rows = [tile([P, S], F32, f"y{n}") for n in range(2)] + [
             reuse.tile([P, S], F32, name=f"y{n}", align_bytes=ALIGN, offset=slab + (n - 1) * S * 4) for n in range(2, N_TILES)
         ]
@@ -123,8 +126,10 @@ def tile_list_prepayment_burnout_cap_kernel(
                 out=we_raw[a], in_=we[K_PASS * a : K_PASS * (a + 1), :].rearrange("(p j) c -> p j c", j=PACK)
             )
 
-        def load_burn(i):
-            nc.sync.dma_start(out=burn_in[i][:], in_=burn.rearrange("(p t) j -> p t j", t=PACK)[:, 2 * i : 2 * i + 2, :])
+        def load_burn(u):
+            nc.sync.dma_start(
+                out=burn_in[u][:], in_=burn.rearrange("(p t) j -> p t j", t=PACK)[:, :, u * HALF : (u + 1) * HALF]
+            )
 
         def load_wc():
             nc.sync.dma_start(
@@ -191,8 +196,7 @@ def tile_list_prepayment_burnout_cap_kernel(
             )
 
         def add_burn(engine, u, t0, t1):
-            given = burn_in[t0 // 2][:, t0 % 2 : t0 % 2 + t1 - t0, u * HALF : (u + 1) * HALF]
-            engine.tensor_tensor(h[u][:, t0:t1, :], given, prod[u][:, t0:t1, :], ALU.add)
+            engine.tensor_tensor(h[u][:, t0:t1, :], burn_in[u][:, t0:t1, :], prod[u][:, t0:t1, :], ALU.add)
 
         def store_h(u):
             nc.sync.dma_start(
@@ -212,13 +216,13 @@ def tile_list_prepayment_burnout_cap_kernel(
             nc.sync.dma_start(out=words[:, u * HALF : (u + 1) * HALF], in_=h_q[u])
 
         def weave_wl(i, copy):
-            weave(copy, wl_bf[i][:], wl_raw[i][:])
+            weave(copy, wl_bf[i][:], wl_raw[0][:] if i == 0 else wl_raw[1][:, :, (i - 1) * WL_PIECE : i * WL_PIECE])
 
         def quant_wl(i):
             nc.vector.quantize_mx(out=wl_q[i][:].bitcast(FP8X4), scales=wl_s[i][:], in_=wl_bf[i][:])
 
         def cap_bank(k):
-            return k % (2 * PACK)
+            return (0, 1, 2, 3, 4, 5, 6, 7, 0, 1, 6, 7)[k]
 
         def cap_tile(n, u):
             acc = bank(cap_bank(HALVES * n + u), f"cap{u}{n}")
@@ -233,8 +237,8 @@ def tile_list_prepayment_burnout_cap_kernel(
             nc.scalar.copy(out=y[u][n], in_=acc[:])
 
         def min_tile(n, u):
-            acc = bank(PACK + (HALVES * n + u) % PACK, f"load{u}{n}")
-            piece, c0 = divmod(n * P, WL_CUTS[1])
+            acc = bank(2 + (HALVES * n + u) % PACK, f"load{u}{n}")
+            piece, c0 = divmod(n * P, WL_PIECE)
             nc.tensor.matmul_mx(
                 out=acc[:], lhsT=wl_q[piece][:, c0 : c0 + P].bitcast(FP8X4),
                 lhsT_scale=wl_s[piece][:, c0 : c0 + P], rhs=h_q[u].bitcast(FP8X4),
@@ -301,7 +305,8 @@ def tile_list_prepayment_burnout_cap_kernel(
         inc_out(0, inc_banks[0])
         inc_out(1, inc_banks[1])
         expo_banks = [[bank(PACK * u + t, f"expo{u}{t}") for t in range(PACK)] for u in range(HALVES)]
-        nc.vector.quantize_mx(out=we_q[0][:].bitcast(FP8X4), scales=we_s[0][:], in_=we_first_bf[:])
+        for i in range(2):
+            quant_we(0, i)
         weave_we(1, 0, nc.vector.tensor_copy)
         for i in range(2):
             quant_we(1, i)
@@ -313,19 +318,16 @@ def tile_list_prepayment_burnout_cap_kernel(
         for t in range(PACK):
             for a in range(PASSES):
                 expo_pass(1, expo_banks[1], a, [t])
-        for t in range(GPSIMD_SLICES):
-            add_burn(nc.gpsimd, 1, t, t + 1)
-        add_burn(nc.vector, 0, 2, PACK)
+        add_burn(nc.vector, 0, GPSIMD_SLICES, PACK)
         store_h(0)
         weave_h(0)
-        add_burn(nc.vector, 1, 2, PACK)
+        add_burn(nc.vector, 1, 0, PACK)
         store_h(1)
         cut = HALF // 2
         weave(nc.scalar.copy, h_bf[1][:, 0 : cut * PACK], h[1][:, :, 0:cut])
 
         weave_wl(0, nc.vector.tensor_copy)
         weave(nc.vector.tensor_copy, h_bf[1][:, cut * PACK :], h[1][:, :, cut:])
-        weave_wl(1, nc.scalar.copy)
         quant_wl(0)
         quant_h(0)
         store_h_words(0)
@@ -335,6 +337,8 @@ def tile_list_prepayment_burnout_cap_kernel(
         for n in range(N_TILES):
             for u in range(HALVES):
                 cap_tile(n, u)
+            if n in (2, 3):
+                weave_wl(n - 1, nc.scalar.copy)
 
         for n in range(N_TILES):
             for u in range(HALVES):
@@ -343,5 +347,5 @@ def tile_list_prepayment_burnout_cap_kernel(
                     store_y(n, u * HALF, (u + 1) * HALF)
             if n < N_TILES - 1:
                 store_y(n, 0, S)
-            if n == 1:
-                quant_wl(1)
+            if n in (0, 2):
+                quant_wl(n // 2 + 1)

@@ -104,9 +104,9 @@ def tile_list_prepayment_burnout_cap_kernel(
         h_words = tile([P, S], I32, "h_words")
         h_q = [h_words[:, u * HALF : (u + 1) * HALF] for u in range(HALVES)]
         h_s = tile([P, S], U8, "h_s")
-        for i in (1, 2):
-            at = 2 * slab + 3 * S * 4 + (i - 1) * WL_PIECE * PACK * 2
-            wl_bf[i] = reuse.tile([P, WL_PIECE * PACK], BF16, name=f"wl_bf{i}", align_bytes=ALIGN, offset=at)
+        at = 2 * slab + 3 * S * 4
+        wl_bf[1] = reuse.tile([P, WL_PIECE * PACK], BF16, name="wl_bf1", align_bytes=ALIGN, offset=at)
+        wl_bf[2] = tile([P, HALF * PACK], BF16, "h_bf1")[:, 0 : WL_PIECE * PACK]
         y_rows = [tile([P, S], F32, f"y{n}") for n in range(2)] + [
             reuse.tile([P, S], F32, name=f"y{n}", align_bytes=ALIGN, offset=slab + (n - 1) * S * 4) for n in range(2, N_TILES)
         ]
@@ -333,12 +333,17 @@ def tile_list_prepayment_burnout_cap_kernel(
         store_h_words(0)
         quant_h(1)
         store_h_words(1)
+        nc.gpsimd.tensor_scalar(
+            wl_bf[2].rearrange("p (c t) -> p c t", t=PACK),
+            wl_raw[1][:, :, WL_PIECE:].rearrange("p t c -> p c t"),
+            1.0, 0.0, ALU.mult, ALU.add,
+        )
         store_h_scales()
         for n in range(N_TILES):
             for u in range(HALVES):
                 cap_tile(n, u)
-            if n in (2, 3):
-                weave_wl(n - 1, nc.scalar.copy)
+            if n == 2:
+                weave_wl(1, nc.scalar.copy)
 
         for n in range(N_TILES):
             for u in range(HALVES):

@@ -31,6 +31,8 @@ ROWS = PASSES * BLOCKS
 V_COL, WI_COL, WC_COL, PLANE = 0, S, S + H, S + H + N
 WL_PIECE = 2 * P
 WL_CUTS = (0, 2 * P, N)
+WHOLE_ROWS = 1
+LAST_CUT = 3 * P
 GPSIMD_SLICES = 3
 
 
@@ -244,7 +246,11 @@ def tile_list_prepayment_burnout_cap_kernel(
                 lhsT_scale=wl_s[piece][:, c0 : c0 + P], rhs=h_q[u].bitcast(FP8X4),
                 rhs_scale=h_s[:, u * HALF : (u + 1) * HALF], start=True, stop=True,
             )
-            nc.vector.tensor_tensor(y[u][n], y[u][n], acc[:], ALU.min)
+            last = (n, u) == (N_TILES - 1, HALVES - 1)
+            for c0, c1 in ((0, LAST_CUT), (LAST_CUT, HALF)) if last else ((0, HALF),):
+                nc.vector.tensor_tensor(y[u][n][:, c0:c1], y[u][n][:, c0:c1], acc[:, c0:c1], ALU.min)
+                if n >= WHOLE_ROWS:
+                    store_y(n, u * HALF + c0, u * HALF + c1)
 
         def store_y(n, c0, c1):
             nc.sync.dma_start(out=out_0[n * P : (n + 1) * P, c0:c1], in_=y_rows[n][:, c0:c1])
@@ -348,9 +354,7 @@ def tile_list_prepayment_burnout_cap_kernel(
         for n in range(N_TILES):
             for u in range(HALVES):
                 min_tile(n, u)
-                if n == N_TILES - 1:
-                    store_y(n, u * HALF, (u + 1) * HALF)
-            if n < N_TILES - 1:
+            if n < WHOLE_ROWS:
                 store_y(n, 0, S)
             if n in (0, 2):
                 quant_wl(n // 2 + 1)

@@ -29,11 +29,13 @@ LIVE = 4
 BLOCKS = 16
 ROWS = PASSES * BLOCKS
 V_COL, WI_COL, WC_COL, PLANE = 0, S, S + H, S + H + N
+BANKS = 8
+SLICE_BYTES = HALF * 4
 WL_PIECE = 2 * P
-WL_CUTS = (0, 2 * P, N)
-WHOLE_ROWS = 1
-LAST_CUT = 3 * P
 GPSIMD_SLICES = 3
+H_CUT = HALF // 2
+LOAD_BANKS = (2, 3, 4)
+LAST_CUT = 3 * P
 
 
 def tile_list_prepayment_burnout_cap_kernel(
@@ -49,7 +51,7 @@ def tile_list_prepayment_burnout_cap_kernel(
         psum = ctx.enter_context(tc.psum_pool(name="psum", bufs=1))
 
         def bank(b, name):
-            return psum.tile([P, HALF], F32, name=name, offset=b * HALF * 4)
+            return psum.tile([P, HALF], F32, name=name, offset=b * SLICE_BYTES)
 
         def tile(shape, dtype, name):
             return keep.tile(shape, dtype, name=name, align_bytes=ALIGN)
@@ -61,6 +63,9 @@ def tile_list_prepayment_burnout_cap_kernel(
             late_bytes.append(start + 4 * math.prod(shape[1:]))
             return late.tile(shape, dtype, name=name, align_bytes=ALIGN, offset=start)
 
+        def reuse_tile(shape, dtype, name, slices):
+            return reuse.tile(shape, dtype, name=name, align_bytes=ALIGN, offset=slices * SLICE_BYTES)
+
         offsets = lists.tile([P, S // 16], U16, name="offsets")
         tab_s = tile([P, T], U8, "tab_s")
         plane_pair = tile([P, PASSES * PLANE], U8, "plane_pair")
@@ -70,48 +75,35 @@ def tile_list_prepayment_burnout_cap_kernel(
         wi_q = tile([P, PASSES * 2 * H], U8, "wi_q")
         tab = [tile([P, T], I32, "tab0"), late_tile([P, T], I32, "tab1")]
         v = [[tile([P, HALF], U32, f"v{a}{u}") for u in range(HALVES)] for a in range(PASSES)]
-        we_last_at = late_bytes[-1]
-        we_raw = [None, late_tile([P, 6, H], F32, "we_raw1")[:, 0:PACK, :]]
-        we_raw[0] = late_tile([P, PACK, H], F32, "we_raw0")[:]
-        we_first_bf = tile([P, H * PACK], BF16, "we_first_bf")
-        we_bf = [
-            [we_first_bf[:, H * 2 * i : H * 2 * (i + 1)] for i in range(2)],
-            [tile([P, H * 2], BF16, f"we_bf1{i}")[:] for i in range(2)],
-        ]
+        we_raw = [late_tile([P, PACK, H], F32, f"we_raw{a}") for a in range(PASSES)]
+        we_last_at = late_bytes[-2]
+        we_bf = [[tile([P, H * 2], BF16, f"we_bf{a}{i}") for i in range(2)] for a in range(PASSES)]
         we_q = [tile([P, H], U32, f"we_q{a}") for a in range(PASSES)]
         we_s = [tile([P, H], U8, f"we_s{a}") for a in range(PASSES)]
-        wl_raw = [late_tile([P, PACK, WL_CUTS[i + 1] - WL_CUTS[i]], F32, f"wl_raw{i}") for i in range(2)]
-        wl_bf = [tile([P, WL_PIECE * PACK], BF16, "wl_bf0"), None, None]
+        wl_first = late_tile([P, PACK, WL_PIECE], F32, "wl_first")
+        wl_rest = late_tile([P, PACK, N - WL_PIECE], F32, "wl_rest")
+        wl_raw = [wl_first[:], wl_rest[:, :, 0:WL_PIECE], wl_rest[:, :, WL_PIECE:]]
         wl_q = [tile([P, WL_PIECE], U32, f"wl_q{i}") for i in range(3)]
         wl_s = [tile([P, WL_PIECE], U8, f"wl_s{i}") for i in range(3)]
         wc_q = late_tile([P, PASSES * N], I32, "wc_q")
         burn_in = [late_tile([P, PACK, HALF], F32, f"burn_in{u}") for u in range(HALVES)]
-        slice_bytes = HALF * 4
-        inc_tiles = [tile([P, HALF], F32, f"inc{i}") for i in range(4)] + [
-            late.tile([P, HALF], F32, name=f"inc{i}", align_bytes=ALIGN, offset=we_last_at + (i - 4) * slice_bytes)
-            for i in range(4, 8)
+        inc = [
+            [tile([P, HALF], F32, f"inc0{t}") for t in range(PACK)],
+            [
+                late.tile([P, HALF], F32, name=f"inc1{t}", align_bytes=ALIGN, offset=we_last_at + t * SLICE_BYTES)
+                for t in range(PACK)
+            ],
         ]
-        inc = [inc_tiles[PACK * u : PACK * (u + 1)] for u in range(HALVES)]
-        slab = PACK * HALF * 4
-        prod_area = [
-            reuse.tile([P, 2, PACK, HALF], F32, name=f"prod{u}", align_bytes=ALIGN, offset=2 * u * slab)
-            for u in range(HALVES)
-        ]
-        prod = [prod_area[u][:, 0, :, :] for u in range(HALVES)]
-        h = [
-            tile([P, PACK, HALF], F32, "h0"),
-            reuse.tile([P, PACK, HALF], F32, name="h1", align_bytes=ALIGN, offset=0),
-        ]
+        prod = [reuse_tile([P, 2 * PACK, HALF], F32, f"prod{u}", 2 * PACK * u)[:, 0:PACK, :] for u in range(HALVES)]
+        h = [tile([P, PACK, HALF], F32, "h0"), reuse_tile([P, PACK, HALF], F32, "h1", 0)]
         h_bf = [tile([P, HALF * PACK], BF16, f"h_bf{u}") for u in range(HALVES)]
         h_words = tile([P, S], I32, "h_words")
         h_q = [h_words[:, u * HALF : (u + 1) * HALF] for u in range(HALVES)]
         h_s = tile([P, S], U8, "h_s")
-        at = 2 * slab + 3 * S * 4
-        wl_bf[1] = reuse.tile([P, WL_PIECE * PACK], BF16, name="wl_bf1", align_bytes=ALIGN, offset=at)
-        wl_bf[2] = tile([P, HALF * PACK], BF16, "h_bf1")[:, 0 : WL_PIECE * PACK]
-        y_rows = [tile([P, S], F32, f"y{n}") for n in range(2)] + [
-            reuse.tile([P, S], F32, name=f"y{n}", align_bytes=ALIGN, offset=slab + (n - 1) * S * 4) for n in range(2, N_TILES)
-        ]
+        wl_bf = [tile([P, WL_PIECE * PACK], BF16, "wl_bf0")]
+        wl_bf.extend(reuse_tile([P, WL_PIECE * PACK], BF16, f"wl_bf{i}", 14) for i in (1, 2))
+        y_rows = [tile([P, S], F32, f"y{n}") for n in range(2)]
+        y_rows.extend(reuse_tile([P, S], F32, f"y{n}", 2 * n + 2) for n in range(2, N_TILES))
         y = [[y_rows[n][:, u * HALF : (u + 1) * HALF] for n in range(N_TILES)] for u in range(HALVES)]
         v_s_area = late.tile([P, late_bytes[-1]], U8, name="v_s_area", align_bytes=ALIGN, offset=0)
         v_s = v_s_area[:, 0:S]
@@ -125,7 +117,7 @@ def tile_list_prepayment_burnout_cap_kernel(
 
         def load_we(a):
             nc.sync.dma_start(
-                out=we_raw[a], in_=we[K_PASS * a : K_PASS * (a + 1), :].rearrange("(p j) c -> p j c", j=PACK)
+                out=we_raw[a][:], in_=we[K_PASS * a : K_PASS * (a + 1), :].rearrange("(p j) c -> p j c", j=PACK)
             )
 
         def load_burn(u):
@@ -139,15 +131,18 @@ def tile_list_prepayment_burnout_cap_kernel(
                 in_=wc_words.rearrange("a p c i -> p a (c i)").bitcast(I32),
             )
 
-        def load_wl(i):
+        def load_wl():
             rows_in = wl.rearrange("(p j) c -> p j c", j=PACK)
-            nc.sync.dma_start(out=wl_raw[i][:], in_=rows_in[:, :, WL_CUTS[i] : WL_CUTS[i + 1]])
+            nc.sync.dma_start(out=wl_first[:], in_=rows_in[:, :, 0:WL_PIECE])
+            nc.sync.dma_start(out=wl_rest[:], in_=rows_in[:, :, WL_PIECE:N])
 
         def move_planes():
+            staged = PASSES * LIVE
             for quad in range(P // QUADRANT):
+                live = plane_pair[QUADRANT * quad : QUADRANT * quad + LIVE, :]
                 nc.sync.dma_start(
-                    out=plane_pair[QUADRANT * quad : QUADRANT * quad + LIVE, :].rearrange("p (a c) -> p a c", a=PASSES).bitcast(I32),
-                    in_=rows[PASSES * LIVE * quad : PASSES * LIVE * (quad + 1), :].bitcast(I32),
+                    out=live.rearrange("p (a c) -> p a c", a=PASSES).bitcast(I32),
+                    in_=rows[staged * quad : staged * (quad + 1), :].bitcast(I32),
                 )
 
         def gather(a, u):
@@ -156,40 +151,41 @@ def tile_list_prepayment_burnout_cap_kernel(
 
         def weave_we(a, i, copy):
             copy(
-                out=we_bf[a][i].rearrange("p (t m j) -> p m j t", m=P, j=PACK),
-                in_=we_raw[a].rearrange("p j (m t) -> p m j t", t=PACK)[:, :, :, 2 * i : 2 * i + 2],
+                out=we_bf[a][i][:].rearrange("p (t m j) -> p m j t", m=P, j=PACK),
+                in_=we_raw[a][:].rearrange("p j (m t) -> p m j t", t=PACK)[:, :, :, 2 * i : 2 * i + 2],
             )
 
         def quant_we(a, i):
             cols = slice(2 * i * P, 2 * (i + 1) * P)
-            nc.vector.quantize_mx(out=we_q[a][:, cols].bitcast(FP8X4), scales=we_s[a][:, cols], in_=we_bf[a][i])
+            nc.vector.quantize_mx(out=we_q[a][:, cols].bitcast(FP8X4), scales=we_s[a][:, cols], in_=we_bf[a][i][:])
 
         def v_plane(a, u):
             return planes[a][:, V_COL + u * HALF : V_COL + (u + 1) * HALF]
 
-        def inc_pass(u, accs, a, slices=range(PACK)):
-            for t in slices:
+        def inc_pass(u, a):
+            for t in range(PACK):
                 c0 = a * H + t * P
                 nc.tensor.matmul_mx(
-                    out=accs[t][:], lhsT=wi_q[:, 2 * c0 : 2 * (c0 + P)].bitcast(FP4X4),
+                    out=inc_banks[u][t][:], lhsT=wi_q[:, 2 * c0 : 2 * (c0 + P)].bitcast(FP4X4),
                     lhsT_scale=planes[a][:, WI_COL + t * P : WI_COL + (t + 1) * P],
                     rhs=v[a][u][:].bitcast(FP8X4), rhs_scale=v_plane(a, u), start=(a == 0), stop=(a == PASSES - 1),
                 )
 
-        def inc_out(u, accs):
+        def inc_out(u):
             for t in range(PACK):
-                nc.scalar.copy(out=inc[u][t][:], in_=accs[t][:])
+                nc.scalar.copy(out=inc[u][t][:], in_=inc_banks[u][t][:])
 
-        def expo_pass(u, accs, a, slices=range(PACK)):
-            for t in slices:
-                nc.tensor.matmul_mx(
-                    out=accs[t][:], lhsT=we_q[a][:, t * P : (t + 1) * P].bitcast(FP8X4),
-                    lhsT_scale=we_s[a][:, t * P : (t + 1) * P],
-                    rhs=v[a][u][:].bitcast(FP8X4), rhs_scale=v_plane(a, u),
-                    start=(a == 0), stop=(a == PASSES - 1),
-                )
-                if a == PASSES - 1:
-                    nc.vector.tensor_tensor(prod[u][:, t, :], inc[u][t][:], accs[t][:], ALU.mult)
+        def products(u):
+            for t in range(PACK):
+                acc = bank(PACK * u + t, f"expo{u}{t}")
+                for a in range(PASSES):
+                    nc.tensor.matmul_mx(
+                        out=acc[:], lhsT=we_q[a][:, t * P : (t + 1) * P].bitcast(FP8X4),
+                        lhsT_scale=we_s[a][:, t * P : (t + 1) * P],
+                        rhs=v[a][u][:].bitcast(FP8X4), rhs_scale=v_plane(a, u),
+                        start=(a == 0), stop=(a == PASSES - 1),
+                    )
+                nc.vector.tensor_tensor(prod[u][:, t, :], inc[u][t][:], acc[:], ALU.mult)
 
         def weave(copy, dst, src):
             copy(
@@ -205,29 +201,22 @@ def tile_list_prepayment_burnout_cap_kernel(
                 out=out_1.rearrange("(p t) j -> p t j", t=PACK)[:, :, u * HALF : (u + 1) * HALF], in_=h[u][:]
             )
 
-        def weave_h(u):
-            weave(nc.scalar.copy, h_bf[u][:], h[u][:])
+        def weave_h(copy, u, c0, c1):
+            weave(copy, h_bf[u][:, c0 * PACK : c1 * PACK], h[u][:, :, c0:c1])
 
         def quant_h(u):
             nc.vector.quantize_mx(
                 out=h_q[u].bitcast(FP8X4), scales=h_s[:, u * HALF : (u + 1) * HALF], in_=h_bf[u][:]
             )
-
-        def store_h_words(u):
             words = out_2[0].rearrange("p m t -> p (m t)").bitcast(I32)
             nc.sync.dma_start(out=words[:, u * HALF : (u + 1) * HALF], in_=h_q[u])
-
-        def weave_wl(i, copy):
-            weave(copy, wl_bf[i][:], wl_raw[0][:] if i == 0 else wl_raw[1][:, :, (i - 1) * WL_PIECE : i * WL_PIECE])
 
         def quant_wl(i):
             nc.vector.quantize_mx(out=wl_q[i][:].bitcast(FP8X4), scales=wl_s[i][:], in_=wl_bf[i][:])
 
-        def cap_bank(k):
-            return (0, 1, 2, 3, 4, 5, 6, 7, 0, 1, 6, 7)[k]
-
         def cap_tile(n, u):
-            acc = bank(cap_bank(HALVES * n + u), f"cap{u}{n}")
+            k = HALVES * n + u
+            acc = bank(k if k < BANKS else (0, 1, BANKS - 2, BANKS - 1)[k - BANKS], f"cap{u}{n}")
             for a in range(PASSES):
                 c0 = a * N + n * P
                 nc.tensor.matmul_mx(
@@ -239,7 +228,7 @@ def tile_list_prepayment_burnout_cap_kernel(
             nc.scalar.copy(out=y[u][n], in_=acc[:])
 
         def min_tile(n, u):
-            acc = bank(2 + (HALVES * n + u) % PACK, f"load{u}{n}")
+            acc = bank(LOAD_BANKS[(HALVES * n + u) % len(LOAD_BANKS)], f"load{u}{n}")
             piece, c0 = divmod(n * P, WL_PIECE)
             nc.tensor.matmul_mx(
                 out=acc[:], lhsT=wl_q[piece][:, c0 : c0 + P].bitcast(FP8X4),
@@ -247,13 +236,13 @@ def tile_list_prepayment_burnout_cap_kernel(
                 rhs_scale=h_s[:, u * HALF : (u + 1) * HALF], start=True, stop=True,
             )
             last = (n, u) == (N_TILES - 1, HALVES - 1)
-            for c0, c1 in ((0, LAST_CUT), (LAST_CUT, HALF)) if last else ((0, HALF),):
-                nc.vector.tensor_tensor(y[u][n][:, c0:c1], y[u][n][:, c0:c1], acc[:, c0:c1], ALU.min)
-                if n >= WHOLE_ROWS:
-                    store_y(n, u * HALF + c0, u * HALF + c1)
+            for j0, j1 in ((0, LAST_CUT), (LAST_CUT, HALF)) if last else ((0, HALF),):
+                nc.vector.tensor_tensor(y[u][n][:, j0:j1], y[u][n][:, j0:j1], acc[:, j0:j1], ALU.min)
+                if n > 0:
+                    store_y(n, u * HALF + j0, u * HALF + j1)
 
-        def store_y(n, c0, c1):
-            nc.sync.dma_start(out=out_0[n * P : (n + 1) * P, c0:c1], in_=y_rows[n][:, c0:c1])
+        def store_y(n, j0, j1):
+            nc.sync.dma_start(out=out_0[n * P : (n + 1) * P, j0:j1], in_=y_rows[n][:, j0:j1])
 
         def store_h_scales():
             for r in range(LIVE):
@@ -271,7 +260,6 @@ def tile_list_prepayment_burnout_cap_kernel(
             out=wi_raw[:].rearrange("p (a c) -> p a c", a=PASSES).bitcast(I32),
             in_=wi_words.rearrange("a p c -> p a c").bitcast(I32),
         )
-
 
         for part in (slice(32, 64), slice(64, P)):
             nc.vector.memset(wi_s_raw[part, :].bitcast(I32), 0)
@@ -297,64 +285,57 @@ def tile_list_prepayment_burnout_cap_kernel(
         load_burn(0)
         load_wc()
         load_burn(1)
-        load_wl(0)
-        load_wl(1)
+        load_wl()
 
         inc_banks = [[bank(PACK * u + t, f"inc{u}{t}") for t in range(PACK)] for u in range(HALVES)]
         for a in range(PASSES):
             for u in range(HALVES):
                 gather(a, u)
-                inc_pass(u, inc_banks[u], a)
+                inc_pass(u, a)
         weave_we(0, 0, nc.vector.tensor_copy)
         weave_we(0, 1, nc.vector.tensor_copy)
         weave_we(1, 1, nc.scalar.copy)
-        inc_out(0, inc_banks[0])
-        inc_out(1, inc_banks[1])
-        expo_banks = [[bank(PACK * u + t, f"expo{u}{t}") for t in range(PACK)] for u in range(HALVES)]
-        for i in range(2):
-            quant_we(0, i)
+        for u in range(HALVES):
+            inc_out(u)
+        quant_we(0, 0)
+        quant_we(0, 1)
         weave_we(1, 0, nc.vector.tensor_copy)
-        for i in range(2):
-            quant_we(1, i)
-        for t in range(PACK):
-            for a in range(PASSES):
-                expo_pass(0, expo_banks[0], a, [t])
+        quant_we(1, 0)
+        quant_we(1, 1)
+
+        products(0)
         for t in range(GPSIMD_SLICES):
             add_burn(nc.gpsimd, 0, t, t + 1)
-        for t in range(PACK):
-            for a in range(PASSES):
-                expo_pass(1, expo_banks[1], a, [t])
+        products(1)
         add_burn(nc.vector, 0, GPSIMD_SLICES, PACK)
         store_h(0)
-        weave_h(0)
+        weave_h(nc.scalar.copy, 0, 0, HALF)
         add_burn(nc.vector, 1, 0, PACK)
         store_h(1)
-        cut = HALF // 2
-        weave(nc.scalar.copy, h_bf[1][:, 0 : cut * PACK], h[1][:, :, 0:cut])
+        weave_h(nc.scalar.copy, 1, 0, H_CUT)
 
-        weave_wl(0, nc.vector.tensor_copy)
-        weave(nc.vector.tensor_copy, h_bf[1][:, cut * PACK :], h[1][:, :, cut:])
+        weave(nc.vector.tensor_copy, wl_bf[0][:], wl_raw[0])
+        weave_h(nc.vector.tensor_copy, 1, H_CUT, HALF)
         quant_wl(0)
-        quant_h(0)
-        store_h_words(0)
-        quant_h(1)
-        store_h_words(1)
-        nc.gpsimd.tensor_scalar(
-            wl_bf[2].rearrange("p (c t) -> p c t", t=PACK),
-            wl_raw[1][:, :, WL_PIECE:].rearrange("p t c -> p c t"),
-            1.0, 0.0, ALU.mult, ALU.add,
-        )
+        for u in range(HALVES):
+            quant_h(u)
         store_h_scales()
+
         for n in range(N_TILES):
             for u in range(HALVES):
                 cap_tile(n, u)
-            if n == 2:
-                weave_wl(1, nc.scalar.copy)
+            if n == 1:
+                weave(nc.scalar.copy, wl_bf[1][:], wl_raw[1])
 
         for n in range(N_TILES):
             for u in range(HALVES):
                 min_tile(n, u)
-            if n < WHOLE_ROWS:
-                store_y(n, 0, S)
-            if n in (0, 2):
-                quant_wl(n // 2 + 1)
+            if n == 0:
+                store_y(0, 0, S)
+                quant_wl(1)
+                nc.gpsimd.tensor_scalar(
+                    wl_bf[2][:].rearrange("p (c t) -> p c t", t=PACK), wl_raw[2].rearrange("p t c -> p c t"),
+                    1.0, 0.0, ALU.mult, ALU.add,
+                )
+            if n == 2:
+                quant_wl(2)

@@ -189,8 +189,8 @@ def tile_list_prepayment_burnout_cap_kernel(
 
         def weave(copy, dst, src):
             copy(
-                out=dst.rearrange("p (c i t) -> p c t i", i=4, t=PACK),
-                in_=src.rearrange("p t (c i) -> p c t i", i=4),
+                out=dst.rearrange("p (c i t) -> p c t i", i=2, t=PACK),
+                in_=src.rearrange("p t (c i) -> p c t i", i=2),
             )
 
         def add_burn(engine, u, t0, t1):

@@ -28,7 +28,7 @@ QUADRANT = 32
 LIVE = 4
 BLOCKS = 16
 ROWS = PASSES * BLOCKS
-V_COL, WI_COL, WC_COL, PLANE = 0, S, S + H, S + H + N
+V_COL, WI_COL, PLANE = 0, S, S + H
 BANKS = 8
 SLICE_BYTES = HALF * 4
 WL_PIECE = 2 * P
@@ -86,6 +86,8 @@ def tile_list_prepayment_burnout_cap_kernel(
         wl_q = [tile([P, WL_PIECE], U32, f"wl_q{i}") for i in range(3)]
         wl_s = [tile([P, WL_PIECE], U8, f"wl_s{i}") for i in range(3)]
         wc_q = late_tile([P, PASSES * N], I32, "wc_q")
+        wc_s = tile([P, N // 4], I32, "wc_s")
+        wc_planes = [wc_s[:].bitcast(U8)[LIVE * (a + 1) : P, :] for a in range(PASSES)]
         burn_in = [late_tile([P, PACK, HALF], F32, f"burn_in{u}") for u in range(HALVES)]
         inc = [
             [tile([P, HALF], F32, f"inc0{t}") for t in range(PACK)],
@@ -125,6 +127,14 @@ def tile_list_prepayment_burnout_cap_kernel(
                 out=burn_in[u][:], in_=burn.rearrange("(p t) j -> p t j", t=PACK)[:, :, u * HALF : (u + 1) * HALF]
             )
 
+        def load_wc_scales():
+            for quad in range(P // QUADRANT):
+                first = QUADRANT * quad + LIVE
+                nc.gpsimd.dma_start(
+                    out=wc_s[first : first + PASSES * LIVE, :],
+                    in_=wc_scales[:, LIVE * quad : LIVE * (quad + 1), :].bitcast(I32),
+                )
+
         def load_wc():
             nc.sync.dma_start(
                 out=wc_q[:].rearrange("p (a c) -> p a c", a=PASSES),
@@ -138,7 +148,7 @@ def tile_list_prepayment_burnout_cap_kernel(
 
         def move_planes():
             staged = PASSES * LIVE
-            for quad in range(P // QUADRANT):
+            for quad in (0, 2, 1, 3):
                 live = plane_pair[QUADRANT * quad : QUADRANT * quad + LIVE, :]
                 nc.sync.dma_start(
                     out=live.rearrange("p (a c) -> p a c", a=PASSES).bitcast(I32),
@@ -221,7 +231,7 @@ def tile_list_prepayment_burnout_cap_kernel(
                 c0 = a * N + n * P
                 nc.tensor.matmul_mx(
                     out=acc[:], lhsT=wc_q[:, c0 : c0 + P].bitcast(FP8X4),
-                    lhsT_scale=planes[a][:, WC_COL + n * P : WC_COL + (n + 1) * P],
+                    lhsT_scale=wc_planes[a][:, n * P : (n + 1) * P],
                     rhs=v[a][u][:].bitcast(FP8X4), rhs_scale=v_plane(a, u),
                     start=(a == 0), stop=(a == PASSES - 1),
                 )
@@ -254,7 +264,6 @@ def tile_list_prepayment_burnout_cap_kernel(
         nc.sync.dma_start(offsets[:], offs)
         load_scale_rows(tab_s[0:ROWS, :], tab_scales)
         load_scale_rows(wi_s_raw[0:ROWS, :], wi_scales)
-        load_scale_rows(rows[0:ROWS, WC_COL:PLANE], wc_scales)
         load_tab(0)
         nc.sync.dma_start(
             out=wi_raw[:].rearrange("p (a c) -> p a c", a=PASSES).bitcast(I32),
@@ -265,10 +274,10 @@ def tile_list_prepayment_burnout_cap_kernel(
             nc.vector.memset(wi_s_raw[part, :].bitcast(I32), 0)
         nc.vector.memset(tab_s[64:P, :].bitcast(I32), 0)
         nc.gpsimd.memset(tab_s[32:64, :].bitcast(I32), 0)
-        nc.gpsimd.memset(plane_pair[:].bitcast(I32), 0)
+        load_wc_scales()
 
         nc.vector.tensor_copy(
-            out=rows[:, WI_COL:WC_COL].rearrange("p (t m) -> p m t", t=PACK),
+            out=rows[:, WI_COL:PLANE].rearrange("p (t m) -> p m t", t=PACK),
             in_=wi_s_raw[:].rearrange("p (m t) -> p m t", t=PACK),
         )
         nc.vector.tensor_copy(v_s, tab_s[:].indirect(offsets[:]))

@@ -46,6 +46,7 @@ def tile_list_prepayment_burnout_cap_kernel(
     with ExitStack() as ctx:
         lists = ctx.enter_context(tc.tile_pool(name="lists", bufs=1))
         keep = ctx.enter_context(tc.tile_pool(name="keep", bufs=1))
+        first = ctx.enter_context(tc.tile_pool(name="first", bufs=1))
         late = ctx.enter_context(tc.tile_pool(name="late", bufs=1))
         reuse = ctx.enter_context(tc.tile_pool(name="reuse", bufs=1))
         psum = ctx.enter_context(tc.psum_pool(name="psum", bufs=1))
@@ -73,22 +74,31 @@ def tile_list_prepayment_burnout_cap_kernel(
         wi_raw = tile([P, PASSES * 2 * H], U8, "wi_raw")
         wi_s_raw = tile([P, H], U8, "wi_s_raw")
         wi_q = tile([P, PASSES * 2 * H], U8, "wi_q")
-        tab = [tile([P, T], I32, "tab0"), late_tile([P, T], I32, "tab1")]
+        tab = [first.tile([P, T], I32, name="tab0", align_bytes=ALIGN, offset=0), late_tile([P, T], I32, "tab1")]
         v = [[tile([P, HALF], U32, f"v{a}{u}") for u in range(HALVES)] for a in range(PASSES)]
-        we_raw = [late_tile([P, PACK, H], F32, f"we_raw{a}") for a in range(PASSES)]
+        last_at = late_bytes[-1]
+        we_area = late_tile([P, PASSES * N + PACK * (HALF + N)], F32, "we_area")
+        we_raw = [we_area[:, 0 : PACK * H].rearrange("p (j c) -> p j c", j=PACK), late_tile([P, PACK, H], F32, "we1")[:]]
         we_last_at = late_bytes[-2]
+        last_bytes = [last_at]
+
+        def last_tile(shape, dtype, name):
+            start = last_bytes[-1]
+            last_bytes.append(start + 4 * math.prod(shape[1:]))
+            return late.tile(shape, dtype, name=name, align_bytes=ALIGN, offset=start)
+
         we_bf = [[tile([P, H * 2], BF16, f"we_bf{a}{i}") for i in range(2)] for a in range(PASSES)]
         we_q = [tile([P, H], U32, f"we_q{a}") for a in range(PASSES)]
         we_s = [tile([P, H], U8, f"we_s{a}") for a in range(PASSES)]
-        wl_first = late_tile([P, PACK, WL_PIECE], F32, "wl_first")
-        wl_rest = late_tile([P, PACK, N - WL_PIECE], F32, "wl_rest")
+        wl_first = last_tile([P, PACK, WL_PIECE], F32, "wl_first")
+        wl_rest = last_tile([P, PACK, N - WL_PIECE], F32, "wl_rest")
         wl_raw = [wl_first[:], wl_rest[:, :, 0:WL_PIECE], wl_rest[:, :, WL_PIECE:]]
         wl_q = [tile([P, WL_PIECE], U32, f"wl_q{i}") for i in range(3)]
         wl_s = [tile([P, WL_PIECE], U8, f"wl_s{i}") for i in range(3)]
-        wc_q = late_tile([P, PASSES * N], I32, "wc_q")
-        wc_s = tile([P, N // 4], I32, "wc_s")
+        wc_q = last_tile([P, PASSES * N], I32, "wc_q")
+        wc_s = first.tile([P, N // 4], I32, name="wc_s", align_bytes=ALIGN, offset=0)
         wc_planes = [wc_s[:].bitcast(U8)[LIVE * (a + 1) : P, :] for a in range(PASSES)]
-        burn_in = [late_tile([P, PACK, HALF], F32, f"burn_in{u}") for u in range(HALVES)]
+        burn_in = [late_tile([P, PACK, HALF], F32, "burn_in0"), last_tile([P, PACK, HALF], F32, "burn_in1")]
         inc = [
             [tile([P, HALF], F32, f"inc0{t}") for t in range(PACK)],
             [
@@ -119,7 +129,7 @@ def tile_list_prepayment_burnout_cap_kernel(
 
         def load_we(a):
             nc.sync.dma_start(
-                out=we_raw[a][:], in_=we[K_PASS * a : K_PASS * (a + 1), :].rearrange("(p j) c -> p j c", j=PACK)
+                out=we_raw[a], in_=we[K_PASS * a : K_PASS * (a + 1), :].rearrange("(p j) c -> p j c", j=PACK)
             )
 
         def load_burn(u):
@@ -159,15 +169,17 @@ def tile_list_prepayment_burnout_cap_kernel(
             cols = HALF // 16
             nc.vector.tensor_copy(v[a][u][:], tab[a][:].bitcast(U32).indirect(offsets[:, u * cols : (u + 1) * cols]))
 
-        def weave_we(a, i, copy):
+        def weave_we(a, i, copy, m0=0, m1=P):
             copy(
-                out=we_bf[a][i][:].rearrange("p (t m j) -> p m j t", m=P, j=PACK),
-                in_=we_raw[a][:].rearrange("p j (m t) -> p m j t", t=PACK)[:, :, :, 2 * i : 2 * i + 2],
+                out=we_bf[a][i][:].rearrange("p (t m j) -> p m j t", m=P, j=PACK)[:, m0:m1],
+                in_=we_raw[a].rearrange("p j (m t) -> p m j t", t=PACK)[:, m0:m1, :, 2 * i : 2 * i + 2],
             )
 
-        def quant_we(a, i):
-            cols = slice(2 * i * P, 2 * (i + 1) * P)
-            nc.vector.quantize_mx(out=we_q[a][:, cols].bitcast(FP8X4), scales=we_s[a][:, cols], in_=we_bf[a][i][:])
+        def quant_we(a, i, t0=0, t1=2):
+            cols = slice((2 * i + t0) * P, (2 * i + t1) * P)
+            nc.vector.quantize_mx(
+                out=we_q[a][:, cols].bitcast(FP8X4), scales=we_s[a][:, cols], in_=we_bf[a][i][:, t0 * H : t1 * H]
+            )
 
         def v_plane(a, u):
             return planes[a][:, V_COL + u * HALF : V_COL + (u + 1) * HALF]
@@ -261,8 +273,8 @@ def tile_list_prepayment_burnout_cap_kernel(
                     in_=h_s[r:P:QUADRANT, :].bitcast(I32),
                 )
 
-        nc.sync.dma_start(offsets[:], offs)
         load_scale_rows(tab_s[0:ROWS, :], tab_scales)
+        nc.sync.dma_start(offsets[:], offs)
         load_scale_rows(wi_s_raw[0:ROWS, :], wi_scales)
         load_tab(0)
         nc.sync.dma_start(
@@ -274,7 +286,6 @@ def tile_list_prepayment_burnout_cap_kernel(
             nc.vector.memset(wi_s_raw[part, :].bitcast(I32), 0)
         nc.vector.memset(tab_s[64:P, :].bitcast(I32), 0)
         nc.gpsimd.memset(tab_s[32:64, :].bitcast(I32), 0)
-        load_wc_scales()
 
         nc.vector.tensor_copy(
             out=rows[:, WI_COL:PLANE].rearrange("p (t m) -> p m t", t=PACK),
@@ -292,24 +303,27 @@ def tile_list_prepayment_burnout_cap_kernel(
         load_we(0)
         load_we(1)
         load_burn(0)
-        load_wc()
-        load_burn(1)
-        load_wl()
 
         inc_banks = [[bank(PACK * u + t, f"inc{u}{t}") for t in range(PACK)] for u in range(HALVES)]
         for a in range(PASSES):
             for u in range(HALVES):
                 gather(a, u)
                 inc_pass(u, a)
+            if a == 0:
+                load_wc_scales()
         weave_we(0, 0, nc.vector.tensor_copy)
         weave_we(0, 1, nc.vector.tensor_copy)
+        load_wc()
+        load_burn(1)
+        load_wl()
         weave_we(1, 1, nc.scalar.copy)
         for u in range(HALVES):
             inc_out(u)
         quant_we(0, 0)
         quant_we(0, 1)
         weave_we(1, 0, nc.vector.tensor_copy)
-        quant_we(1, 0)
+        quant_we(1, 0, 0, 1)
+        quant_we(1, 0, 1, 2)
         quant_we(1, 1)
 
         products(0)

@@ -28,13 +28,15 @@ QUADRANT = 32
 LIVE = 4
 BLOCKS = 16
 ROWS = PASSES * BLOCKS
+STAGED = P - ROWS
 V_COL, WI_COL, PLANE = 0, S, S + H
+WC_CUT = 2 * P
 BANKS = 8
 SLICE_BYTES = HALF * 4
 WL_PIECE = 2 * P
 GPSIMD_SLICES = 3
 H_CUT = HALF // 2
-LOAD_BANKS = (2, 3, 4)
+LOAD_BANKS = (0, 1, 2)
 LAST_CUT = 3 * P
 
 
@@ -95,7 +97,8 @@ def tile_list_prepayment_burnout_cap_kernel(
         wl_raw = [wl_first[:], wl_rest[:, :, 0:WL_PIECE], wl_rest[:, :, WL_PIECE:]]
         wl_q = [tile([P, WL_PIECE], U32, f"wl_q{i}") for i in range(3)]
         wl_s = [tile([P, WL_PIECE], U8, f"wl_s{i}") for i in range(3)]
-        wc_q = last_tile([P, PASSES * N], I32, "wc_q")
+        wc_first = last_tile([P, PASSES, WC_CUT], I32, "wc_first")
+        wc_rest = last_tile([P, PASSES, N - WC_CUT], I32, "wc_rest")
         wc_s = first.tile([P, N // 4], I32, name="wc_s", align_bytes=ALIGN, offset=0)
         wc_planes = [wc_s[:].bitcast(U8)[LIVE * (a + 1) : P, :] for a in range(PASSES)]
         burn_in = [late_tile([P, PACK, HALF], F32, "burn_in0"), last_tile([P, PACK, HALF], F32, "burn_in1")]
@@ -106,17 +109,20 @@ def tile_list_prepayment_burnout_cap_kernel(
                 for t in range(PACK)
             ],
         ]
-        prod = [reuse_tile([P, 2 * PACK, HALF], F32, f"prod{u}", 2 * PACK * u)[:, 0:PACK, :] for u in range(HALVES)]
+        prod = [reuse_tile([P, 5, HALF], F32, "prod0", 0)[:, 0:PACK, :], reuse_tile([P, 9, HALF], F32, "prod1", 5)[:, 0:PACK, :]]
         h = [tile([P, PACK, HALF], F32, "h0"), reuse_tile([P, PACK, HALF], F32, "h1", 0)]
-        h_bf = [tile([P, HALF * PACK], BF16, f"h_bf{u}") for u in range(HALVES)]
+        h_bf = [reuse_tile([P, HALF * PACK], BF16, "h_bf0", 14), tile([P, H_CUT * PACK], BF16, "h_bf1")]
+        h_bf.append(tile([P, P * PACK], BF16, "h_bf2"))
+        h_bf.append(reuse_tile([P, P * PACK], BF16, "h_bf3", 14))
+        h_parts = ((0, 0, HALF), (1, 0, H_CUT), (1, H_CUT, H_CUT + P), (1, H_CUT + P, HALF))
         h_words = tile([P, S], I32, "h_words")
         h_q = [h_words[:, u * HALF : (u + 1) * HALF] for u in range(HALVES)]
         h_s = tile([P, S], U8, "h_s")
         wl_bf = [tile([P, WL_PIECE * PACK], BF16, "wl_bf0")]
-        wl_bf.extend(reuse_tile([P, WL_PIECE * PACK], BF16, f"wl_bf{i}", 14) for i in (1, 2))
-        y_rows = [tile([P, S], F32, f"y{n}") for n in range(2)]
-        y_rows.extend(reuse_tile([P, S], F32, f"y{n}", 2 * n + 2) for n in range(2, N_TILES))
-        y = [[y_rows[n][:, u * HALF : (u + 1) * HALF] for n in range(N_TILES)] for u in range(HALVES)]
+        wl_bf.extend(reuse_tile([P, WL_PIECE * PACK], BF16, f"wl_bf{i}", 13) for i in (1, 2))
+        y_all = [tile([P, HALF], F32, f"y{k}")[:] for k in range(3)]
+        y_all.extend(reuse_tile([P, HALF], F32, f"y{k}", k + 1)[:] for k in range(3, HALVES * N_TILES))
+        y = [y_all[u::HALVES] for u in range(HALVES)]
         v_s_area = late.tile([P, late_bytes[-1]], U8, name="v_s_area", align_bytes=ALIGN, offset=0)
         v_s = v_s_area[:, 0:S]
         rows = tile([P, PLANE], U8, "rows")
@@ -145,16 +151,11 @@ def tile_list_prepayment_burnout_cap_kernel(
                     in_=wc_scales[:, LIVE * quad : LIVE * (quad + 1), :].bitcast(I32),
                 )
 
-        def load_wc():
-            nc.sync.dma_start(
-                out=wc_q[:].rearrange("p (a c) -> p a c", a=PASSES),
-                in_=wc_words.rearrange("a p c i -> p a (c i)").bitcast(I32),
-            )
+        def load_wc(dst, c0, c1):
+            nc.sync.dma_start(out=dst[:], in_=wc_words.rearrange("a p c i -> p a (c i)").bitcast(I32)[:, :, c0:c1])
 
-        def load_wl():
-            rows_in = wl.rearrange("(p j) c -> p j c", j=PACK)
-            nc.sync.dma_start(out=wl_first[:], in_=rows_in[:, :, 0:WL_PIECE])
-            nc.sync.dma_start(out=wl_rest[:], in_=rows_in[:, :, WL_PIECE:N])
+        def load_wl(dst, c0, c1):
+            nc.sync.dma_start(out=dst[:], in_=wl.rearrange("(p j) c -> p j c", j=PACK)[:, :, c0:c1])
 
         def move_planes():
             staged = PASSES * LIVE
@@ -162,7 +163,7 @@ def tile_list_prepayment_burnout_cap_kernel(
                 live = plane_pair[QUADRANT * quad : QUADRANT * quad + LIVE, :]
                 nc.sync.dma_start(
                     out=live.rearrange("p (a c) -> p a c", a=PASSES).bitcast(I32),
-                    in_=rows[staged * quad : staged * (quad + 1), :].bitcast(I32),
+                    in_=rows[STAGED + staged * quad : STAGED + staged * (quad + 1), :].bitcast(I32),
                 )
 
         def gather(a, u):
@@ -223,13 +224,17 @@ def tile_list_prepayment_burnout_cap_kernel(
                 out=out_1.rearrange("(p t) j -> p t j", t=PACK)[:, :, u * HALF : (u + 1) * HALF], in_=h[u][:]
             )
 
-        def weave_h(copy, u, c0, c1):
-            weave(copy, h_bf[u][:, c0 * PACK : c1 * PACK], h[u][:, :, c0:c1])
+        def weave_h(copy, i):
+            u, c0, c1 = h_parts[i]
+            weave(copy, h_bf[i][:], h[u][:, :, c0:c1])
 
-        def quant_h(u):
+        def quant_h(i):
+            u, c0, c1 = h_parts[i]
             nc.vector.quantize_mx(
-                out=h_q[u].bitcast(FP8X4), scales=h_s[:, u * HALF : (u + 1) * HALF], in_=h_bf[u][:]
+                out=h_q[u][:, c0:c1].bitcast(FP8X4), scales=h_s[:, u * HALF + c0 : u * HALF + c1], in_=h_bf[i][:]
             )
+
+        def store_words(u):
             words = out_2[0].rearrange("p m t -> p (m t)").bitcast(I32)
             nc.sync.dma_start(out=words[:, u * HALF : (u + 1) * HALF], in_=h_q[u])
 
@@ -238,19 +243,19 @@ def tile_list_prepayment_burnout_cap_kernel(
 
         def cap_tile(n, u):
             k = HALVES * n + u
-            acc = bank(k if k < BANKS else (0, 1, BANKS - 2, BANKS - 1)[k - BANKS], f"cap{u}{n}")
+            acc = bank(k if k < BANKS else k - BANKS + len(LOAD_BANKS), f"cap{u}{n}")
             for a in range(PASSES):
-                c0 = a * N + n * P
+                words, c0 = (wc_first, n * P) if n * P < WC_CUT else (wc_rest, n * P - WC_CUT)
                 nc.tensor.matmul_mx(
-                    out=acc[:], lhsT=wc_q[:, c0 : c0 + P].bitcast(FP8X4),
+                    out=acc[:], lhsT=words[:, a, c0 : c0 + P].bitcast(FP8X4),
                     lhsT_scale=wc_planes[a][:, n * P : (n + 1) * P],
                     rhs=v[a][u][:].bitcast(FP8X4), rhs_scale=v_plane(a, u),
                     start=(a == 0), stop=(a == PASSES - 1),
                 )
             nc.scalar.copy(out=y[u][n], in_=acc[:])
 
-        def min_tile(n, u):
-            acc = bank(LOAD_BANKS[(HALVES * n + u) % len(LOAD_BANKS)], f"load{u}{n}")
+        def min_tile(k, n, u):
+            acc = bank(LOAD_BANKS[k % len(LOAD_BANKS)], f"load{u}{n}")
             piece, c0 = divmod(n * P, WL_PIECE)
             nc.tensor.matmul_mx(
                 out=acc[:], lhsT=wl_q[piece][:, c0 : c0 + P].bitcast(FP8X4),
@@ -260,11 +265,9 @@ def tile_list_prepayment_burnout_cap_kernel(
             last = (n, u) == (N_TILES - 1, HALVES - 1)
             for j0, j1 in ((0, LAST_CUT), (LAST_CUT, HALF)) if last else ((0, HALF),):
                 nc.vector.tensor_tensor(y[u][n][:, j0:j1], y[u][n][:, j0:j1], acc[:, j0:j1], ALU.min)
-                if n > 0:
-                    store_y(n, u * HALF + j0, u * HALF + j1)
-
-        def store_y(n, j0, j1):
-            nc.sync.dma_start(out=out_0[n * P : (n + 1) * P, j0:j1], in_=y_rows[n][:, j0:j1])
+                nc.sync.dma_start(
+                    out=out_0[n * P : (n + 1) * P, u * HALF + j0 : u * HALF + j1], in_=y[u][n][:, j0:j1]
+                )
 
         def store_h_scales():
             for r in range(LIVE):
@@ -273,19 +276,17 @@ def tile_list_prepayment_burnout_cap_kernel(
                     in_=h_s[r:P:QUADRANT, :].bitcast(I32),
                 )
 
-        load_scale_rows(tab_s[0:ROWS, :], tab_scales)
+        load_scale_rows(tab_s[STAGED:P, :], tab_scales)
         nc.sync.dma_start(offsets[:], offs)
-        load_scale_rows(wi_s_raw[0:ROWS, :], wi_scales)
+        load_scale_rows(wi_s_raw[STAGED:P, :], wi_scales)
         load_tab(0)
         nc.sync.dma_start(
             out=wi_raw[:].rearrange("p (a c) -> p a c", a=PASSES).bitcast(I32),
             in_=wi_words.rearrange("a p c -> p a c").bitcast(I32),
         )
 
-        for part in (slice(32, 64), slice(64, P)):
-            nc.vector.memset(wi_s_raw[part, :].bitcast(I32), 0)
-        nc.vector.memset(tab_s[64:P, :].bitcast(I32), 0)
-        nc.gpsimd.memset(tab_s[32:64, :].bitcast(I32), 0)
+        nc.vector.memset(tab_s[0:STAGED, :].bitcast(I32), 0)
+        nc.vector.memset(wi_s_raw[0:STAGED, :].bitcast(I32), 0)
 
         nc.vector.tensor_copy(
             out=rows[:, WI_COL:PLANE].rearrange("p (t m) -> p m t", t=PACK),
@@ -313,12 +314,15 @@ def tile_list_prepayment_burnout_cap_kernel(
                 load_wc_scales()
         weave_we(0, 0, nc.vector.tensor_copy)
         weave_we(0, 1, nc.vector.tensor_copy)
-        load_wc()
+        load_wc(wc_first, 0, WC_CUT)
+        load_wl(wl_first, 0, WL_PIECE)
+        load_wc(wc_rest, WC_CUT, N)
         load_burn(1)
-        load_wl()
+        load_wl(wl_rest, WL_PIECE, N)
         weave_we(1, 1, nc.scalar.copy)
         for u in range(HALVES):
             inc_out(u)
+        weave(nc.scalar.copy, wl_bf[0][:], wl_raw[0])
         quant_we(0, 0)
         quant_we(0, 1)
         weave_we(1, 0, nc.vector.tensor_copy)
@@ -332,33 +336,38 @@ def tile_list_prepayment_burnout_cap_kernel(
         products(1)
         add_burn(nc.vector, 0, GPSIMD_SLICES, PACK)
         store_h(0)
-        weave_h(nc.scalar.copy, 0, 0, HALF)
+        weave_h(nc.scalar.copy, 0)
         add_burn(nc.vector, 1, 0, PACK)
         store_h(1)
-        weave_h(nc.scalar.copy, 1, 0, H_CUT)
+        weave_h(nc.scalar.copy, 1)
 
-        weave(nc.vector.tensor_copy, wl_bf[0][:], wl_raw[0])
-        weave_h(nc.vector.tensor_copy, 1, H_CUT, HALF)
         quant_wl(0)
-        for u in range(HALVES):
-            quant_h(u)
+        weave_h(nc.vector.tensor_copy, 2)
+        quant_h(0)
+        store_words(0)
+        weave_h(nc.vector.tensor_copy, 3)
+        quant_h(2)
+        quant_h(3)
+        quant_h(1)
+        store_words(1)
         store_h_scales()
 
-        for n in range(N_TILES):
+        for n in range(BANKS // HALVES):
             for u in range(HALVES):
                 cap_tile(n, u)
             if n == 1:
                 weave(nc.scalar.copy, wl_bf[1][:], wl_raw[1])
 
-        for n in range(N_TILES):
-            for u in range(HALVES):
-                min_tile(n, u)
-            if n == 0:
-                store_y(0, 0, S)
+        order = [(2 * piece + i, u) for piece in range(3) for u in range(HALVES) for i in range(2)]
+        for k, (n, u) in enumerate(order):
+            min_tile(k, n, u)
+            if 2 <= k < 6:
+                cap_tile(*divmod(BANKS + k - 2, HALVES))
+            if k == 1:
                 quant_wl(1)
                 nc.gpsimd.tensor_scalar(
                     wl_bf[2][:].rearrange("p (c t) -> p c t", t=PACK), wl_raw[2].rearrange("p t c -> p c t"),
                     1.0, 0.0, ALU.mult, ALU.add,
                 )
-            if n == 2:
+            if k == 5:
                 quant_wl(2)

@@ -1,4 +1,3 @@
-import math
 from contextlib import ExitStack
 
 import concourse.mybir as mybir
@@ -27,17 +26,16 @@ N_TILES = N // P
 QUADRANT = 32
 LIVE = 4
 BLOCKS = 16
-ROWS = PASSES * BLOCKS
-STAGED = P - ROWS
+STAGED = P - PASSES * BLOCKS
 V_COL, WI_COL, PLANE = 0, S, S + H
-WC_CUT = 2 * P
 BANKS = 8
-SLICE_BYTES = HALF * 4
+KIB = 1024
 WL_PIECE = 2 * P
-GPSIMD_SLICES = 3
-H_CUT = HALF // 2
-LOAD_BANKS = (0, 1, 2)
-LAST_CUT = 3 * P
+PIECES = N // WL_PIECE
+GPSIMD_COLS = 3 * HALF
+H_CUTS = (224, 128)
+LATE_BANKS = (0, 1, 5, 6)
+LOAD_BANKS = (2, 3, 2, 3, 4, 2, 3, 4, 2, 3, 4, 2)
 
 
 def tile_list_prepayment_burnout_cap_kernel(
@@ -48,26 +46,19 @@ def tile_list_prepayment_burnout_cap_kernel(
     with ExitStack() as ctx:
         lists = ctx.enter_context(tc.tile_pool(name="lists", bufs=1))
         keep = ctx.enter_context(tc.tile_pool(name="keep", bufs=1))
-        first = ctx.enter_context(tc.tile_pool(name="first", bufs=1))
-        late = ctx.enter_context(tc.tile_pool(name="late", bufs=1))
-        reuse = ctx.enter_context(tc.tile_pool(name="reuse", bufs=1))
+        shared = ctx.enter_context(tc.tile_pool(name="shared", bufs=1))
         psum = ctx.enter_context(tc.psum_pool(name="psum", bufs=1))
 
         def bank(b, name):
-            return psum.tile([P, HALF], F32, name=name, offset=b * SLICE_BYTES)
+            return psum.tile([P, HALF], F32, name=name, offset=b * HALF * 4)
 
         def tile(shape, dtype, name):
             return keep.tile(shape, dtype, name=name, align_bytes=ALIGN)
 
-        late_bytes = [0]
+        def placed(shape, dtype, name, kib):
+            return shared.tile(shape, dtype, name=name, align_bytes=ALIGN, offset=kib * KIB)
 
-        def late_tile(shape, dtype, name):
-            start = late_bytes[-1]
-            late_bytes.append(start + 4 * math.prod(shape[1:]))
-            return late.tile(shape, dtype, name=name, align_bytes=ALIGN, offset=start)
-
-        def reuse_tile(shape, dtype, name, slices):
-            return reuse.tile(shape, dtype, name=name, align_bytes=ALIGN, offset=slices * SLICE_BYTES)
+        TAB0, TAB1, WE1, BURN0, WE0, PROD, WL_BF = 0, 16, 32, 40, 48, 74, 90
 
         offsets = lists.tile([P, S // 16], U16, name="offsets")
         tab_s = tile([P, T], U8, "tab_s")
@@ -76,56 +67,45 @@ def tile_list_prepayment_burnout_cap_kernel(
         wi_raw = tile([P, PASSES * 2 * H], U8, "wi_raw")
         wi_s_raw = tile([P, H], U8, "wi_s_raw")
         wi_q = tile([P, PASSES * 2 * H], U8, "wi_q")
-        tab = [first.tile([P, T], I32, name="tab0", align_bytes=ALIGN, offset=0), late_tile([P, T], I32, "tab1")]
+        rows = tile([P, PLANE], U8, "rows")
+        v_s_area = placed([P, (PROD - TAB1) * KIB], U8, "v_s_area", TAB1)
+        v_s = v_s_area[:, 0:S]
+        tab = [placed([P, T], I32, "tab0", TAB0), placed([P, T], I32, "tab1", TAB1)]
         v = [[tile([P, HALF], U32, f"v{a}{u}") for u in range(HALVES)] for a in range(PASSES)]
-        last_at = late_bytes[-1]
-        we_area = late_tile([P, PASSES * N + PACK * (HALF + N)], F32, "we_area")
-        we_raw = [we_area[:, 0 : PACK * H].rearrange("p (j c) -> p j c", j=PACK), late_tile([P, PACK, H], F32, "we1")[:]]
-        we_last_at = late_bytes[-2]
-        last_bytes = [last_at]
-
-        def last_tile(shape, dtype, name):
-            start = last_bytes[-1]
-            last_bytes.append(start + 4 * math.prod(shape[1:]))
-            return late.tile(shape, dtype, name=name, align_bytes=ALIGN, offset=start)
-
+        we_area = placed([P, (PROD - WE0) * KIB // 4], F32, "we_area", WE0)
+        we_raw = [we_area[:, 0 : PACK * H].rearrange("p (j c) -> p j c", j=PACK), placed([P, PACK, H], F32, "we1", WE1)[:]]
         we_bf = [[tile([P, H * 2], BF16, f"we_bf{a}{i}") for i in range(2)] for a in range(PASSES)]
         we_q = [tile([P, H], U32, f"we_q{a}") for a in range(PASSES)]
         we_s = [tile([P, H], U8, f"we_s{a}") for a in range(PASSES)]
-        wl_first = last_tile([P, PACK, WL_PIECE], F32, "wl_first")
-        wl_rest = last_tile([P, PACK, N - WL_PIECE], F32, "wl_rest")
+        wc_q = placed([P, PASSES, N], I32, "wc_q", WE0)
+        burn_in = [placed([P, 2, S], F32, "burn0", BURN0), placed([P, 2, S], F32, "burn1", WE0 + 6)]
+        wl_first = placed([P, PACK, WL_PIECE], F32, "wl_first", WE0 + 14)
+        wl_rest = placed([P, PACK, N - WL_PIECE], F32, "wl_rest", WE0 + 18)
         wl_raw = [wl_first[:], wl_rest[:, :, 0:WL_PIECE], wl_rest[:, :, WL_PIECE:]]
-        wl_q = [tile([P, WL_PIECE], U32, f"wl_q{i}") for i in range(3)]
-        wl_s = [tile([P, WL_PIECE], U8, f"wl_s{i}") for i in range(3)]
-        wc_first = last_tile([P, PASSES, WC_CUT], I32, "wc_first")
-        wc_rest = last_tile([P, PASSES, N - WC_CUT], I32, "wc_rest")
-        wc_s = first.tile([P, N // 4], I32, name="wc_s", align_bytes=ALIGN, offset=0)
-        wc_planes = [wc_s[:].bitcast(U8)[LIVE * (a + 1) : P, :] for a in range(PASSES)]
-        burn_in = [late_tile([P, PACK, HALF], F32, "burn_in0"), last_tile([P, PACK, HALF], F32, "burn_in1")]
-        inc = [
-            [tile([P, HALF], F32, f"inc0{t}") for t in range(PACK)],
-            [
-                late.tile([P, HALF], F32, name=f"inc1{t}", align_bytes=ALIGN, offset=we_last_at + t * SLICE_BYTES)
-                for t in range(PACK)
-            ],
-        ]
-        prod = [reuse_tile([P, 5, HALF], F32, "prod0", 0)[:, 0:PACK, :], reuse_tile([P, 9, HALF], F32, "prod1", 5)[:, 0:PACK, :]]
-        h = [tile([P, PACK, HALF], F32, "h0"), reuse_tile([P, PACK, HALF], F32, "h1", 0)]
-        h_bf = [reuse_tile([P, HALF * PACK], BF16, "h_bf0", 14), tile([P, H_CUT * PACK], BF16, "h_bf1")]
-        h_bf.append(tile([P, P * PACK], BF16, "h_bf2"))
-        h_bf.append(reuse_tile([P, P * PACK], BF16, "h_bf3", 14))
-        h_parts = ((0, 0, HALF), (1, 0, H_CUT), (1, H_CUT, H_CUT + P), (1, H_CUT + P, HALF))
-        h_words = tile([P, S], I32, "h_words")
-        h_q = [h_words[:, u * HALF : (u + 1) * HALF] for u in range(HALVES)]
-        h_s = tile([P, S], U8, "h_s")
+        wl_q = [tile([P, WL_PIECE], U32, f"wl_q{i}") for i in range(PIECES)]
+        wl_s = [tile([P, WL_PIECE], U8, f"wl_s{i}") for i in range(PIECES)]
         wl_bf = [tile([P, WL_PIECE * PACK], BF16, "wl_bf0")]
-        wl_bf.extend(reuse_tile([P, WL_PIECE * PACK], BF16, f"wl_bf{i}", 13) for i in (1, 2))
-        y_all = [tile([P, HALF], F32, f"y{k}")[:] for k in range(3)]
-        y_all.extend(reuse_tile([P, HALF], F32, f"y{k}", k + 1)[:] for k in range(3, HALVES * N_TILES))
-        y = [y_all[u::HALVES] for u in range(HALVES)]
-        v_s_area = late.tile([P, late_bytes[-1]], U8, name="v_s_area", align_bytes=ALIGN, offset=0)
-        v_s = v_s_area[:, 0:S]
-        rows = tile([P, PLANE], U8, "rows")
+        wl_bf.extend(placed([P, WL_PIECE * PACK], BF16, f"wl_bf{i}", WL_BF) for i in (1, 2))
+        wc_s = placed([P, N // 4], I32, "wc_s", TAB0)
+        wc_planes = [wc_s[:].bitcast(U8)[LIVE * (a + 1) : P, :] for a in range(PASSES)]
+        inc = [
+            placed([P, HALF], F32, f"inc{b}", WE1 + b - 1) if b % HALVES else tile([P, HALF], F32, f"inc{b}")
+            for b in range(BANKS)
+        ]
+        prod = placed([P, PACK * S], F32, "prod", PROD)
+        h = tile([P, PACK, S], F32, "h")
+        h_flat = h[:].rearrange("p t j -> p (t j)")
+        h_bf = [tile([P, HALF * PACK], BF16, f"h_bf{u}") for u in range(HALVES)]
+        h_words = tile([P, S], I32, "h_words")
+        h_s = tile([P, S], U8, "h_s")
+        y_first = tile([P, 2, S], F32, "y_first")
+        y = [y_first[:, n, :] for n in range(2)]
+        y.extend(placed([P, S], F32, f"y{n}", PROD + 4 * (n - 2))[:] for n in range(2, N_TILES))
+        order = [(n, u) for u in range(HALVES) for n in range(2)]
+        order.extend((n, u) for n in range(2, N_TILES) for u in range(HALVES))
+
+        def half(u):
+            return slice(u * HALF, (u + 1) * HALF)
 
         def load_tab(a):
             nc.sync.dma_start(out=tab[a][:], in_=tab_words[a].rearrange("p t i -> p (t i)").bitcast(I32))
@@ -138,10 +118,8 @@ def tile_list_prepayment_burnout_cap_kernel(
                 out=we_raw[a], in_=we[K_PASS * a : K_PASS * (a + 1), :].rearrange("(p j) c -> p j c", j=PACK)
             )
 
-        def load_burn(u):
-            nc.sync.dma_start(
-                out=burn_in[u][:], in_=burn.rearrange("(p t) j -> p t j", t=PACK)[:, :, u * HALF : (u + 1) * HALF]
-            )
+        def load_burn(i):
+            nc.sync.dma_start(out=burn_in[i][:], in_=burn.rearrange("(p t) j -> p t j", t=PACK)[:, 2 * i : 2 * i + 2, :])
 
         def load_wc_scales():
             for quad in range(P // QUADRANT):
@@ -150,9 +128,6 @@ def tile_list_prepayment_burnout_cap_kernel(
                     out=wc_s[first : first + PASSES * LIVE, :],
                     in_=wc_scales[:, LIVE * quad : LIVE * (quad + 1), :].bitcast(I32),
                 )
-
-        def load_wc(dst, c0, c1):
-            nc.sync.dma_start(out=dst[:], in_=wc_words.rearrange("a p c i -> p a (c i)").bitcast(I32)[:, :, c0:c1])
 
         def load_wl(dst, c0, c1):
             nc.sync.dma_start(out=dst[:], in_=wl.rearrange("(p j) c -> p j c", j=PACK)[:, :, c0:c1])
@@ -170,10 +145,10 @@ def tile_list_prepayment_burnout_cap_kernel(
             cols = HALF // 16
             nc.vector.tensor_copy(v[a][u][:], tab[a][:].bitcast(U32).indirect(offsets[:, u * cols : (u + 1) * cols]))
 
-        def weave_we(a, i, copy, m0=0, m1=P):
+        def weave_we(a, i, copy):
             copy(
-                out=we_bf[a][i][:].rearrange("p (t m j) -> p m j t", m=P, j=PACK)[:, m0:m1],
-                in_=we_raw[a].rearrange("p j (m t) -> p m j t", t=PACK)[:, m0:m1, :, 2 * i : 2 * i + 2],
+                out=we_bf[a][i][:].rearrange("p (t m j) -> p m j t", m=P, j=PACK),
+                in_=we_raw[a].rearrange("p j (m t) -> p m j t", t=PACK)[:, :, :, 2 * i : 2 * i + 2],
             )
 
         def quant_we(a, i, t0=0, t1=2):
@@ -185,30 +160,26 @@ def tile_list_prepayment_burnout_cap_kernel(
         def v_plane(a, u):
             return planes[a][:, V_COL + u * HALF : V_COL + (u + 1) * HALF]
 
+        def times_v(acc, words, plane, dtype, a, u):
+            nc.tensor.matmul_mx(
+                out=acc[:], lhsT=words.bitcast(dtype), lhsT_scale=plane,
+                rhs=v[a][u][:].bitcast(FP8X4), rhs_scale=v_plane(a, u), start=(a == 0), stop=(a == PASSES - 1),
+            )
+
         def inc_pass(u, a):
             for t in range(PACK):
                 c0 = a * H + t * P
-                nc.tensor.matmul_mx(
-                    out=inc_banks[u][t][:], lhsT=wi_q[:, 2 * c0 : 2 * (c0 + P)].bitcast(FP4X4),
-                    lhsT_scale=planes[a][:, WI_COL + t * P : WI_COL + (t + 1) * P],
-                    rhs=v[a][u][:].bitcast(FP8X4), rhs_scale=v_plane(a, u), start=(a == 0), stop=(a == PASSES - 1),
+                times_v(
+                    inc_banks[2 * t + u], wi_q[:, 2 * c0 : 2 * (c0 + P)],
+                    planes[a][:, WI_COL + t * P : WI_COL + (t + 1) * P], FP4X4, a, u,
                 )
 
-        def inc_out(u):
-            for t in range(PACK):
-                nc.scalar.copy(out=inc[u][t][:], in_=inc_banks[u][t][:])
-
-        def products(u):
-            for t in range(PACK):
-                acc = bank(PACK * u + t, f"expo{u}{t}")
-                for a in range(PASSES):
-                    nc.tensor.matmul_mx(
-                        out=acc[:], lhsT=we_q[a][:, t * P : (t + 1) * P].bitcast(FP8X4),
-                        lhsT_scale=we_s[a][:, t * P : (t + 1) * P],
-                        rhs=v[a][u][:].bitcast(FP8X4), rhs_scale=v_plane(a, u),
-                        start=(a == 0), stop=(a == PASSES - 1),
-                    )
-                nc.vector.tensor_tensor(prod[u][:, t, :], inc[u][t][:], acc[:], ALU.mult)
+        def product(b):
+            t, u = divmod(b, HALVES)
+            acc = bank(b, f"expo{b}")
+            for a in range(PASSES):
+                times_v(acc, we_q[a][:, t * P : (t + 1) * P], we_s[a][:, t * P : (t + 1) * P], FP8X4, a, u)
+            nc.vector.tensor_tensor(prod[:, b * HALF : (b + 1) * HALF], inc[b][:], acc[:], ALU.mult)
 
         def weave(copy, dst, src):
             copy(
@@ -216,60 +187,53 @@ def tile_list_prepayment_burnout_cap_kernel(
                 in_=src.rearrange("p t (c i) -> p c t i", i=2),
             )
 
-        def add_burn(engine, u, t0, t1):
-            engine.tensor_tensor(h[u][:, t0:t1, :], burn_in[u][:, t0:t1, :], prod[u][:, t0:t1, :], ALU.add)
+        def add_burn(engine, lo, hi):
+            pair = lo // (2 * S)
+            flat = burn_in[pair][:].rearrange("p t j -> p (t j)")
+            engine.tensor_tensor(h_flat[:, lo:hi], flat[:, lo - pair * 2 * S : hi - pair * 2 * S], prod[:, lo:hi], ALU.add)
 
-        def store_h(u):
+        def store_h(i):
             nc.sync.dma_start(
-                out=out_1.rearrange("(p t) j -> p t j", t=PACK)[:, :, u * HALF : (u + 1) * HALF], in_=h[u][:]
+                out=out_1.rearrange("(p t) j -> p t j", t=PACK)[:, 2 * i : 2 * i + 2, :], in_=h[:, 2 * i : 2 * i + 2, :]
             )
 
-        def weave_h(copy, i):
-            u, c0, c1 = h_parts[i]
-            weave(copy, h_bf[i][:], h[u][:, :, c0:c1])
+        def weave_h(copy, u, c0, c1):
+            weave(copy, h_bf[u][:, c0 * PACK : c1 * PACK], h[:, :, u * HALF + c0 : u * HALF + c1])
 
-        def quant_h(i):
-            u, c0, c1 = h_parts[i]
-            nc.vector.quantize_mx(
-                out=h_q[u][:, c0:c1].bitcast(FP8X4), scales=h_s[:, u * HALF + c0 : u * HALF + c1], in_=h_bf[i][:]
-            )
-
-        def store_words(u):
-            words = out_2[0].rearrange("p m t -> p (m t)").bitcast(I32)
-            nc.sync.dma_start(out=words[:, u * HALF : (u + 1) * HALF], in_=h_q[u])
+        def quant_h(u):
+            nc.vector.quantize_mx(out=h_words[:, half(u)].bitcast(FP8X4), scales=h_s[:, half(u)], in_=h_bf[u][:])
 
         def quant_wl(i):
             nc.vector.quantize_mx(out=wl_q[i][:].bitcast(FP8X4), scales=wl_s[i][:], in_=wl_bf[i][:])
 
-        def cap_tile(n, u):
-            k = HALVES * n + u
-            acc = bank(k if k < BANKS else k - BANKS + len(LOAD_BANKS), f"cap{u}{n}")
+        def cap_unit(k):
+            n, u = order[k]
+            acc = bank(k if k < BANKS else LATE_BANKS[k - BANKS], f"cap{k}")
             for a in range(PASSES):
-                words, c0 = (wc_first, n * P) if n * P < WC_CUT else (wc_rest, n * P - WC_CUT)
-                nc.tensor.matmul_mx(
-                    out=acc[:], lhsT=words[:, a, c0 : c0 + P].bitcast(FP8X4),
-                    lhsT_scale=wc_planes[a][:, n * P : (n + 1) * P],
-                    rhs=v[a][u][:].bitcast(FP8X4), rhs_scale=v_plane(a, u),
-                    start=(a == 0), stop=(a == PASSES - 1),
-                )
-            nc.scalar.copy(out=y[u][n], in_=acc[:])
+                times_v(acc, wc_q[:, a, n * P : (n + 1) * P], wc_planes[a][:, n * P : (n + 1) * P], FP8X4, a, u)
+            nc.scalar.copy(out=y[n][:, half(u)], in_=acc[:])
 
-        def min_tile(k, n, u):
-            acc = bank(LOAD_BANKS[k % len(LOAD_BANKS)], f"load{u}{n}")
+        def min_unit(k):
+            n, u = order[k]
+            acc = bank(LOAD_BANKS[k], f"load{k}")
             piece, c0 = divmod(n * P, WL_PIECE)
             nc.tensor.matmul_mx(
-                out=acc[:], lhsT=wl_q[piece][:, c0 : c0 + P].bitcast(FP8X4),
-                lhsT_scale=wl_s[piece][:, c0 : c0 + P], rhs=h_q[u].bitcast(FP8X4),
-                rhs_scale=h_s[:, u * HALF : (u + 1) * HALF], start=True, stop=True,
+                out=acc[:], lhsT=wl_q[piece][:, c0 : c0 + P].bitcast(FP8X4), lhsT_scale=wl_s[piece][:, c0 : c0 + P],
+                rhs=h_words[:, half(u)].bitcast(FP8X4), rhs_scale=h_s[:, half(u)], start=True, stop=True,
             )
-            last = (n, u) == (N_TILES - 1, HALVES - 1)
-            for j0, j1 in ((0, LAST_CUT), (LAST_CUT, HALF)) if last else ((0, HALF),):
-                nc.vector.tensor_tensor(y[u][n][:, j0:j1], y[u][n][:, j0:j1], acc[:, j0:j1], ALU.min)
-                nc.sync.dma_start(
-                    out=out_0[n * P : (n + 1) * P, u * HALF + j0 : u * HALF + j1], in_=y[u][n][:, j0:j1]
-                )
+            nc.vector.tensor_tensor(y[n][:, half(u)], y[n][:, half(u)], acc[:], ALU.min)
+            rows_n = slice(n * P, (n + 1) * P)
+            if n < 2:
+                if n == 1:
+                    pair = out_0[0 : 2 * P, :].rearrange("(n p) j -> p n j", p=P)
+                    nc.sync.dma_start(out=pair[:, :, half(u)], in_=y_first[:, :, half(u)])
+            elif n == N_TILES - 1:
+                nc.sync.dma_start(out=out_0[rows_n, half(u)], in_=y[n][:, half(u)])
+            elif u == HALVES - 1:
+                nc.sync.dma_start(out=out_0[rows_n, :], in_=y[n])
 
-        def store_h_scales():
+        def store_planes():
+            nc.sync.dma_start(out=out_2[0].rearrange("p m t -> p (m t)").bitcast(I32), in_=h_words[:])
             for r in range(LIVE):
                 nc.sync.dma_start(
                     out=out_3[0].rearrange("(q r) m -> r q m", r=LIVE)[r].bitcast(I32),
@@ -279,15 +243,14 @@ def tile_list_prepayment_burnout_cap_kernel(
         load_scale_rows(tab_s[STAGED:P, :], tab_scales)
         nc.sync.dma_start(offsets[:], offs)
         load_scale_rows(wi_s_raw[STAGED:P, :], wi_scales)
-        load_tab(0)
         nc.sync.dma_start(
             out=wi_raw[:].rearrange("p (a c) -> p a c", a=PASSES).bitcast(I32),
             in_=wi_words.rearrange("a p c -> p a c").bitcast(I32),
         )
+        load_tab(0)
 
         nc.vector.memset(tab_s[0:STAGED, :].bitcast(I32), 0)
         nc.vector.memset(wi_s_raw[0:STAGED, :].bitcast(I32), 0)
-
         nc.vector.tensor_copy(
             out=rows[:, WI_COL:PLANE].rearrange("p (t m) -> p m t", t=PACK),
             in_=wi_s_raw[:].rearrange("p (m t) -> p m t", t=PACK),
@@ -305,7 +268,7 @@ def tile_list_prepayment_burnout_cap_kernel(
         load_we(1)
         load_burn(0)
 
-        inc_banks = [[bank(PACK * u + t, f"inc{u}{t}") for t in range(PACK)] for u in range(HALVES)]
+        inc_banks = [bank(b, f"inc_acc{b}") for b in range(BANKS)]
         for a in range(PASSES):
             for u in range(HALVES):
                 gather(a, u)
@@ -314,14 +277,13 @@ def tile_list_prepayment_burnout_cap_kernel(
                 load_wc_scales()
         weave_we(0, 0, nc.vector.tensor_copy)
         weave_we(0, 1, nc.vector.tensor_copy)
-        load_wc(wc_first, 0, WC_CUT)
-        load_wl(wl_first, 0, WL_PIECE)
-        load_wc(wc_rest, WC_CUT, N)
+        nc.sync.dma_start(out=wc_q[:], in_=wc_words.rearrange("a p c i -> p a (c i)").bitcast(I32))
         load_burn(1)
+        load_wl(wl_first, 0, WL_PIECE)
         load_wl(wl_rest, WL_PIECE, N)
         weave_we(1, 1, nc.scalar.copy)
-        for u in range(HALVES):
-            inc_out(u)
+        for b in range(BANKS):
+            nc.scalar.copy(out=inc[b][:], in_=inc_banks[b][:])
         weave(nc.scalar.copy, wl_bf[0][:], wl_raw[0])
         quant_we(0, 0)
         quant_we(0, 1)
@@ -330,39 +292,35 @@ def tile_list_prepayment_burnout_cap_kernel(
         quant_we(1, 0, 1, 2)
         quant_we(1, 1)
 
-        products(0)
-        for t in range(GPSIMD_SLICES):
-            add_burn(nc.gpsimd, 0, t, t + 1)
-        products(1)
-        add_burn(nc.vector, 0, GPSIMD_SLICES, PACK)
+        for b in range(BANKS):
+            product(b)
+            if b * HALF < GPSIMD_COLS:
+                add_burn(nc.gpsimd, b * HALF, min((b + 1) * HALF, GPSIMD_COLS))
+        add_burn(nc.vector, GPSIMD_COLS, 2 * S)
         store_h(0)
-        weave_h(nc.scalar.copy, 0)
-        add_burn(nc.vector, 1, 0, PACK)
+        add_burn(nc.vector, 2 * S, PACK * S - HALF)
+        weave_h(nc.scalar.copy, 0, H_CUTS[0], HALF)
+        add_burn(nc.vector, PACK * S - HALF, PACK * S)
         store_h(1)
-        weave_h(nc.scalar.copy, 1)
+        weave_h(nc.scalar.copy, 1, H_CUTS[1], HALF)
 
+        weave_h(nc.vector.tensor_copy, 0, 0, H_CUTS[0])
         quant_wl(0)
-        weave_h(nc.vector.tensor_copy, 2)
         quant_h(0)
-        store_words(0)
-        weave_h(nc.vector.tensor_copy, 3)
-        quant_h(2)
-        quant_h(3)
-        quant_h(1)
-        store_words(1)
-        store_h_scales()
+        weave_h(nc.vector.tensor_copy, 1, 0, H_CUTS[1])
 
-        for n in range(BANKS // HALVES):
-            for u in range(HALVES):
-                cap_tile(n, u)
-            if n == 1:
+        for k in range(BANKS):
+            cap_unit(k)
+            if k == 3:
                 weave(nc.scalar.copy, wl_bf[1][:], wl_raw[1])
 
-        order = [(2 * piece + i, u) for piece in range(3) for u in range(HALVES) for i in range(2)]
-        for k, (n, u) in enumerate(order):
-            min_tile(k, n, u)
+        for k in range(HALVES * N_TILES):
+            min_unit(k)
+            if k == 0:
+                quant_h(1)
+                store_planes()
             if 2 <= k < 6:
-                cap_tile(*divmod(BANKS + k - 2, HALVES))
+                cap_unit(BANKS + k - 2)
             if k == 1:
                 quant_wl(1)
                 nc.gpsimd.tensor_scalar(

@@ -34,6 +34,7 @@ WL_PIECE = 2 * P
 PIECES = N // WL_PIECE
 GPSIMD_COLS = 3 * HALF
 H_CUTS = (224, 128)
+LAST_CUT = 3 * P
 LATE_BANKS = (0, 1, 5, 6)
 LOAD_BANKS = (2, 3, 2, 3, 4, 2, 3, 4, 2, 3, 4, 2)
 
@@ -202,6 +203,8 @@ def tile_list_prepayment_burnout_cap_kernel(
 
         def quant_h(u):
             nc.vector.quantize_mx(out=h_words[:, half(u)].bitcast(FP8X4), scales=h_s[:, half(u)], in_=h_bf[u][:])
+            words = out_2[0].rearrange("p m t -> p (m t)").bitcast(I32)
+            nc.sync.dma_start(out=words[:, half(u)], in_=h_words[:, half(u)])
 
         def quant_wl(i):
             nc.vector.quantize_mx(out=wl_q[i][:].bitcast(FP8X4), scales=wl_s[i][:], in_=wl_bf[i][:])
@@ -221,19 +224,12 @@ def tile_list_prepayment_burnout_cap_kernel(
                 out=acc[:], lhsT=wl_q[piece][:, c0 : c0 + P].bitcast(FP8X4), lhsT_scale=wl_s[piece][:, c0 : c0 + P],
                 rhs=h_words[:, half(u)].bitcast(FP8X4), rhs_scale=h_s[:, half(u)], start=True, stop=True,
             )
-            nc.vector.tensor_tensor(y[n][:, half(u)], y[n][:, half(u)], acc[:], ALU.min)
-            rows_n = slice(n * P, (n + 1) * P)
-            if n < 2:
-                if n == 1:
-                    pair = out_0[0 : 2 * P, :].rearrange("(n p) j -> p n j", p=P)
-                    nc.sync.dma_start(out=pair[:, :, half(u)], in_=y_first[:, :, half(u)])
-            elif n == N_TILES - 1:
-                nc.sync.dma_start(out=out_0[rows_n, half(u)], in_=y[n][:, half(u)])
-            elif u == HALVES - 1:
-                nc.sync.dma_start(out=out_0[rows_n, :], in_=y[n])
+            for j0, j1 in ((0, LAST_CUT), (LAST_CUT, HALF)) if k == len(order) - 1 else ((0, HALF),):
+                cols = slice(u * HALF + j0, u * HALF + j1)
+                nc.vector.tensor_tensor(y[n][:, cols], y[n][:, cols], acc[:, j0:j1], ALU.min)
+                nc.sync.dma_start(out=out_0[n * P : (n + 1) * P, cols], in_=y[n][:, cols])
 
         def store_planes():
-            nc.sync.dma_start(out=out_2[0].rearrange("p m t -> p (m t)").bitcast(I32), in_=h_words[:])
             for r in range(LIVE):
                 nc.sync.dma_start(
                     out=out_3[0].rearrange("(q r) m -> r q m", r=LIVE)[r].bitcast(I32),

from contextlib import ExitStack

import concourse.mybir as mybir

K, H, N, T, S = 1024, 512, 768, 4096, 1024
FLOPS = 2 * S * (2 * K * H + H * N + K * N)

F32 = mybir.dt.float32
BF16 = mybir.dt.bfloat16
I32 = mybir.dt.int32
U32 = mybir.dt.uint32
U16 = mybir.dt.uint16
U8 = mybir.dt.uint8
FP8X4 = mybir.dt.float8_e4m3fn_x4
FP4X4 = mybir.dt.float4_e2m1fn_x4
ALU = mybir.AluOpType

P = 128
ALIGN = 256
PACK = 4
K_PASS = P * PACK
PASSES = K // K_PASS
HALF = 512
HALVES = S // HALF
N_TILES = N // P
QUADRANT = 32
LIVE = 4
BLOCKS = 16
STAGED = P - PASSES * BLOCKS
V_COL, WI_COL, PLANE = 0, S, S + H
BANKS = 8
KIB = 1024
WL_PIECE = 2 * P
PIECES = N // WL_PIECE
GPSIMD_COLS = 3 * HALF
H_CUTS = (224, 128)
LAST_CUT = 3 * P
LATE_BANKS = (0, 1, 5, 6)
LOAD_BANKS = (2, 3, 2, 3, 4, 2, 3, 4, 2, 3, 4, 2)


def tile_list_prepayment_burnout_cap_kernel(
    tc, tab_words, tab_scales, offs, wi_words, wi_scales, we, burn, wl, wc_words, wc_scales,
    out_0, out_1, out_2, out_3,
):
    nc = tc.nc
    with ExitStack() as ctx:
        lists = ctx.enter_context(tc.tile_pool(name="lists", bufs=1))
        keep = ctx.enter_context(tc.tile_pool(name="keep", bufs=1))
        shared = ctx.enter_context(tc.tile_pool(name="shared", bufs=1))
        psum = ctx.enter_context(tc.psum_pool(name="psum", bufs=1))

        def bank(b, name):
            return psum.tile([P, HALF], F32, name=name, offset=b * HALF * 4)

        def tile(shape, dtype, name):
            return keep.tile(shape, dtype, name=name, align_bytes=ALIGN)

        def placed(shape, dtype, name, kib):
            return shared.tile(shape, dtype, name=name, align_bytes=ALIGN, offset=kib * KIB)

        TAB0, TAB1, WE1, BURN0, WE0, PROD, WL_BF = 0, 16, 32, 40, 48, 74, 90

        offsets = lists.tile([P, S // 16], U16, name="offsets")
        tab_s = tile([P, T], U8, "tab_s")
        plane_pair = tile([P, PASSES * PLANE], U8, "plane_pair")
        planes = [plane_pair[:, a * PLANE : (a + 1) * PLANE] for a in range(PASSES)]
        wi_raw = tile([P, PASSES * 2 * H], U8, "wi_raw")
        wi_s_raw = tile([P, H], U8, "wi_s_raw")
        wi_q = tile([P, PASSES * 2 * H], U8, "wi_q")
        rows = tile([P, PLANE], U8, "rows")
        v_s_area = placed([P, (PROD - TAB1) * KIB], U8, "v_s_area", TAB1)
        v_s = v_s_area[:, 0:S]
        tab = [placed([P, T], I32, "tab0", TAB0), placed([P, T], I32, "tab1", TAB1)]
        v = [[tile([P, HALF], U32, f"v{a}{u}") for u in range(HALVES)] for a in range(PASSES)]
        we_area = placed([P, (PROD - WE0) * KIB // 4], F32, "we_area", WE0)
        we_raw = [we_area[:, 0 : PACK * H].rearrange("p (j c) -> p j c", j=PACK), placed([P, PACK, H], F32, "we1", WE1)[:]]
        we_bf = [[tile([P, H * 2], BF16, f"we_bf{a}{i}") for i in range(2)] for a in range(PASSES)]
        we_q = [tile([P, H], U32, f"we_q{a}") for a in range(PASSES)]
        we_s = [tile([P, H], U8, f"we_s{a}") for a in range(PASSES)]
        wc_q = placed([P, PASSES, N], I32, "wc_q", WE0)
        burn_in = [placed([P, 2, S], F32, "burn0", BURN0), placed([P, 2, S], F32, "burn1", WE0 + 6)]
        wl_first = placed([P, PACK, WL_PIECE], F32, "wl_first", WE0 + 14)
        wl_rest = placed([P, PACK, N - WL_PIECE], F32, "wl_rest", WE0 + 18)
        wl_raw = [wl_first[:], wl_rest[:, :, 0:WL_PIECE], wl_rest[:, :, WL_PIECE:]]
        wl_q = [tile([P, WL_PIECE], U32, f"wl_q{i}") for i in range(PIECES)]
        wl_s = [tile([P, WL_PIECE], U8, f"wl_s{i}") for i in range(PIECES)]
        wl_bf = [tile([P, WL_PIECE * PACK], BF16, "wl_bf0")]
        wl_bf.extend(placed([P, WL_PIECE * PACK], BF16, f"wl_bf{i}", WL_BF) for i in (1, 2))
        wc_s = placed([P, N // 4], I32, "wc_s", TAB0)
        wc_planes = [wc_s[:].bitcast(U8)[LIVE * (a + 1) : P, :] for a in range(PASSES)]
        inc = [
            placed([P, HALF], F32, f"inc{b}", WE1 + b - 1) if b % HALVES else tile([P, HALF], F32, f"inc{b}")
            for b in range(BANKS)
        ]
        prod = placed([P, PACK * S], F32, "prod", PROD)
        h = tile([P, PACK, S], F32, "h")
        h_flat = h[:].rearrange("p t j -> p (t j)")
        h_bf = [tile([P, HALF * PACK], BF16, f"h_bf{u}") for u in range(HALVES)]
        h_words = tile([P, S], I32, "h_words")
        h_s = tile([P, S], U8, "h_s")
        y_first = tile([P, 2, S], F32, "y_first")
        y = [y_first[:, n, :] for n in range(2)]
        y.extend(placed([P, S], F32, f"y{n}", PROD + 4 * (n - 2))[:] for n in range(2, N_TILES))
        order = [(n, u) for u in range(HALVES) for n in range(2)]
        order.extend((n, u) for n in range(2, N_TILES) for u in range(HALVES))

        def half(u):
            return slice(u * HALF, (u + 1) * HALF)

        def load_tab(a):
            nc.sync.dma_start(out=tab[a][:], in_=tab_words[a].rearrange("p t i -> p (t i)").bitcast(I32))

        def load_scale_rows(dst, src):
            nc.sync.dma_start(out=dst.bitcast(I32), in_=src.rearrange("a q c -> q a c").bitcast(I32))

        def load_we(a):
            nc.sync.dma_start(
                out=we_raw[a], in_=we[K_PASS * a : K_PASS * (a + 1), :].rearrange("(p j) c -> p j c", j=PACK)
            )

        def load_burn(i):
            nc.sync.dma_start(out=burn_in[i][:], in_=burn.rearrange("(p t) j -> p t j", t=PACK)[:, 2 * i : 2 * i + 2, :])

        def load_wc_scales():
            for quad in range(P // QUADRANT):
                first = QUADRANT * quad + LIVE
                nc.gpsimd.dma_start(
                    out=wc_s[first : first + PASSES * LIVE, :],
                    in_=wc_scales[:, LIVE * quad : LIVE * (quad + 1), :].bitcast(I32),
                )

        def load_wl(dst, c0, c1):
            nc.sync.dma_start(out=dst[:], in_=wl.rearrange("(p j) c -> p j c", j=PACK)[:, :, c0:c1])

        def move_planes():
            staged = PASSES * LIVE
            for quad in (0, 2, 1, 3):
                live = plane_pair[QUADRANT * quad : QUADRANT * quad + LIVE, :]
                nc.sync.dma_start(
                    out=live.rearrange("p (a c) -> p a c", a=PASSES).bitcast(I32),
                    in_=rows[STAGED + staged * quad : STAGED + staged * (quad + 1), :].bitcast(I32),
                )

        def gather(a, u):
            cols = HALF // 16
            nc.vector.tensor_copy(v[a][u][:], tab[a][:].bitcast(U32).indirect(offsets[:, u * cols : (u + 1) * cols]))

        def weave_we(a, i, copy):
            copy(
                out=we_bf[a][i][:].rearrange("p (t m j) -> p m j t", m=P, j=PACK),
                in_=we_raw[a].rearrange("p j (m t) -> p m j t", t=PACK)[:, :, :, 2 * i : 2 * i + 2],
            )

        def quant_we(a, i, t0=0, t1=2):
            cols = slice((2 * i + t0) * P, (2 * i + t1) * P)
            nc.vector.quantize_mx(
                out=we_q[a][:, cols].bitcast(FP8X4), scales=we_s[a][:, cols], in_=we_bf[a][i][:, t0 * H : t1 * H]
            )

        def v_plane(a, u):
            return planes[a][:, V_COL + u * HALF : V_COL + (u + 1) * HALF]

        def times_v(acc, words, plane, dtype, a, u):
            nc.tensor.matmul_mx(
                out=acc[:], lhsT=words.bitcast(dtype), lhsT_scale=plane,
                rhs=v[a][u][:].bitcast(FP8X4), rhs_scale=v_plane(a, u), start=(a == 0), stop=(a == PASSES - 1),
            )

        def inc_pass(u, a):
            for t in range(PACK):
                c0 = a * H + t * P
                times_v(
                    inc_banks[2 * t + u], wi_q[:, 2 * c0 : 2 * (c0 + P)],
                    planes[a][:, WI_COL + t * P : WI_COL + (t + 1) * P], FP4X4, a, u,
                )

        def product(b):
            t, u = divmod(b, HALVES)
            acc = bank(b, f"expo{b}")
            for a in range(PASSES):
                times_v(acc, we_q[a][:, t * P : (t + 1) * P], we_s[a][:, t * P : (t + 1) * P], FP8X4, a, u)
            nc.vector.tensor_tensor(prod[:, b * HALF : (b + 1) * HALF], inc[b][:], acc[:], ALU.mult)

        def weave(copy, dst, src):
            copy(
                out=dst.rearrange("p (c i t) -> p c t i", i=2, t=PACK),
                in_=src.rearrange("p t (c i) -> p c t i", i=2),
            )

        def add_burn(engine, lo, hi):
            pair = lo // (2 * S)
            flat = burn_in[pair][:].rearrange("p t j -> p (t j)")
            engine.tensor_tensor(h_flat[:, lo:hi], flat[:, lo - pair * 2 * S : hi - pair * 2 * S], prod[:, lo:hi], ALU.add)

        def store_h(i):
            nc.sync.dma_start(
                out=out_1.rearrange("(p t) j -> p t j", t=PACK)[:, 2 * i : 2 * i + 2, :], in_=h[:, 2 * i : 2 * i + 2, :]
            )

        def weave_h(copy, u, c0, c1):
            weave(copy, h_bf[u][:, c0 * PACK : c1 * PACK], h[:, :, u * HALF + c0 : u * HALF + c1])

        def quant_h(u):
            nc.vector.quantize_mx(out=h_words[:, half(u)].bitcast(FP8X4), scales=h_s[:, half(u)], in_=h_bf[u][:])
            words = out_2[0].rearrange("p m t -> p (m t)").bitcast(I32)
            nc.sync.dma_start(out=words[:, half(u)], in_=h_words[:, half(u)])

        def quant_wl(i):
            nc.vector.quantize_mx(out=wl_q[i][:].bitcast(FP8X4), scales=wl_s[i][:], in_=wl_bf[i][:])

        def cap_unit(k):
            n, u = order[k]
            acc = bank(k if k < BANKS else LATE_BANKS[k - BANKS], f"cap{k}")
            for a in range(PASSES):
                times_v(acc, wc_q[:, a, n * P : (n + 1) * P], wc_planes[a][:, n * P : (n + 1) * P], FP8X4, a, u)
            nc.scalar.copy(out=y[n][:, half(u)], in_=acc[:])

        def min_unit(k):
            n, u = order[k]
            acc = bank(LOAD_BANKS[k], f"load{k}")
            piece, c0 = divmod(n * P, WL_PIECE)
            nc.tensor.matmul_mx(
                out=acc[:], lhsT=wl_q[piece][:, c0 : c0 + P].bitcast(FP8X4), lhsT_scale=wl_s[piece][:, c0 : c0 + P],
                rhs=h_words[:, half(u)].bitcast(FP8X4), rhs_scale=h_s[:, half(u)], start=True, stop=True,
            )
            for j0, j1 in ((0, LAST_CUT), (LAST_CUT, HALF)) if k == len(order) - 1 else ((0, HALF),):
                cols = slice(u * HALF + j0, u * HALF + j1)
                nc.vector.tensor_tensor(y[n][:, cols], y[n][:, cols], acc[:, j0:j1], ALU.min)
                nc.sync.dma_start(out=out_0[n * P : (n + 1) * P, cols], in_=y[n][:, cols])

        def store_planes():
            for r in range(LIVE):
                nc.sync.dma_start(
                    out=out_3[0].rearrange("(q r) m -> r q m", r=LIVE)[r].bitcast(I32),
                    in_=h_s[r:P:QUADRANT, :].bitcast(I32),
                )

        load_scale_rows(tab_s[STAGED:P, :], tab_scales)
        nc.sync.dma_start(offsets[:], offs)
        load_scale_rows(wi_s_raw[STAGED:P, :], wi_scales)
        nc.sync.dma_start(
            out=wi_raw[:].rearrange("p (a c) -> p a c", a=PASSES).bitcast(I32),
            in_=wi_words.rearrange("a p c -> p a c").bitcast(I32),
        )
        load_tab(0)

        nc.vector.memset(tab_s[0:STAGED, :].bitcast(I32), 0)
        nc.vector.memset(wi_s_raw[0:STAGED, :].bitcast(I32), 0)
        nc.vector.tensor_copy(
            out=rows[:, WI_COL:PLANE].rearrange("p (t m) -> p m t", t=PACK),
            in_=wi_s_raw[:].rearrange("p (m t) -> p m t", t=PACK),
        )
        nc.vector.tensor_copy(v_s, tab_s[:].indirect(offsets[:]))
        nc.vector.tensor_copy(out=rows[:, V_COL:WI_COL].bitcast(I32), in_=v_s.bitcast(I32))
        nc.vector.tensor_copy(
            out=wi_q[:].bitcast(U16).rearrange("p (a t m) -> p a m t", a=PASSES, t=PACK),
            in_=wi_raw[:].bitcast(U16).rearrange("p (a m t) -> p a m t", a=PASSES, t=PACK),
        )

        move_planes()
        load_tab(1)
        load_we(0)
        load_we(1)
        load_burn(0)

        inc_banks = [bank(b, f"inc_acc{b}") for b in range(BANKS)]
        for a in range(PASSES):
            for u in range(HALVES):
                gather(a, u)
                inc_pass(u, a)
            if a == 0:
                load_wc_scales()
        weave_we(0, 0, nc.vector.tensor_copy)
        weave_we(0, 1, nc.vector.tensor_copy)
        nc.sync.dma_start(out=wc_q[:], in_=wc_words.rearrange("a p c i -> p a (c i)").bitcast(I32))
        load_burn(1)
        load_wl(wl_first, 0, WL_PIECE)
        load_wl(wl_rest, WL_PIECE, N)
        weave_we(1, 1, nc.scalar.copy)
        for b in range(BANKS):
            nc.scalar.copy(out=inc[b][:], in_=inc_banks[b][:])
        weave(nc.scalar.copy, wl_bf[0][:], wl_raw[0])
        quant_we(0, 0)
        quant_we(0, 1)
        weave_we(1, 0, nc.vector.tensor_copy)
        quant_we(1, 0, 0, 1)
        quant_we(1, 0, 1, 2)
        quant_we(1, 1)

        for b in range(BANKS):
            product(b)
            if b * HALF < GPSIMD_COLS:
                add_burn(nc.gpsimd, b * HALF, min((b + 1) * HALF, GPSIMD_COLS))
        add_burn(nc.vector, GPSIMD_COLS, 2 * S)
        store_h(0)
        add_burn(nc.vector, 2 * S, PACK * S - HALF)
        weave_h(nc.scalar.copy, 0, H_CUTS[0], HALF)
        add_burn(nc.vector, PACK * S - HALF, PACK * S)
        store_h(1)
        weave_h(nc.scalar.copy, 1, H_CUTS[1], HALF)

        weave_h(nc.vector.tensor_copy, 0, 0, H_CUTS[0])
        quant_wl(0)
        quant_h(0)
        weave_h(nc.vector.tensor_copy, 1, 0, H_CUTS[1])

        for k in range(BANKS):
            cap_unit(k)
            if k == 3:
                weave(nc.scalar.copy, wl_bf[1][:], wl_raw[1])

        for k in range(HALVES * N_TILES):
            min_unit(k)
            if k == 0:
                quant_h(1)
                store_planes()
            if 2 <= k < 6:
                cap_unit(BANKS + k - 2)
            if k == 1:
                quant_wl(1)
                nc.gpsimd.tensor_scalar(
                    wl_bf[2][:].rearrange("p (c t) -> p c t", t=PACK), wl_raw[2].rearrange("p t c -> p c t"),
                    1.0, 0.0, ALU.mult, ALU.add,
                )
            if k == 5:
                quant_wl(2)
